import numpy as np, ml_dtypes
CORES = [10,34,74,98]
N = 4
import mx_ref
BF = ml_dtypes.bfloat16
def gcols(t, e):
    v = np.concatenate([t.reshape(8, 16, -1, 4), np.zeros((8, 16, 1, 4), BF)], axis=2)
    return np.ascontiguousarray(np.stack([v[g][:, e[g]] for g in range(8)])).reshape(128, -1)
def tile(rs):
    return np.stack(rs, axis=2).reshape(128, -1).astype(BF)
def pick(q, e):
    c = np.concatenate([q[0].reshape(128, -1, 4), np.zeros((128, 1, 4), np.uint8)], axis=1); s = np.concatenate([q[1], np.ones((16, 1), np.uint8)], axis=1)
    return (np.ascontiguousarray(c[:, e].reshape(128, -1)), np.ascontiguousarray(s[:, e]))
def join(*qs):
    return (np.concatenate([q[0] for q in qs], axis=1), np.concatenate([q[1] for q in qs], axis=1))
def put(q, e, v):
    c, s = q[0].reshape(128, -1, 4).copy(), q[1].copy(); c[:, e] = v[0].reshape(128, -1, 4); s[:, e] = v[1]
    return (c.reshape(128, -1), s)
def pk(c, s):
    return (np.ascontiguousarray(c), mx_ref.live(s))
def emit(q):
    return q[0], q[1]
def packed(v, rng):
    q = [mx_ref.quantize(np.ascontiguousarray(v[r])) for r in range(N)]
    return np.stack([a for a, b in q]), np.stack([mx_ref.plane(b, rng) for a, b in q])
def values_of_codes():
    e, c = np.zeros((128, 128, 4), np.float32), np.zeros((128, 2, 4), np.uint8)
    e[np.arange(128), np.arange(128), 0] = 1
    c[:127, :, 0] = np.arange(256).reshape(2, 128).T[:127]
    return mx_ref.matmul(mx_ref.quantize(e.reshape(128, 512).astype(BF)), (c.reshape(128, 8), np.full((16, 2), 127, np.uint8))).T.reshape(-1).astype(np.float64)
CODE_VALUE, SCALE_VALUE = values_of_codes(), 2.0 ** (np.arange(256) - 127.0)
def decode(q):
    return (CODE_VALUE[q[0]].reshape(16, 8, -1, 4) * SCALE_VALUE[q[1]][:, None, :, None] + 0.0).reshape(128, -1).astype(np.float32)
def f(rng, *shape):
    return mx_ref.flush((rng.standard_normal(shape, dtype=np.float32) * np.exp2(rng.integers(-2, 3, shape[:-1] + (1,)))).astype(BF))
def wide(rng, *shape, cols=0):
    v = rng.standard_normal(shape, dtype=np.float32) * np.exp2(rng.integers(-12, 13, shape)).astype(np.float32)
    if cols: v *= np.repeat(np.exp2(rng.integers(-cols, cols + 1, shape[:-2] + (1, shape[-1] // 4))) * (rng.random(shape[:-2] + (1, shape[-1] // 4)) > 0.0625), 4, axis=-1).astype(np.float32)
    return mx_ref.flush(v.astype(BF))
C, S, K, W, M, R = 480, 48, 10, 3, 2, 3
def big(v):
    v = v.astype(np.float32)
    v[np.abs(v) < np.float32(2.0 ** -16)] = 0
    return v.astype(BF)
def numbers_of(rng):
    return {"x": big(f(rng, N, 128, 4 * C)), "u": np.array(f(rng, N, 128, 512)), "v": np.array(f(rng, N, 128, 512))}
def layers(rng):
    return big(f(rng, N, 128, 2048)).reshape(N, 8, 16, 4, 8, 16, 4)
def weights(rng, w):
    c, p = packed(np.ascontiguousarray(w).reshape(N, 128, 2048), rng)
    return {"wc": c, "ws": p}
def bare(u):
    u = u.reshape(N, 128, 128, 4)
    u[:, :, ::16] = 0
    u[:, :, 1::16] = 0
    return u
def setup_inputs(rng):
    return {**numbers_of(rng), **weights(rng, layers(rng))}
def setup_inputs_ties(rng):
    d = numbers_of(rng)
    o = rng.permutation(N)
    x = d["x"].reshape(N, 8, 16, C, 4)
    x[:, :, :2] = 0
    x[:, :, :2, :, 0] = rng.integers(0, 3, (N, 8, 2, C)).astype(np.float32).astype(BF)
    u = bare(d["u"])
    for r in range(N):
        for h in range(0, 128, 16):
            u[r, h, h, 0] = 0.0 if r == o[0] else -1.0 if r == o[1] else 1.0
            u[r, h + 1, h + 1, 0] = u[r, h, h, 0]
    w = layers(rng)
    w[:, :, :, :, :, :2] = 0
    return {"x": x.reshape(N, 128, 4 * C), "u": u.reshape(N, 128, 512), "v": d["v"], **weights(rng, w)}
def setup_inputs_near(rng):
    d = numbers_of(rng)
    x = d["x"].astype(np.float32).reshape(N, 8, 16, C, 4)
    x[:, :, 0] = 0
    x[:, :, 8:] = 0
    u = bare(d["u"])
    s = rng.integers(0, 16, (N, 8, 2, C))
    s = ((s[..., None] >> np.arange(4)) & 1) * np.exp2(np.arange(4) - 23.0)
    h = rng.permutation(8)
    for i in range(8):
        g, k, p = h[i], i // 2, 16 * h[i]
        a = 1.0 if k == 0 else 2.0 ** -30
        if k == 2: x[:, g, 8:10, :, :i - 3] = (1.0 + 0.125 * rng.integers(0, 8, (N, 2, C, i - 3))) * 2.0 ** -30
        else: x[:, g, 8:10] = s[:, g]
        if k < 2:
            x[:, g, 0, :, 0] = 1.0 - 2.0 * (i % 2)
            x[:, g, 11, :, 0] = 2.0 ** -10
        if k == 3:
            for r in range(N): x[r, g, 0, rng.permutation(C)[:2], 0] = np.array([2.0 ** 29, -2.0 ** 29])
        for j in range(2):
            u[:, p + 8 + j, p + j] = a
            if i == 5:
                u[:, p + 8 + j, p + j, 0] = 1.125 * a
                u[:, p + 8 + j, p + j, 1] = -a
            if k < 2:
                u[:, p, p + j, 0] = a
                u[:, p + 11, p + j, 0] = a
            if k == 3: u[:, p, p + j, 0] = 1.0
    w = layers(rng)
    for i in [0, 8, 9, 10, 11, 12, 13, 14, 15]:
        w[:, :, i] = 0
        w[:, :, :, :, :, i] = 0
    return {"x": x.reshape(N, 128, 4 * C).astype(BF), "u": u.reshape(N, 128, 512), "v": d["v"], **weights(rng, w)}
def setup_inputs_huge(rng):
    d = numbers_of(rng)
    e = int(rng.integers(N))
    c = (np.argsort(rng.random((N, C)), axis=1) % 2 * 2.0 - 1.0).reshape(N, 1, 1, C, 1)
    c[e] = 1.0
    c[(e + 1) % N] = np.minimum(c[(e + 1) % N], 0.5)
    c[(e - 1) % N] = -1.0
    x = (1.0 - 0.0625 * rng.integers(0, 3, (N, 8, 16, C, 4))) * 2.0 ** 30 * c
    u = bare(d["u"])
    u[:, :, ::16] = (2.0 ** 30 * np.where(rng.random((N, 128, 8, 4)) < 0.25, 0.875, 1.0)).astype(np.float32).astype(BF)
    u[:, :, 1::16] = (2.0 ** 30 * np.where(rng.random((N, 128, 8, 4)) < 0.5, 0.25, 1.0)).astype(np.float32).astype(BF)
    w = np.zeros((N, 128, 4, 128, 4), np.float32)
    i = np.arange(128)
    for b in range(4): w[:, i, b, i, b] = -1
    return {"x": x.astype(np.float32).reshape(N, 128, 4 * C).astype(BF), "u": u.reshape(N, 128, 512), "v": d["v"], **weights(rng, w.astype(BF))}
def setup_inputs_held(rng):
    d = numbers_of(rng)
    x = d["x"].astype(np.float32).reshape(N, 8, 16, C, 4)
    t = (N, 8, 8, C, 4)
    x[:, :, :2] = 0
    x[:, :, 8:] = (1.0 + (2 * rng.integers(0, 64, t) + 1) * 2.0 ** -7) * np.exp2(-1.0 * rng.integers(8, 15, t)) * rng.choice([-1.0, 1.0], t)
    x[:, :, 8, :, 0] = 1.96875 * rng.choice([-1.0, 1.0], (N, 8, C))
    n = np.argsort(rng.random((N, 8, C)), axis=2)
    m = C - 1 - n
    x[:, :, 0, :, :3] = np.stack([m & 7, m & 56, m & 448], axis=-1)
    turn, at = rng.integers(0, 4, (8, S)), rng.integers(0, 2, (8, S))
    g = np.arange(8)[:, None]
    for r in range(N):
        k = n[r] // K
        x[r, :, 1, :, 0] = np.where(n[r] % K == at[g, k], np.array([8.0, 0.0, 2.0, 3.0])[(r + turn[g, k]) % 4], 0.0)
    u = bare(d["u"])
    for h in range(0, 128, 16):
        u[:, h, h, :3] = 1.0
        u[:, h + 1, h + 1, 0] = 1.0
    w = layers(rng)
    w[:, :, 0] = 0
    w[:, :, :, :, :, :2] = 0
    w[:, :, :, :, :, 8:] = 0
    return {"x": x.reshape(N, 128, 4 * C).astype(BF), "u": u.reshape(N, 128, 512), "v": d["v"], **weights(rng, w)}
def setup_inputs_spread(rng):
    d = setup_inputs(rng)
    d["x"] = big(wide(rng, N, 128, 4 * C, cols=6))
    return d
def check_inputs(d):
    b = []
    for k in ("x", "u", "v"):
        a = np.abs(d[k].astype(np.float32))
        if not (np.isfinite(a).all() and ((a == 0) | (a >= 2.0 ** -30) & (a <= 2.0 ** 30)).all()): b.append("a value of " + k)
    none, least, most = [emit(mx_ref.quantize(np.full((128, 16), k, np.float32).astype(BF)))[1][0, 0] for k in (0.0, 2.0 ** -30, 2.0 ** 30)]
    for r in range(N):
        if ((d["wc"][r] == 0x7F) | (d["wc"][r] == 0xFF)).any(): b.append("wc: a code that is no number")
        s = mx_ref.live(d["ws"][r])
        if ((s != none) & ((s < least) | (s > most))).any(): b.append("ws: a scale out of range")
    return b
def reference(x, u, v, wc, ws):
    qu = [mx_ref.quantize(u[r]) for r in range(N)]
    lay = [pk(wc[r], ws[r]) for r in range(N)]
    now = [x[r] for r in range(N)]
    held = np.full((N, 8, S, K), -1)
    cursor = np.zeros((N, 8, S), np.int64)
    kept = [np.zeros((128, 0), BF) for r in range(N)]
    item = np.arange(K)
    for t in range(R):
        score = [mx_ref.matmul(qu[r], mx_ref.quantize(now[r])) for r in range(N)]
        if t == 0: order = np.stack([np.argsort(-(score[r][::16] + np.float32(0.0)), axis=1, kind="stable") for r in range(N)])
        made = []
        for r in range(N):
            e = (r - 1) % N
            k = np.argsort(held[r] >= 0, axis=2, kind="stable")[:, :, :W]
            n = (K * np.arange(S)[:, None] + k).reshape(8, S * W)
            q = mx_ref.quantize(gcols(now[e], np.take_along_axis(order[e], n, axis=1)))
            kept[r] = np.concatenate([kept[r], decode(q).astype(BF)], axis=1)
            theirs = mx_ref.matmul(qu[r], q)[1::16]
            own = np.take_along_axis(score[r][1::16], np.take_along_axis(order[r], n, axis=1), axis=1)
            np.put_along_axis(held[r], k, np.where(theirs < own, -1, S * W * t + np.arange(S * W)).reshape(8, S, W), axis=2)
            lead = np.argmin(np.concatenate([held[r], np.full((8, S, 1), -1)], axis=2) >= 0, axis=2)
            end = np.minimum(cursor[r] + M, lead)
            goes = (item >= cursor[r][:, :, None]) & (item < end[:, :, None])
            cursor[r] = end
            where = np.zeros((8, C), np.int64)
            np.put_along_axis(where, order[r], np.where(goes, C + held[r], order[r].reshape(8, S, K)).reshape(8, C), axis=1)
            other = gcols(np.concatenate([now[r], kept[r]], axis=1), where)
            z = ((now[r].astype(np.float32) + other.astype(np.float32)) * np.float32(0.5)).astype(BF)
            qz = mx_ref.quantize(z)
            made.append(tile([mx_ref.matmul(pick(lay[r], np.arange(128 * b, 128 * b + 128)), qz) * np.float32(0.03125) + z[:, b::4].astype(np.float32) for b in range(4)]))
        now = made
    y, sk = np.zeros((N, 128, C), np.float32), np.zeros((N, 8, C), np.float32)
    oc, osc = np.zeros((N, 128, 4 * C), np.uint8), np.zeros((N, 16, C), np.uint8)
    for r in range(N):
        q = mx_ref.quantize(now[r])
        y[r] = mx_ref.matmul(mx_ref.quantize(v[r]), q)
        sk[r] = held[r].reshape(8, C)
        oc[r], osc[r] = emit(q)
    return {"y": y, "sk": sk, "oc": oc, "osc": osc}

@@ -1,0 +1,566 @@
+import numpy as np
+from concourse.mybir import dt, AluOpType as A, ActivationFunctionType as F
+
+C, NS, R = 480, 144, 3
+BIG, MAGIC, OFF = 1e29, 12582912.0, 1024.0
+TILES = [["d", 29, 28, 27]] + [[c for c in range(h, h - 4, -1) if c > 0] for h in range(26, 0, -4)]
+WIDTH = [480] + [max(128, 16 * t[0]) for t in TILES[1:]]
+START = [sum(WIDTH[:i]) for i in range(len(WIDTH))]
+ON_SCALAR = (29, 28, 27)
+LISTS = [("LA", 96), ("LW0", 96), ("L3", 256), ("LW1", 96), ("LD", 32), ("LR", 32), ("LR0", 32), ("LR5", 32), ("LH", 32),
+         ("LE", 32), ("LC", 96), ("LT", 96), ("LS", 96), ("LO", 96), ("LK", 32)]
+CONSTS = [("c16", 32), ("X8", 80), ("J5", 96), ("NV", 80), ("N0", 16), ("DUM", 32), ("T4", 32), ("HB", 32), ("S0", 32),
+          ("TH0", 16), ("IDX", 24), ("NA", 24), ("FX", 24), ("K8", 240), ("K5", 96), ("K3", 96), ("H4", 16)]
+LAT = {k: (sum(v for _, v in LISTS[:i]), w) for i, (k, w) in enumerate(LISTS)}
+CAT = {k: (sum(v for _, v in CONSTS[:i]), w) for i, (k, w) in enumerate(CONSTS)}
+NL, NC = sum(w for _, w in LISTS), sum(w for _, w in CONSTS)
+
+SCRATCH = {}
+
+
+def _sb(name, n, d):
+    SCRATCH[name] = ("sbuf", [128, n], d)
+
+
+def _mx(name, n):
+    _sb("q" + name, n, "float8_e4m3fn_x4")
+    _sb("s" + name, n, "uint8")
+
+
+for _k, _w in [("xz", 4 * C + 384), ("xp", 4 * C), ("xs1", 4 * C), ("xs2", 4 * C), ("xs3", 4 * C), ("ub", 512), ("vb", 512),
+               ("ones", 512), ("zb", 512), ("band0", 512), ("band", 512), ("tri", 512), ("eye", 2048), ("iq", C), ("dg", C), ("keep", C),
+               ("ext", C), ("mt", 4 * sum(WIDTH)), ("junk", 7000), ("sg", 4 * C), ("rowd", C), ("tt", 4 * NS), ("hh", 4 * NS * R),
+               ("xg", 384), ("bl", 384), ("cmp", NS), ("hs", NS), ("acs", NS), ("k16", NS), ("h144", NS)]:
+    _sb(_k, _w, "bfloat16")
+for _k, _w in [("pm", 8), ("cc", NC), ("cl", NL), ("cls", NL), ("mm", C), ("yy", C), ("jj", C), ("ob", C), ("ex", C), ("rs", 32), ("w1", 32),
+               ("w2", 32), ("w3", 32), ("w4", 32), ("c0", 32), ("tab", 96), ("orep", 96), ("s1", C), ("bp", NS), ("cm", NS), ("oh", 240),
+               ("pr", 240), ("l0", 320), ("l1", 160), ("dd", 16), ("th", 16), ("cu", 16), ("tg", 64), ("nv", 192), ("dum", 32), ("o2", 96),
+               ("o5", 96), ("sel", 96), ("eq", 16), ("fr", 32), ("an", 80), ("yo", C), ("sko", 32)]:
+    _sb(_k, _w, "float32")
+for _k, _w in [("pi", 8), ("ui", 16)]:
+    _sb(_k, _w, "int32")
+for _k, _w in [("ul", 16), ("lt0", 2), ("lp", 32), ("ll", NL // 16), ("pos", 30), ("tl0", 16), ("bl16", 16), ("ws1", 10), ("ws2", 10),
+               ("wl1", 10), ("wl2", 10), ("gl", 64), ("sl", 32)]:
+    _sb(_k, _w, "uint16")
+for _k, _w in [("u", 128), ("u0", 128), ("u1", 128), ("v", 128), ("w", 512), ("e", 512), ("b", 128), ("r", 128), ("x", C), ("z", C), ("m", sum(WIDTH))]:
+    _mx(_k, _w)
+for _t in range(R):
+    _mx("t%d" % _t, NS)
+    _mx("a%d" % _t, NS)
+for _t in range(8):
+    SCRATCH["p%d" % _t] = ("psum", [128, 512], "float32")
+DMAS = ["dx", "dx2", "du", "dv", "dw", "dws", "d1", "d2", "d3", "dz", "dz2", "dout"]
+SEMAPHORES = ["eV", "eS", "eP", "eG", "snt", "ar0", "ar1", "ar2", "aow", "aw1", "aw2"] + DMAS
+
+
+def rank_program(g, core, T, topo):
+    rank = T.rank_of(core)
+    if rank is None:
+        return
+    n = len(T.cores)
+    nxt, prv = T.cores[(rank + 1) % n], T.cores[(rank - 1) % n]
+    Q = {"V": g.vector, "S": g.scalar, "P": g.tensor, "G": g, "Y": g.sync}
+    count, waited, wr, rd = {}, {}, {}, {}
+    names = list(SEMAPHORES)
+
+    def ap(name, lo=0, hi=None, st=1):
+        hi = SCRATCH[name][1][1] if hi is None else hi
+        return (T[name][:, lo:hi:st] if st > 1 else T[name][:, lo:hi], [(name, lo, hi, st)])
+
+    def ind(w, o):
+        return (w[0].indirect(o[0]), w[1] + o[1])
+
+    def u8(v):
+        return (v[0].bitcast(dt.uint8), v[1])
+
+    def u32(v):
+        return (v[0].bitcast(dt.uint32), v[1])
+
+    def cells(name):
+        if name not in wr:
+            k = 1 if SCRATCH[name][0] == "psum" else SCRATCH[name][1][1]
+            wr[name] = np.zeros((len(names), k), np.int64)
+            rd[name] = np.zeros((len(names), k), np.int64)
+        return wr[name], rd[name]
+
+    def sl(r):
+        return slice(0, 1) if SCRATCH[r[0]][0] == "psum" else slice(r[1], r[2], r[3])
+
+    def wait(e, s, v):
+        if waited.get((e, s), 0) < v:
+            Q[e].wait_ge(T.sem[s], int(v))
+            waited[(e, s)] = v
+
+    def mark(s, v, reads, writes):
+        i = names.index(s)
+        for r in writes:
+            w, q = cells(r[0])
+            w[:, sl(r)] = 0
+            q[:, sl(r)] = 0
+            w[i, sl(r)] = v
+        for r in reads:
+            cells(r[0])[1][i, sl(r)] = v
+
+    def op(e, call, reads, writes, sem=None, inc=1, chain=False):
+        reads = [r for v in reads if isinstance(v, tuple) for r in v[1]]
+        writes = [r for v in writes for r in v[1]]
+        s = sem or "e" + e
+        need = np.zeros(len(names), np.int64)
+        for r in reads:
+            w, q = cells(r[0])
+            need = np.maximum(need, w[:, sl(r)].max(axis=1))
+            if SCRATCH[r[0]][0] == "psum":
+                o = q[:, 0].copy()
+                o[names.index(s)] = 0
+                need = np.maximum(need, o)
+        for r in writes:
+            w, q = cells(r[0])
+            need = np.maximum(need, np.maximum(w[:, sl(r)].max(axis=1), q[:, sl(r)].max(axis=1)))
+        if chain:
+            need[names.index(s)] = 0
+        for i in np.nonzero(need)[0]:
+            wait(e, names[i], need[i])
+        ins = call()
+        if ins is not None:
+            ins.then_inc(T.sem[s], inc)
+        count[s] = count.get(s, 0) + inc
+        mark(s, count[s], reads, writes)
+
+    def x(v):
+        return v[0] if isinstance(v, tuple) else v
+
+    def tt(o, a, b, f):
+        op("V", lambda: g.vector.tensor_tensor(o[0], a[0], b[0], f), [a, b], [o])
+
+    def ts(o, a, s1, f1, s2=None, f2=None):
+        if f2 is None:
+            op("V", lambda: g.vector.tensor_scalar(o[0], a[0], x(s1), None, f1), [a, s1], [o])
+        else:
+            op("V", lambda: g.vector.tensor_scalar(o[0], a[0], x(s1), x(s2), f1, f2), [a, s1, s2], [o])
+
+    def cp(o, a):
+        op("V", lambda: g.vector.tensor_copy(o[0], a[0]), [a], [o])
+
+    def scan(o, a, b, f0, f1):
+        op("V", lambda: g.vector.tensor_tensor_scan(o[0], a[0], b[0], 0.0, f0, f1), [a, b], [o])
+
+    def fill(o, c):
+        op("V", lambda: g.vector.memset(o[0], c), [], [o])
+
+    def act(o, a, f, scale=None, bias=None, acc=None):
+        kw = {}
+        if scale is not None:
+            kw["scale"] = scale
+        if bias is not None:
+            kw["bias"] = x(bias)
+        if acc is not None:
+            kw["accum_out"] = acc[0]
+        op("S", lambda: g.scalar.activation(o[0], a[0], f, **kw), [a, bias], [o] + ([acc] if acc else []))
+
+    def quant(name, src, lo=0, hi=None):
+        q, s = ap("q" + name, lo, hi), ap("s" + name, lo, hi)
+        op("V", lambda: g.vector.quantize_mx(q[0], s[0], src[0]), [src], [q, s])
+
+    def mm(bank, wn, w0, xn, lo, hi, start=True, stop=True):
+        o = ap("p%d" % bank, 0, hi - lo)
+        a = [ap("q" + wn, w0, w0 + 128), ap("s" + wn, w0, w0 + 128), ap("q" + xn, lo, hi), ap("s" + xn, lo, hi)]
+        op("P", lambda: g.tensor.matmul_mx(o[0], a[0][0], a[1][0], a[2][0], a[3][0], start, stop), a, [o], chain=not start)
+
+    def iota(o, pat, base=0, cm=0):
+        small = SCRATCH[o[1][0][0]][2] != "int32"
+        op("G", lambda: g.iota(o[0], pat, base, cm, allow_small_or_imprecise_dtypes=True) if small else g.iota(o[0], pat, base, cm), [], [o])
+
+    def aff(o, a, pat, f, fl, base, cm):
+        op("G", lambda: g.affine_select(o[0], a[0], pat, f, fl, base, cm), [a], [o])
+
+    def load(e, sem, o, src):
+        op(e, lambda: Q[e].dma_start(o[0], src), [], [o], sem=sem, inc=16)
+
+    def store(e, dst, src, view=None):
+        op(e, lambda: Q[e].dma_start(dst, src[0] if view is None else view), [src], [], sem="dout", inc=16)
+
+    def send(dst, o, a, sem):
+        rid, pid = topo.addr(dst)[:2]
+        mask = topo.mask(core, dst)
+
+        def call():
+            g.remote_dma(o[0], a[0], T.sem[sem], T.sem.snt, pid, rid, mask)
+        op("G", call, [a], [], sem="snt", inc=len(topo.engines(core, dst)))
+
+    def arrives(src, sem, views):
+        count[sem] = len(views) * len(topo.engines(src, core))
+        mark(sem, count[sem], [], [r for v in views for r in v[1]])
+
+    def cc(name, lo=0, hi=None, st=1):
+        a, w = CAT[name]
+        return ap("cc", a + lo, a + (w if hi is None else hi), st)
+
+    def cl(name, lo=0, hi=None):
+        a, w = LAT[name]
+        return ap("cl", a + lo, a + (w if hi is None else hi))
+
+    def ll(name, k):
+        a = LAT[name][0] // 16
+        return ap("ll", a, a + k)
+
+    def slot(k, t, lo, hi):
+        return ap("mt", 4 * (START[k] + lo) + t, 4 * (START[k] + hi), 4)
+
+    def gap(k):
+        lo = 16 * TILES[k][-1] if len(TILES[k]) == 4 else 0
+        return ap("mt", 4 * (START[k] + lo), 4 * (START[k] + WIDTH[k]))
+
+    def zero(o):
+        act(o, ap("zb", 0, o[1][0][2] - o[1][0][1]), F.Copy)
+
+    pm, pmoff, pc, pm10 = ap("pm", 0, 1), ap("pm", 1, 2), ap("pm", 2, 3), ap("pm", 3, 4)
+    X0 = 384
+    X = ap("xz", X0, X0 + 4 * C)
+    H = C // 2
+
+    def xb(b):
+        return ap("xz", X0 + b, X0 + 4 * C, 4)
+
+    def half(h):
+        return ap("xz", X0 + 4 * H * h, X0 + 4 * H * (h + 1))
+
+    def plane(b):
+        return ap("xp", C * b, C * b + C)
+
+    for t in range(R):
+        arrives(prv, "ar%d" % t, [ap("qa%d" % t), ap("sa%d" % t)])
+    arrives(prv, "aow", [ap("tab", 64, 92)])
+    arrives(nxt, "aw1", [ap("wl1")])
+    arrives(nxt, "aw2", [ap("wl2")])
+
+    load("Y", "dx", half(0), T.x[:, 0:2 * C])
+    load("Y", "dx2", half(1), T.x[:, 2 * C:4 * C])
+    load("S", "du", ap("ub"), T.u[:, :])
+    fill(ap("ones"), 1.0)
+    fill(ap("zb"), 0.0)
+    wait("Y", "dx2", 16)
+    zero(ap("yo"))
+    zf = [ap(k, lo, min(w, lo + C)) for k, w in (("cc", NC), ("cl", NL)) for lo in range(0, w, C)]
+    zh = [gap(k) for k in (1, 2, 3, 6, 7)] + [ap("eye", 512 * b, 512 * b + 512) for b in range(4)] + [ap("xz", 0, X0)]
+    for sem, src, zeros in (("dz2", "yo", zf), ("dz", "zb", zh)):
+        for o in zeros:
+            z = ap(src, 0, o[1][0][2] - o[1][0][1])
+            op("Y", lambda: g.sync.dma_start(o[0], z[0]), [z], [o], sem=sem, inc=16)
+        mark(sem, count[sem], [ap(src)[1][0]], [r for o in zeros for r in o[1]])
+    for t in range(1, 4):
+        load("Y", "d%d" % t, ap("xs%d" % t, 0, 4 * C - t), T.x[:, t:4 * C])
+    load("Y", "dw", u8(ap("qw")), T.wc[:, :])
+    load("Y", "dws", ap("sw"), T.ws[:, :])
+    load("Y", "dv", ap("vb"), T.v[:, :])
+
+    iota(ap("pi", 0, 1), [[0, 1]], 0, 1)
+    iota(ap("iq"), [[0, 30], [1, 16]])
+    iota(ap("ui"), [[1, 2], [16, 8]])
+    iota(ap("w2", 0, 16), [[0, 16]])
+    iota(ap("w2", 0, 9), [[16, 3], [48, 3]], 15)
+    iota(ap("w3", 0, 30), [[1, 10], [160, 3]])
+    for k in (4, 5, 0):
+        zero(gap(k))
+    ts(ap("pi", 1, 2), ap("pi", 0, 1), 15, A.bitwise_and)
+    cp(pm, ap("pi", 1, 2))
+    act(pmoff, pm, F.Identity, scale=-OFF, bias=15 * OFF)
+    act(pc, pm, F.Identity, scale=OFF - 1, bias=16 - 15 * OFF)
+    act(pm10, pm, F.Copy, scale=10.0)
+    ts(ap("dg"), ap("iq"), pm, A.is_equal)
+    ts(ap("keep"), ap("iq"), pm, A.is_gt)
+    cp(ap("ul"), ap("ui"))
+    act(ap("ext"), ap("keep"), F.Identity, scale=2.0 ** 20 + OFF, bias=-2.0 ** 20)
+    ts(ap("lp", 0, 30), ap("w3", 0, 30), pm10, A.add)
+    aff(ap("band0"), ap("ones"), [[-16, 8], [0, 64]], A.is_ge, 0.0, 0, 1)
+    aff(ap("band"), ap("band0"), [[16, 8], [0, 64]], A.is_ge, 0.0, 15, -1)
+    aff(ap("tri"), ap("band"), [[1, 128], [200, 4]], A.is_gt, 0.0, 0, -1)
+    quant("u", ap("ub"))
+    cp(u32(ap("qu0")), ind(u32(ap("qu")), ap("ul", 0, 8)))
+    act(ap("su0"), ind(ap("su"), ap("ul", 0, 8)), F.Copy)
+    zero(ap("rs", 0, 1))
+    zero(ap("tab", 0, 64))
+    iota(ap("jj"), [[1, C]])
+    iota(cc("c16"), [[16, 32]])
+    scan(ap("w1", 0, 16), ap("ext", 0, 16), ap("w2", 0, 16), A.add, A.max)
+    ts(ap("lt0", 0, 1), ap("w1", 15, 16), pmoff, A.subtract)
+
+    for lo, hi, pat, base in [(0, 4, [[0, 4]], 0), (4, 6, [[0, 2]], 1), (6, 8, [[1, 2]], 2), (8, 10, [[0, 2]], 1),
+                              (10, 14, [[0, 2], [1, 2]], 2), (14, 16, [[1, 2]], 3), (16, 24, [[1, 2], [1, 2], [1, 2]], 2)]:
+        iota(cc("IDX", lo, hi), pat, base)
+    for lo, hi, pat, base in [(0, 4, [[0, 4]], 7), (4, 6, [[0, 2]], 15), (6, 8, [[64, 2]], 23), (8, 10, [[0, 2]], 15),
+                              (10, 14, [[0, 2], [64, 2]], 23), (14, 16, [[8, 2]], 87), (16, 18, [[64, 2]], 23),
+                              (18, 22, [[0, 2], [8, 2]], 87), (22, 24, [[8, 2]], 95)]:
+        iota(cc("FX", lo, hi), pat, base)
+    for i in range(3):
+        iota(cc("NA", 8 * i, 8 * i + 8), [[3, 2], [3, 2], [3, 2]], 9 + 3 * i)
+    iota(cl("LA", 0, 72), [[48, 3], [0, 24]], 47)
+    iota(cl("LD", 0, 12), [[48, 3], [16, 2], [0, 2]], 15)
+    iota(cl("LR", 0, 24), [[0, 4], [2, 2], [4, 3]], 1)
+    iota(cl("LR0", 0, 24), [[0, 4], [1, 6]])
+    iota(cl("LR5", 0, 24), [[0, 4], [10, 2], [20, 3]], 4)
+    iota(cl("LH", 0, 24), [[0, 4], [5, 2], [10, 3]], 64)
+    iota(cl("LE", 0, 12), [[24, 3], [0, 2], [8, 2]], 7)
+    iota(cl("LC", 0, 60), [[1, 3], [0, 20]])
+    iota(cl("LC", 60, 90), [[1, 3], [0, 10]])
+    for c in range(3):
+        iota(cl("LT", 20 * c, 20 * c + 20), [[3, 2], [0, 2], [3, 5]], c)
+    iota(cl("LT", 60, 90), [[1, 3], [3, 2], [3, 5]], 32)
+    iota(cl("LS", 0, 81), [[0, 9], [8, 9]], 7)
+    iota(cl("LO", 0, 81), [[1, 27], [0, 3]])
+    iota(cl("LK", 0, 30), [[1, 3], [3, 10]])
+    for b in range(4):
+        aff(ap("eye", 513 * b, 512 * b + 512, 4), ap("ones", 0, 128), [[1, 128]], A.is_equal, 0.0, 0, -1)
+    iota(cc("X8"), [[0, 10], [1, 8]])
+    aff(cc("K8"), ap("ones", 0, 240), [[0, 30], [1, 8]], A.is_gt, 0.0, 0, 0)
+    aff(ap("acs"), ap("ones", 0, NS), [[0, 9], [1, 16]], A.is_gt, 2.0, 0, 0)
+    aff(ap("h144"), ap("acs"), [[0, 3], [1, 48]], A.is_gt, 0.0, 0, 0)
+    iota(cc("DUM"), [[16, 32]])
+    iota(cc("T4", 0, 24), [[1, 4], [0, 6]], X0)
+    iota(cc("S0", 0, 24), [[NS, 4], [16, 2], [48, 3]])
+    iota(cc("TH0"), [[0, 4], [2, 2], [0, 2]], 1)
+    for c in range(3):
+        iota(cc("N0", c, 9, 3), [[16385, 3]], 49200 * c + 1)
+        iota(cc("NV", 24 * c + 7, 24 * c + 24, 8), [[16385, 3]], 49200 * c + 1)
+    iota(cc("HB", 0, 24), [[NS, 4], [0, 6]])
+    iota(cc("J5", 0, 90), [[0, 18], [1, 5]])
+    aff(cc("K5", 0, 90), ap("ones", 0, 90), [[0, 18], [1, 5]], A.is_gt, 0.0, 0, 0)
+    aff(cc("K3"), ap("ones", 0, 96), [[0, 32], [1, 3]], A.is_gt, 0.0, 0, 0)
+    iota(cc("H4"), [[0, 4], [1, 2], [1, 2]])
+
+    used = [0]
+
+    def scores(h):
+        quant("x", half(h), H * h, H * h + H)
+        mm(4 + h, "u0", 0, "x", H * h, H * h + H)
+
+    def columns(h):
+        tt(ap("mm", H * h, H * h + H), ap("p%d" % (4 + h), 0, H), ap("dg", 0, H), A.mult)
+        scan(ap("yy", H * h, H * h + H), ap("keep", 0, H), ap("mm", H * h, H * h + H), A.mult, A.add)
+
+    def pack(k):
+        quant("m", ap("mt", 4 * START[k], 4 * (START[k] + WIDTH[k])), START[k], START[k] + WIDTH[k])
+
+    def count_tile(k):
+        mm(2, "r" if k == 0 else "b", 0, "m", START[k], START[k] + WIDTH[k], k == 0, k == len(TILES) - 1)
+
+    def compare(k, bank):
+        for t, c in enumerate(TILES[k]):
+            if c != "d" and c not in ON_SCALAR:
+                w = 16 * c
+                ts(slot(k, t, 0, w), ap(bank, 0, w), ap("yy", w + 15, w + 16), A.is_lt)
+                act(ap("junk", used[0], used[0] + w), slot(k, t, 0, w), F.Identity, acc=ap("rs", c, c + 1))
+                used[0] += w
+
+    def on_scalar(k):
+        for t, c in enumerate(TILES[k]):
+            if c in ON_SCALAR:
+                i = ON_SCALAR.index(c)
+                act(ap("sg", C * i, C * i + 16 * c), ap("p1", 0, 16 * c), F.Sign, scale=-1.0, bias=ap("yy", 16 * c + 15, 16 * c + 16))
+        for t, c in enumerate(TILES[k]):
+            if c in ON_SCALAR:
+                i = ON_SCALAR.index(c)
+                act(slot(k, t, 0, 16 * c), ap("sg", C * i, C * i + 16 * c), F.Relu, acc=ap("rs", c, c + 1))
+
+    scores(0)
+    columns(0)
+    compare(4, "p4")
+    scores(1)
+    mm(1, "u0", 0, "x", 0, C)
+    mm(0, "u0", 0, "x", 0, C)
+    compare(5, "p4")
+    columns(1)
+    act(ap("c0", 0, 30), cc("c16", 0, 30), F.Identity, bias=pc)
+    on_scalar(0)
+    on_scalar(1)
+    tt(slot(0, 0, 0, C), ap("p0", 0, C), ap("yy"), A.is_le)
+    pack(4)
+    pack(5)
+    quant("r", ap("tri"))
+    quant("b", ap("band"))
+    compare(0, "p0")
+    scan(ap("rowd"), ap("keep"), slot(0, 0, 0, C), A.mult, A.add)
+    compare(1, "p0")
+    pack(0)
+    for k in (0, 4, 5):
+        count_tile(k)
+    tt(ap("w1", 0, 30), ap("c0", 0, 30), ap("rowd", 15, C, 16), A.subtract)
+    for k, j in ((2, 1), (3, 2), (6, 3), (7, 6)):
+        compare(k, "p0")
+        pack(j)
+        count_tile(j)
+    pack(7)
+    count_tile(7)
+    for c in range(3):
+        for o in (cl("LW0", 24 * c, 24 * c + 24), cl("L3", 80 + 24 * c, 104 + 24 * c)):
+            act(o, cc("IDX"), F.Identity, scale=3.0, bias=float(c))
+        act(cl("L3", 24 * c, 24 * c + 24), cc("NA"), F.Identity, bias=64.0 + c)
+        act(cl("L3", 160 + 24 * c, 184 + 24 * c), cc("NA"), F.Identity, bias=float(c))
+        act(cl("LW1", 24 * c, 24 * c + 24), cc("FX"), F.Identity, bias=24.0 * c)
+    act(ap("su1"), ind(ap("su"), ap("ul", 8, 16)), F.Copy)
+    act(ap("cm"), ap("dg", 0, NS), F.Identity, scale=-2 * BIG, bias=BIG)
+    act(ap("dum"), cc("DUM"), F.Identity, bias=pm)
+    for t in range(R):
+        act(ap("pm", 4 + t, 5 + t), pm, F.Identity, scale=1027.0 / 1024, bias=t * (4 * NS + NS / 1024))
+    tt(ap("w2", 0, 30), ap("w1", 0, 30), ap("rs", 0, 30), A.subtract)
+    scan(ap("ex"), ap("ext"), ap("p2", 0, C), A.add, A.max)
+    tt(ap("w1", 0, 30), ap("w2", 0, 30), ap("ex", 15, C, 16), A.add)
+    cp(ap("pos"), ap("w1", 0, 30))
+    op("V", lambda: g.vector.tensor_copy(T.ob[:, :].indirect(T.pos[:, :]), T.jj[:, :]), [ap("pos"), ap("jj")], [ap("ob")])
+    cp(ap("mm", 0, NS), ind(ap("ob"), ap("lp", 0, 9)))
+    act(ap("yy", 0, 320), ind(ap("ob"), ap("lp", 8, 28)), F.Copy)
+    scan(ap("ex", 0, NS), ap("ext", 0, NS), ap("mm", 0, NS), A.add, A.max)
+    ts(ap("tl0"), ind(ap("ex", 0, NS), ap("lt0", 0, 1)), pmoff, A.subtract, 4.0, A.mult)
+
+    def gather_t(b, win, lst, scale, on_v):
+        o = ap("tt", b, 4 * NS, 4)
+        if on_v:
+            ts(o, ind(win, lst), scale, A.mult)
+        else:
+            act(o, ind(win, lst), F.Copy, scale=scale)
+
+    def send_t(t):
+        quant("t%d" % t, ap("tt"))
+        send(nxt, u8(ap("qa%d" % t)), u8(ap("qt%d" % t)), "ar%d" % t)
+        send(nxt, ap("sa%d" % t), ap("st%d" % t), "ar%d" % t)
+
+    for b in range(3):
+        gather_t(b, X if b == 0 else ap("xs%d" % b, 0, 4 * C - 3), ap("tl0", 0, 9), 1.0, False)
+    scan(ap("ex", NS, 448), ap("ext", NS, 448), ap("yy", 16, 320), A.add, A.max)
+    ts(ap("tab", 0, 28), ap("ex", 15, 448, 16), pmoff, A.subtract, 4.0, A.mult)
+    send(nxt, ap("tab", 64, 92), ap("tab", 0, 28), "aow")
+    gather_t(3, ap("xs3", 0, 4 * C - 3), ap("tl0", 0, 9), 1.0, True)
+    send_t(0)
+
+    def lists_of_targets(src, w):
+        a = CAT["T4"][0]
+        tt(ap("tg", 0, w), src, ap("cc", a, a + w), A.add)
+        cp(ap("gl", 0, w), ap("tg", 0, w))
+        act(ap("xg"), ind(ap("xz"), ap("gl", 0, 24)), F.Copy, scale=0.5)
+
+    def own_scores():
+        tt(ap("bp"), ind(ap("s1"), ap("bl16", 0, 9)), ap("cm"), A.max)
+
+    def choose(out, lo, w, win, lst):
+        tt(ap("pr", 0, w), ind(win, ll(lst, w // 16)), ap("oh", 0, w), A.mult)
+        scan(ap(out, lo, lo + w), cc("K8", 0, w), ap("pr", 0, w), A.mult, A.add)
+
+    cp(u32(ap("qu1")), ind(u32(ap("qu")), ap("ul", 8, 16)))
+    mm(3, "u1", 0, "x", 0, C)
+    act(ap("s1"), ap("p3", 0, C), F.Copy)
+    for lo in range(0, NL, C):
+        hi = min(NL, lo + C)
+        scan(ap("cls", lo, hi), ap("ext", 0, hi - lo), ap("cl", lo, hi), A.add, A.max)
+    ts(ap("ll"), ap("cls", 15, NL, 16), pmoff, A.subtract)
+    lists_of_targets(ind(ap("tab", 0, 32), ll("LR0", 2)), 32)
+    quant("e", ap("eye"))
+    ts(ap("bl16"), ind(ap("ex", 0, NS), ap("lt0", 0, 1)), pmoff, A.subtract)
+    own_scores()
+    ts(ap("gl", 32, 56), cc("S0", 0, 24), pm, A.add)
+    quant("v", ap("vb"))
+    act(ap("tab", 32, 41), cc("N0", 0, 9), F.Identity, scale=1.0 / 1024, bias=ap("pm", 4, 5))
+    act(ap("orep"), ind(ap("tab", 0, 32), ll("LO", 6)), F.Copy)
+
+    for t in range(R):
+        last = t == R - 1
+        a = "a%d" % t
+        mm(0, "u1", 0, a, 0, NS)
+        for b in range(4):
+            mm(4 + b, "e", 128 * b, a, 0, NS)
+        for b in range(4):
+            act(ap("hh", 4 * NS * t + NS * b, 4 * NS * t + NS * b + NS), ap("p%d" % (4 + b), 0, NS), F.Copy, scale=0.5)
+        tt(ap("cmp"), ap("p0", 0, NS), ap("bp"), A.is_ge)
+        scan(ap("hs"), ap("h144"), ap("cmp"), A.mult, A.add)
+        if not last:
+            tt(ap("oh", 0, 80), ind(ap("hs"), ll("LA", 5)), cc("X8"), A.is_equal)
+            choose("l%d" % t, 0, 80, ap("tab", 64, 92) if t == 0 else ap("l0", 0, 160), "LW%d" % t)
+            ts(ap("ws%d" % (t + 1)), ap("l%d" % t, 7, 80, 8), 0.25, A.mult)
+            send(prv, ap("wl%d" % (t + 1)), ap("ws%d" % (t + 1)), "aw%d" % (t + 1))
+            act(ap("nv", 96 * t, 96 * t + 96), ind(cc("NV"), ll("LS", 6)), F.Identity, scale=1.0 / 1024, bias=ap("pm", 5 + t, 6 + t))
+        if t == 0:
+            for h in (1, 2):
+                act(ap("oh", 80 * h, 80 * h + 80), ap("oh", 0, 80), F.Copy)
+        if t == 1:
+            aff(ap("k16"), ap("ones", 0, NS), [[0, 9], [1, 16]], A.is_gt, 0.0, 0, 0)
+            iota(ap("an"), [[0, 80]])
+            iota(ap("fr"), [[0, 32]], -1)
+        tt(ap("dd"), ind(ap("hs"), ll("LD", 1)), cc("TH0") if t == 0 else ap("th"), A.is_ge)
+        tt(ap("w1"), ind(ap("dd"), ll("LR", 2)), ap("tg", 0, 32), A.mult)
+        tt(ap("w2"), ap("w1"), ap("dum"), A.max)
+        cp(ap("sl"), ap("w2"))
+        tt(ap("bl"), ind(ap("hh", 0, 4 * NS * (t + 1)), ap("gl", 32, 56)), ap("xg"), A.add)
+        op("V", lambda: g.vector.tensor_copy(T.xz[:, :].indirect(T.sl[:, 0:24]), T.bl[:, :]), [ap("sl", 0, 24), ap("bl")], [ap("xz")])
+        quant("z", X)
+        for b in range(4):
+            act(plane(b), xb(b), F.Copy, scale=32.0)
+            mm(b, "w", 128 * b, "z", 0, C)
+        if t == 0:
+            tt(ap("cu", 0, 3), ap("dd", 1, 12, 4), ap("dd", 3, 12, 4), A.add)
+        elif t == 1:
+            tt(ap("cu", 4, 7), ap("dd", 1, 12, 4), ap("dd", 3, 12, 4), A.add)
+            tt(ap("cu", 8, 11), ap("cu", 0, 3), ap("cu", 4, 7), A.add)
+        if not last:
+            tt(ap("o5"), ind(ap("cu", 8 * t, 8 * t + 3), ll("LC", 6)), cc("J5"), A.is_equal)
+        else:
+            scan(ap("acs"), ap("k16"), ap("cmp"), A.mult, A.add)
+            cp(ap("an", 7, 72, 8), ap("acs", 15, NS, 16))
+        for b in range(4):
+            tt(plane(b), ap("p%d" % b, 0, C), plane(b), A.add)
+            if not last:
+                gather_t(b, plane(b), ap("wl%d" % (t + 1), 0, 9), 2.0 ** -5, False)
+        if last:
+            break
+        ts(xb(3), plane(3), 2.0 ** -5, A.mult)
+        send_t(t + 1)
+        for b in range(3):
+            act(xb(b), plane(b), F.Copy, scale=2.0 ** -5)
+        if t == 0:
+            choose("l0", 80, 240, ap("tab", 0, 92), "L3")
+            own = ap("l0", 160, 240)
+        else:
+            choose("l1", 80, 80, ap("l0", 160, 320), "LW1")
+            own = ap("l1", 80, 160)
+        k0 = own[1][0][1]
+        ts(ap("bl16", 0, 9), ap(own[1][0][0], k0 + 7, k0 + 72, 8), 0.25, A.mult)
+        tt(ap("o2"), ind(own, ll("LS", 6)), ap("orep"), A.is_equal)
+        tt(ap("pr", 0, 81), ap("o2", 0, 81), ap("nv", 96 * t, 96 * t + 81), A.mult)
+        scan(ap("sel", 0, 81), cc("K3", 0, 81), ap("pr", 0, 81), A.mult, A.max)
+        tt(ap("tab", 32, 59), ap("tab", 32, 59), ap("sel", 2, 81, 3), A.max)
+        if t == 1:
+            ts(ap("w3", 0, 27), ap("tab", 32, 59), MAGIC, A.add, MAGIC, A.subtract)
+            act(ap("c0", 0, 27), ap("w3", 0, 27), F.Identity, bias=1.0 / 1024)
+        quant("x", X)
+        mm(4, "u1", 0, "x", 0, C)
+        act(ap("s1"), ap("p4", 0, C), F.Copy)
+        tt(ap("pr", 0, 96), ind(ap("tab", 0, 64), ll("LT", 6)), ap("o5"), A.mult)
+        scan(ap("sel", 0, 90), cc("K5", 0, 90), ap("pr", 0, 90), A.mult, A.add)
+        lists_of_targets(ind(ap("sel", 0, 90), ll("LR5", 4)), 64)
+        tt(ap("eq"), ind(own, ll("LE", 1)), ap("sel", 4, 80, 5), A.is_equal)
+        scan(ap("th"), cc("H4"), ap("eq"), A.mult, A.add)
+        if t == 1:
+            tt(ap("w4", 0, 27), ap("tab", 32, 59), ap("c0", 0, 27), A.subtract)
+        own_scores()
+
+    for h in range(2):
+        for b in range(4):
+            o, a = ap("xz", X0 + 4 * H * h + b, X0 + 4 * H * (h + 1), 4), ap("xp", C * b + H * h, C * b + H * h + H)
+            if b < 2:
+                act(o, a, F.Copy, scale=2.0 ** -5)
+            else:
+                ts(o, a, 2.0 ** -5, A.mult)
+        quant("x", half(h), H * h, H * h + H)
+        mm(4 + h, "v", 0, "x", H * h, H * h + H)
+        store("Y", T.oc[:, 4 * H * h:4 * H * (h + 1)], u8(ap("qx", H * h, H * h + H)))
+    for h in range(2):
+        act(ap("yo", H * h, H * h + H), ap("p%d" % (4 + h), 0, H), F.Copy)
+        store("S", T.y[:, H * h:H * h + H], ap("yo", H * h, H * h + H))
+    for k in range(4):
+        store("Y", T.osc[4 * k:4 * k + 4, :], ap("sx"), T.sx[32 * k:32 * k + 4, :])
+    tt(ap("pr", 0, 96), ind(ap("an"), ll("LS", 6)), ap("o2"), A.is_lt)
+    scan(ap("sel", 0, 81), cc("K3", 0, 81), ap("pr", 0, 81), A.mult, A.max)
+    tt(ap("fr", 0, 27), ap("w4", 0, 27), ap("sel", 2, 81, 3), A.subtract)
+    ts(ap("sko"), ind(ap("fr"), ll("LK", 2)), 1024.0, A.mult, -1.0, A.max)
+    for c in range(3):
+        store("YSY"[c], T.sk[:, 160 * c:160 * c + 160], ap("sko", 10 * c, 10 * c + 10))
+    for s in names:
+        if count.get(s, 0):
+            wait("Y", s, count[s])

@@ -3,13 +3,14 @@ from concourse.mybir import dt, AluOpType as A, ActivationFunctionType as F
 
 C, NS, R = 480, 144, 3
 BIG, MAGIC, OFF = 1e29, 12582912.0, 1024.0
+X0 = 2048
 TILES = [["d", 29, 28, 27]] + [[c for c in range(h, h - 4, -1) if c > 0] for h in range(26, 0, -4)]
 WIDTH = [480] + [max(128, 16 * t[0]) for t in TILES[1:]]
 START = [sum(WIDTH[:i]) for i in range(len(WIDTH))]
 ON_SCALAR = (29, 28, 27)
 LISTS = [("LA", 96), ("LW0", 96), ("L3", 256), ("LW1", 96), ("LD", 32), ("LR", 32), ("LR0", 32), ("LR5", 32), ("LH", 32),
          ("LE", 32), ("LC", 96), ("LT", 96), ("LS", 96), ("LO", 96), ("LK", 32)]
-CONSTS = [("c16", 32), ("X8", 80), ("J5", 96), ("NV", 80), ("N0", 16), ("DUM", 32), ("T4", 32), ("HB", 32), ("S0", 32),
+CONSTS = [("c16", 32), ("X8", 80), ("J5", 96), ("NV", 80), ("N0", 16), ("T4", 32), ("HB", 32), ("S0", 32),
           ("TH0", 16), ("IDX", 24), ("NA", 24), ("FX", 24), ("K8", 240), ("K5", 96), ("K3", 96), ("H4", 16)]
 LAT = {k: (sum(v for _, v in LISTS[:i]), w) for i, (k, w) in enumerate(LISTS)}
 CAT = {k: (sum(v for _, v in CONSTS[:i]), w) for i, (k, w) in enumerate(CONSTS)}
@@ -27,14 +28,14 @@ def _mx(name, n):
     _sb("s" + name, n, "uint8")
 
 
-for _k, _w in [("xz", 4 * C + 384), ("xp", 4 * C), ("xs1", 4 * C), ("xs2", 4 * C), ("xs3", 4 * C), ("ub", 512), ("vb", 512),
+for _k, _w in [("xz", 4 * C + X0), ("xp", 4 * C), ("xs1", 4 * C), ("xs2", 4 * C), ("xs3", 4 * C), ("ub", 512), ("vb", 512),
                ("ones", 512), ("zb", 512), ("band0", 512), ("band", 512), ("tri", 512), ("eye", 2048), ("iq", C), ("dg", C), ("keep", C),
                ("ext", C), ("mt", 4 * sum(WIDTH)), ("junk", 7000), ("sg", 4 * C), ("rowd", C), ("tt", 4 * NS), ("hh", 4 * NS * R),
                ("xg", 384), ("bl", 384), ("cmp", NS), ("hs", NS), ("acs", NS), ("k16", NS), ("h144", NS)]:
     _sb(_k, _w, "bfloat16")
 for _k, _w in [("pm", 8), ("cc", NC), ("cl", NL), ("cls", NL), ("mm", C), ("yy", C), ("jj", C), ("ob", C), ("ex", C), ("rs", 32), ("w1", 32),
                ("w2", 32), ("w3", 32), ("w4", 32), ("c0", 32), ("tab", 96), ("orep", 96), ("s1", C), ("bp", NS), ("cm", NS), ("oh", 240),
-               ("pr", 240), ("l0", 320), ("l1", 160), ("dd", 16), ("th", 16), ("cu", 16), ("tg", 64), ("nv", 192), ("dum", 32), ("o2", 96),
+               ("pr", 240), ("l0", 320), ("l1", 160), ("dd", 16), ("th", 16), ("cu", 16), ("tg", 64), ("nv", 192), ("tf", 32), ("o2", 96),
                ("o5", 96), ("sel", 96), ("eq", 16), ("fr", 32), ("an", 80), ("yo", C), ("sko", 32)]:
     _sb(_k, _w, "float32")
 for _k, _w in [("pi", 8), ("ui", 16)]:
@@ -49,7 +50,7 @@ for _t in range(R):
     _mx("a%d" % _t, NS)
 for _t in range(8):
     SCRATCH["p%d" % _t] = ("psum", [128, 512], "float32")
-DMAS = ["dx", "dx2", "du", "dv", "dw", "dws", "d1", "d2", "d3", "dz", "dz2", "dout"]
+DMAS = ["dx", "dx2", "du", "dv", "dw", "dws", "d1", "d2", "d3", "dz", "dz2", "dz3", "dout"]
 SEMAPHORES = ["eV", "eS", "eP", "eG", "snt", "ar0", "ar1", "ar2", "aow", "aw1", "aw2"] + DMAS
 
 
@@ -214,7 +215,6 @@ def rank_program(g, core, T, topo):
         act(o, ap("zb", 0, o[1][0][2] - o[1][0][1]), F.Copy)
 
     pm, pmoff, pc, pm10 = ap("pm", 0, 1), ap("pm", 1, 2), ap("pm", 2, 3), ap("pm", 3, 4)
-    X0 = 384
     X = ap("xz", X0, X0 + 4 * C)
     H = C // 2
 
@@ -240,9 +240,10 @@ def rank_program(g, core, T, topo):
     fill(ap("zb"), 0.0)
     wait("Y", "dx2", 16)
     zero(ap("yo"))
-    zf = [ap(k, lo, min(w, lo + C)) for k, w in (("cc", NC), ("cl", NL)) for lo in range(0, w, C)]
-    zh = [gap(k) for k in (1, 2, 3, 6, 7)] + [ap("eye", 512 * b, 512 * b + 512) for b in range(4)] + [ap("xz", 0, X0)]
-    for sem, src, zeros in (("dz2", "yo", zf), ("dz", "zb", zh)):
+    zf = [ap("cl", lo, min(NL, lo + C)) for lo in range(0, NL, C)]
+    zg = [gap(k) for k in (2, 3, 6, 7)]
+    zh = [ap("eye", 512 * b, 512 * b + 512) for b in range(4)]
+    for sem, src, zeros in (("dz2", "yo", zf), ("dz3", "zb", zg), ("dz", "zb", zh)):
         for o in zeros:
             z = ap(src, 0, o[1][0][2] - o[1][0][1])
             op("Y", lambda: g.sync.dma_start(o[0], z[0]), [z], [o], sem=sem, inc=16)
@@ -262,27 +263,28 @@ def rank_program(g, core, T, topo):
     for k in (4, 5, 0):
         zero(gap(k))
     ts(ap("pi", 1, 2), ap("pi", 0, 1), 15, A.bitwise_and)
+    fill(gap(1), 0.0)
     cp(pm, ap("pi", 1, 2))
     act(pmoff, pm, F.Identity, scale=-OFF, bias=15 * OFF)
     act(pc, pm, F.Identity, scale=OFF - 1, bias=16 - 15 * OFF)
     act(pm10, pm, F.Copy, scale=10.0)
-    ts(ap("dg"), ap("iq"), pm, A.is_equal)
     ts(ap("keep"), ap("iq"), pm, A.is_gt)
+    ts(ap("dg"), ap("iq"), pm, A.is_equal)
     cp(ap("ul"), ap("ui"))
     act(ap("ext"), ap("keep"), F.Identity, scale=2.0 ** 20 + OFF, bias=-2.0 ** 20)
-    ts(ap("lp", 0, 30), ap("w3", 0, 30), pm10, A.add)
     aff(ap("band0"), ap("ones"), [[-16, 8], [0, 64]], A.is_ge, 0.0, 0, 1)
     aff(ap("band"), ap("band0"), [[16, 8], [0, 64]], A.is_ge, 0.0, 15, -1)
     aff(ap("tri"), ap("band"), [[1, 128], [200, 4]], A.is_gt, 0.0, 0, -1)
     quant("u", ap("ub"))
+    ts(ap("lp", 0, 30), ap("w3", 0, 30), pm10, A.add)
     cp(u32(ap("qu0")), ind(u32(ap("qu")), ap("ul", 0, 8)))
     act(ap("su0"), ind(ap("su"), ap("ul", 0, 8)), F.Copy)
     zero(ap("rs", 0, 1))
     zero(ap("tab", 0, 64))
+    for lo in range(0, NC, 512):
+        zero(ap("cc", lo, min(NC, lo + 512)))
     iota(ap("jj"), [[1, C]])
     iota(cc("c16"), [[16, 32]])
-    scan(ap("w1", 0, 16), ap("ext", 0, 16), ap("w2", 0, 16), A.add, A.max)
-    ts(ap("lt0", 0, 1), ap("w1", 15, 16), pmoff, A.subtract)
 
     for lo, hi, pat, base in [(0, 4, [[0, 4]], 0), (4, 6, [[0, 2]], 1), (6, 8, [[1, 2]], 2), (8, 10, [[0, 2]], 1),
                               (10, 14, [[0, 2], [1, 2]], 2), (14, 16, [[1, 2]], 3), (16, 24, [[1, 2], [1, 2], [1, 2]], 2)]:
@@ -314,18 +316,9 @@ def rank_program(g, core, T, topo):
     aff(cc("K8"), ap("ones", 0, 240), [[0, 30], [1, 8]], A.is_gt, 0.0, 0, 0)
     aff(ap("acs"), ap("ones", 0, NS), [[0, 9], [1, 16]], A.is_gt, 2.0, 0, 0)
     aff(ap("h144"), ap("acs"), [[0, 3], [1, 48]], A.is_gt, 0.0, 0, 0)
-    iota(cc("DUM"), [[16, 32]])
-    iota(cc("T4", 0, 24), [[1, 4], [0, 6]], X0)
+    iota(cc("T4", 0, 24), [[1, 4], [0, 6]])
     iota(cc("S0", 0, 24), [[NS, 4], [16, 2], [48, 3]])
     iota(cc("TH0"), [[0, 4], [2, 2], [0, 2]], 1)
-    for c in range(3):
-        iota(cc("N0", c, 9, 3), [[16385, 3]], 49200 * c + 1)
-        iota(cc("NV", 24 * c + 7, 24 * c + 24, 8), [[16385, 3]], 49200 * c + 1)
-    iota(cc("HB", 0, 24), [[NS, 4], [0, 6]])
-    iota(cc("J5", 0, 90), [[0, 18], [1, 5]])
-    aff(cc("K5", 0, 90), ap("ones", 0, 90), [[0, 18], [1, 5]], A.is_gt, 0.0, 0, 0)
-    aff(cc("K3"), ap("ones", 0, 96), [[0, 32], [1, 3]], A.is_gt, 0.0, 0, 0)
-    iota(cc("H4"), [[0, 4], [1, 2], [1, 2]])
 
     used = [0]
 
@@ -333,8 +326,10 @@ def rank_program(g, core, T, topo):
         quant("x", half(h), H * h, H * h + H)
         mm(4 + h, "u0", 0, "x", H * h, H * h + H)
 
-    def columns(h):
+    def own_column(h):
         tt(ap("mm", H * h, H * h + H), ap("p%d" % (4 + h), 0, H), ap("dg", 0, H), A.mult)
+
+    def spread(h):
         scan(ap("yy", H * h, H * h + H), ap("keep", 0, H), ap("mm", H * h, H * h + H), A.mult, A.add)
 
     def pack(k):
@@ -343,9 +338,9 @@ def rank_program(g, core, T, topo):
     def count_tile(k):
         mm(2, "r" if k == 0 else "b", 0, "m", START[k], START[k] + WIDTH[k], k == 0, k == len(TILES) - 1)
 
-    def compare(k, bank):
+    def compare(k, bank, slots=range(4)):
         for t, c in enumerate(TILES[k]):
-            if c != "d" and c not in ON_SCALAR:
+            if t in slots and c != "d" and c not in ON_SCALAR:
                 w = 16 * c
                 ts(slot(k, t, 0, w), ap(bank, 0, w), ap("yy", w + 15, w + 16), A.is_lt)
                 act(ap("junk", used[0], used[0] + w), slot(k, t, 0, w), F.Identity, acc=ap("rs", c, c + 1))
@@ -362,24 +357,27 @@ def rank_program(g, core, T, topo):
                 act(slot(k, t, 0, 16 * c), ap("sg", C * i, C * i + 16 * c), F.Relu, acc=ap("rs", c, c + 1))
 
     scores(0)
-    columns(0)
+    scan(ap("w1", 0, 16), ap("ext", 0, 16), ap("w2", 0, 16), A.add, A.max)
+    own_column(0)
+    ts(ap("lt0", 0, 1), ap("w1", 15, 16), pmoff, A.subtract)
+    spread(0)
     compare(4, "p4")
     scores(1)
     mm(1, "u0", 0, "x", 0, C)
     mm(0, "u0", 0, "x", 0, C)
-    compare(5, "p4")
-    columns(1)
-    act(ap("c0", 0, 30), cc("c16", 0, 30), F.Identity, bias=pc)
+    compare(5, "p4", (0, 1, 2))
+    own_column(1)
+    compare(5, "p4", (3,))
+    spread(1)
     on_scalar(0)
-    on_scalar(1)
-    tt(slot(0, 0, 0, C), ap("p0", 0, C), ap("yy"), A.is_le)
+    act(ap("c0", 0, 30), cc("c16", 0, 30), F.Identity, bias=pc)
     pack(4)
+    tt(slot(0, 0, 0, C), ap("p0", 0, C), ap("yy"), A.is_le)
     pack(5)
-    quant("r", ap("tri"))
-    quant("b", ap("band"))
-    compare(0, "p0")
     scan(ap("rowd"), ap("keep"), slot(0, 0, 0, C), A.mult, A.add)
     compare(1, "p0")
+    quant("r", ap("tri"))
+    quant("b", ap("band"))
     pack(0)
     for k in (0, 4, 5):
         count_tile(k)
@@ -398,7 +396,6 @@ def rank_program(g, core, T, topo):
         act(cl("LW1", 24 * c, 24 * c + 24), cc("FX"), F.Identity, bias=24.0 * c)
     act(ap("su1"), ind(ap("su"), ap("ul", 8, 16)), F.Copy)
     act(ap("cm"), ap("dg", 0, NS), F.Identity, scale=-2 * BIG, bias=BIG)
-    act(ap("dum"), cc("DUM"), F.Identity, bias=pm)
     for t in range(R):
         act(ap("pm", 4 + t, 5 + t), pm, F.Identity, scale=1027.0 / 1024, bias=t * (4 * NS + NS / 1024))
     tt(ap("w2", 0, 30), ap("w1", 0, 30), ap("rs", 0, 30), A.subtract)
@@ -431,17 +428,31 @@ def rank_program(g, core, T, topo):
     gather_t(3, ap("xs3", 0, 4 * C - 3), ap("tl0", 0, 9), 1.0, True)
     send_t(0)
 
-    def lists_of_targets(src, w):
+    for c in range(3):
+        iota(cc("N0", c, 9, 3), [[16385, 3]], 49200 * c + 1)
+        iota(cc("NV", 24 * c + 7, 24 * c + 24, 8), [[16385, 3]], 49200 * c + 1)
+    iota(cc("HB", 0, 24), [[NS, 4], [0, 6]])
+    iota(cc("J5", 0, 90), [[0, 18], [1, 5]])
+    aff(cc("K5", 0, 90), ap("ones", 0, 90), [[0, 18], [1, 5]], A.is_gt, 0.0, 0, 0)
+    aff(cc("K3"), ap("ones", 0, 96), [[0, 32], [1, 3]], A.is_gt, 0.0, 0, 0)
+    iota(cc("H4"), [[0, 4], [1, 2], [1, 2]])
+
+    def targets(src, w):
         a = CAT["T4"][0]
         tt(ap("tg", 0, w), src, ap("cc", a, a + w), A.add)
+
+    def gather_targets(w):
         cp(ap("gl", 0, w), ap("tg", 0, w))
-        act(ap("xg"), ind(ap("xz"), ap("gl", 0, 24)), F.Copy, scale=0.5)
+        act(ap("tf"), ap("tg", 0, 32), F.Copy, scale=1.0 / X0)
+        act(ap("xg"), ind(X, ap("gl", 0, 24)), F.Copy, scale=0.5)
 
     def own_scores():
         tt(ap("bp"), ind(ap("s1"), ap("bl16", 0, 9)), ap("cm"), A.max)
 
-    def choose(out, lo, w, win, lst):
+    def weigh(w, win, lst):
         tt(ap("pr", 0, w), ind(win, ll(lst, w // 16)), ap("oh", 0, w), A.mult)
+
+    def collect(out, lo, w):
         scan(ap(out, lo, lo + w), cc("K8", 0, w), ap("pr", 0, w), A.mult, A.add)
 
     cp(u32(ap("qu1")), ind(u32(ap("qu")), ap("ul", 8, 16)))
@@ -450,15 +461,14 @@ def rank_program(g, core, T, topo):
     for lo in range(0, NL, C):
         hi = min(NL, lo + C)
         scan(ap("cls", lo, hi), ap("ext", 0, hi - lo), ap("cl", lo, hi), A.add, A.max)
-    ts(ap("ll"), ap("cls", 15, NL, 16), pmoff, A.subtract)
-    lists_of_targets(ind(ap("tab", 0, 32), ll("LR0", 2)), 32)
-    quant("e", ap("eye"))
     ts(ap("bl16"), ind(ap("ex", 0, NS), ap("lt0", 0, 1)), pmoff, A.subtract)
-    own_scores()
+    ts(ap("ll"), ap("cls", 15, NL, 16), pmoff, A.subtract)
     ts(ap("gl", 32, 56), cc("S0", 0, 24), pm, A.add)
+    targets(ind(ap("tab", 0, 32), ll("LR0", 2)), 32)
+    own_scores()
+    gather_targets(32)
+    quant("e", ap("eye"))
     quant("v", ap("vb"))
-    act(ap("tab", 32, 41), cc("N0", 0, 9), F.Identity, scale=1.0 / 1024, bias=ap("pm", 4, 5))
-    act(ap("orep"), ind(ap("tab", 0, 32), ll("LO", 6)), F.Copy)
 
     for t in range(R):
         last = t == R - 1
@@ -472,91 +482,114 @@ def rank_program(g, core, T, topo):
         scan(ap("hs"), ap("h144"), ap("cmp"), A.mult, A.add)
         if not last:
             tt(ap("oh", 0, 80), ind(ap("hs"), ll("LA", 5)), cc("X8"), A.is_equal)
-            choose("l%d" % t, 0, 80, ap("tab", 64, 92) if t == 0 else ap("l0", 0, 160), "LW%d" % t)
+        tt(ap("dd"), ind(ap("hs"), ll("LD", 1)), cc("TH0") if t == 0 else ap("th"), A.is_ge)
+        if not last:
+            weigh(80, ap("tab", 64, 92) if t == 0 else ap("l0", 0, 160), "LW%d" % t)
+        else:
+            scan(ap("acs"), ap("k16"), ap("cmp"), A.mult, A.add)
+        tt(ap("w1"), ind(ap("dd"), ll("LR", 2)), ap("tf"), A.add)
+        if not last:
+            collect("l%d" % t, 0, 80)
+        else:
+            cp(ap("an", 7, 72, 8), ap("acs", 15, NS, 16))
+        ts(ap("sl"), ap("w1"), float(X0), A.mult)
+        if not last:
             ts(ap("ws%d" % (t + 1)), ap("l%d" % t, 7, 80, 8), 0.25, A.mult)
             send(prv, ap("wl%d" % (t + 1)), ap("ws%d" % (t + 1)), "aw%d" % (t + 1))
             act(ap("nv", 96 * t, 96 * t + 96), ind(cc("NV"), ll("LS", 6)), F.Identity, scale=1.0 / 1024, bias=ap("pm", 5 + t, 6 + t))
+        else:
+            for b in (MAGIC, -MAGIC, 1.0 / 1024):
+                act(ap("c0", 0, 27), ap("tab", 32, 59) if b == MAGIC else ap("c0", 0, 27), F.Identity, bias=b)
         if t == 0:
             for h in (1, 2):
                 act(ap("oh", 80 * h, 80 * h + 80), ap("oh", 0, 80), F.Copy)
+            act(ap("tab", 32, 41), cc("N0", 0, 9), F.Identity, scale=1.0 / 1024, bias=ap("pm", 4, 5))
+            act(ap("orep"), ind(ap("tab", 0, 32), ll("LO", 6)), F.Copy)
         if t == 1:
             aff(ap("k16"), ap("ones", 0, NS), [[0, 9], [1, 16]], A.is_gt, 0.0, 0, 0)
             iota(ap("an"), [[0, 80]])
             iota(ap("fr"), [[0, 32]], -1)
-        tt(ap("dd"), ind(ap("hs"), ll("LD", 1)), cc("TH0") if t == 0 else ap("th"), A.is_ge)
-        tt(ap("w1"), ind(ap("dd"), ll("LR", 2)), ap("tg", 0, 32), A.mult)
-        tt(ap("w2"), ap("w1"), ap("dum"), A.max)
-        cp(ap("sl"), ap("w2"))
         tt(ap("bl"), ind(ap("hh", 0, 4 * NS * (t + 1)), ap("gl", 32, 56)), ap("xg"), A.add)
+        if not last:
+            tt(ap("cu", 4 * t, 4 * t + 3), ap("dd", 1, 12, 4), ap("dd", 3, 12, 4), A.add)
+        else:
+            tt(ap("w4", 0, 27), ap("tab", 32, 59), ap("c0", 0, 27), A.subtract)
         op("V", lambda: g.vector.tensor_copy(T.xz[:, :].indirect(T.sl[:, 0:24]), T.bl[:, :]), [ap("sl", 0, 24), ap("bl")], [ap("xz")])
-        quant("z", X)
+        if t == 1:
+            tt(ap("cu", 8, 11), ap("cu", 0, 3), ap("cu", 4, 7), A.add)
+        for h in range(2):
+            quant("z", half(h), H * h, H * h + H)
+            mm(4 * h, "w", 0, "z", H * h, H * h + H)
         for b in range(4):
             act(plane(b), xb(b), F.Copy, scale=32.0)
-            mm(b, "w", 128 * b, "z", 0, C)
-        if t == 0:
-            tt(ap("cu", 0, 3), ap("dd", 1, 12, 4), ap("dd", 3, 12, 4), A.add)
-        elif t == 1:
-            tt(ap("cu", 4, 7), ap("dd", 1, 12, 4), ap("dd", 3, 12, 4), A.add)
-            tt(ap("cu", 8, 11), ap("cu", 0, 3), ap("cu", 4, 7), A.add)
+            if b:
+                mm(b, "w", 128 * b, "z", 0, C)
         if not last:
             tt(ap("o5"), ind(ap("cu", 8 * t, 8 * t + 3), ll("LC", 6)), cc("J5"), A.is_equal)
         else:
-            scan(ap("acs"), ap("k16"), ap("cmp"), A.mult, A.add)
-            cp(ap("an", 7, 72, 8), ap("acs", 15, NS, 16))
+            tt(ap("pr", 0, 96), ind(ap("an"), ll("LS", 6)), ap("o2"), A.is_lt)
+        for h in range(2):
+            pl = ap("xp", H * h, H * h + H)
+            tt(pl, ap("p%d" % (4 * h), 0, H), pl, A.add)
         for b in range(4):
-            tt(plane(b), ap("p%d" % b, 0, C), plane(b), A.add)
+            if b:
+                tt(plane(b), ap("p%d" % b, 0, C), plane(b), A.add)
             if not last:
                 gather_t(b, plane(b), ap("wl%d" % (t + 1), 0, 9), 2.0 ** -5, False)
         if last:
             break
-        ts(xb(3), plane(3), 2.0 ** -5, A.mult)
+        ts(xb(2), plane(2), 2.0 ** -5, A.mult)
+        if t == 1:
+            weigh(80, ap("l0", 160, 320), "LW1")
         send_t(t + 1)
-        for b in range(3):
+        for b in (0, 1, 3):
             act(xb(b), plane(b), F.Copy, scale=2.0 ** -5)
         if t == 0:
-            choose("l0", 80, 240, ap("tab", 0, 92), "L3")
-            own = ap("l0", 160, 240)
-        else:
-            choose("l1", 80, 80, ap("l0", 160, 320), "LW1")
-            own = ap("l1", 80, 160)
+            weigh(240, ap("tab", 0, 92), "L3")
+        collect("l%d" % t, 80, 240 if t == 0 else 80)
+        own = ap("l0", 160, 240) if t == 0 else ap("l1", 80, 160)
         k0 = own[1][0][1]
+        m = 54 + 27 * t
+        k = (m + 15) // 16
+        tt(ap("o2", 0, 16 * k), ind(own, ll("LS", k)), ap("orep", 0, 16 * k), A.is_equal)
         ts(ap("bl16", 0, 9), ap(own[1][0][0], k0 + 7, k0 + 72, 8), 0.25, A.mult)
-        tt(ap("o2"), ind(own, ll("LS", 6)), ap("orep"), A.is_equal)
-        tt(ap("pr", 0, 81), ap("o2", 0, 81), ap("nv", 96 * t, 96 * t + 81), A.mult)
-        scan(ap("sel", 0, 81), cc("K3", 0, 81), ap("pr", 0, 81), A.mult, A.max)
-        tt(ap("tab", 32, 59), ap("tab", 32, 59), ap("sel", 2, 81, 3), A.max)
-        if t == 1:
-            ts(ap("w3", 0, 27), ap("tab", 32, 59), MAGIC, A.add, MAGIC, A.subtract)
-            act(ap("c0", 0, 27), ap("w3", 0, 27), F.Identity, bias=1.0 / 1024)
+        tt(ap("pr", 0, m), ap("o2", 0, m), ap("nv", 96 * t, 96 * t + m), A.mult)
+        scan(ap("sel", 0, m), cc("K3", 0, m), ap("pr", 0, m), A.mult, A.max)
+        tt(ap("tab", 32, 32 + m // 3), ap("tab", 32, 32 + m // 3), ap("sel", 2, m, 3), A.max)
         quant("x", X)
         mm(4, "u1", 0, "x", 0, C)
         act(ap("s1"), ap("p4", 0, C), F.Copy)
         tt(ap("pr", 0, 96), ind(ap("tab", 0, 64), ll("LT", 6)), ap("o5"), A.mult)
         scan(ap("sel", 0, 90), cc("K5", 0, 90), ap("pr", 0, 90), A.mult, A.add)
-        lists_of_targets(ind(ap("sel", 0, 90), ll("LR5", 4)), 64)
+        targets(ind(ap("sel", 0, 90), ll("LR5", 4)), 64)
         tt(ap("eq"), ind(own, ll("LE", 1)), ap("sel", 4, 80, 5), A.is_equal)
+        gather_targets(64)
         scan(ap("th"), cc("H4"), ap("eq"), A.mult, A.add)
-        if t == 1:
-            tt(ap("w4", 0, 27), ap("tab", 32, 59), ap("c0", 0, 27), A.subtract)
         own_scores()
 
-    for h in range(2):
-        for b in range(4):
-            o, a = ap("xz", X0 + 4 * H * h + b, X0 + 4 * H * (h + 1), 4), ap("xp", C * b + H * h, C * b + H * h + H)
-            if b < 2:
-                act(o, a, F.Copy, scale=2.0 ** -5)
-            else:
-                ts(o, a, 2.0 ** -5, A.mult)
+    def unscale(h, b):
+        o, a = ap("xz", X0 + 4 * H * h + b, X0 + 4 * H * (h + 1), 4), ap("xp", C * b + H * h, C * b + H * h + H)
+        if b < 2:
+            act(o, a, F.Copy, scale=2.0 ** -5)
+        else:
+            ts(o, a, 2.0 ** -5, A.mult)
+
+    def finish(h):
         quant("x", half(h), H * h, H * h + H)
         mm(4 + h, "v", 0, "x", H * h, H * h + H)
         store("Y", T.oc[:, 4 * H * h:4 * H * (h + 1)], u8(ap("qx", H * h, H * h + H)))
+
+    for h, b in ((0, 0), (0, 1), (1, 0), (1, 1), (0, 2), (0, 3), (1, 2)):
+        unscale(h, b)
+    finish(0)
+    unscale(1, 3)
+    scan(ap("sel", 0, 81), cc("K3", 0, 81), ap("pr", 0, 81), A.mult, A.max)
+    finish(1)
     for h in range(2):
         act(ap("yo", H * h, H * h + H), ap("p%d" % (4 + h), 0, H), F.Copy)
         store("S", T.y[:, H * h:H * h + H], ap("yo", H * h, H * h + H))
     for k in range(4):
-        store("Y", T.osc[4 * k:4 * k + 4, :], ap("sx"), T.sx[32 * k:32 * k + 4, :])
-    tt(ap("pr", 0, 96), ind(ap("an"), ll("LS", 6)), ap("o2"), A.is_lt)
-    scan(ap("sel", 0, 81), cc("K3", 0, 81), ap("pr", 0, 81), A.mult, A.max)
+        store("YYYS"[k], T.osc[4 * k:4 * k + 4, :], ap("sx"), T.sx[32 * k:32 * k + 4, :])
     tt(ap("fr", 0, 27), ap("w4", 0, 27), ap("sel", 2, 81, 3), A.subtract)
     ts(ap("sko"), ind(ap("fr"), ll("LK", 2)), 1024.0, A.mult, -1.0, A.max)
     for c in range(3):

@@ -7,11 +7,13 @@ X0 = 2048
 TILES = [["d", 29, 28, 27]] + [[c for c in range(h, h - 4, -1) if c > 0] for h in range(26, 0, -4)]
 WIDTH = [480] + [max(128, 16 * t[0]) for t in TILES[1:]]
 START = [sum(WIDTH[:i]) for i in range(len(WIDTH))]
-ON_SCALAR = (29, 28, 27)
-LISTS = [("LA", 96), ("LW0", 96), ("L3", 256), ("LW1", 96), ("LD", 32), ("LR", 32), ("LR0", 32), ("LR5", 32), ("LH", 32),
-         ("LE", 32), ("LC", 96), ("LT", 96), ("LS", 96), ("LO", 96), ("LK", 32)]
-CONSTS = [("c16", 32), ("X8", 80), ("J5", 96), ("NV", 80), ("N0", 16), ("T4", 32), ("HB", 32), ("S0", 32),
-          ("TH0", 16), ("IDX", 24), ("NA", 24), ("FX", 24), ("K8", 240), ("K5", 96), ("K3", 96), ("H4", 16)]
+SPLIT = 23
+PIECES = [(0, 128), (128, 256), (256, C)]
+KW = 240
+LISTS = [("LA", 96), ("LW0", 96), ("L3", 96), ("LW1", 96), ("LD", 32), ("LR", 32), ("LR0", 32), ("LR5", 32), ("LH", 32),
+         ("LE", 32), ("LF", 32), ("LC", 64), ("LT", 64), ("LS", 96), ("LO", 96), ("LK", 32)]
+CONSTS = [("c16", 32), ("X8", 80), ("J5", 72), ("NV", 80), ("N0", 16), ("T4", 32), ("HB", 40), ("S0", 32), ("TH0", 16),
+          ("IDX", 24), ("NA", 24), ("FX", 24), ("K8", 80), ("K5", 64), ("K3", 96), ("N3", 96), ("H4", 16)]
 LAT = {k: (sum(v for _, v in LISTS[:i]), w) for i, (k, w) in enumerate(LISTS)}
 CAT = {k: (sum(v for _, v in CONSTS[:i]), w) for i, (k, w) in enumerate(CONSTS)}
 NL, NC = sum(w for _, w in LISTS), sum(w for _, w in CONSTS)
@@ -29,14 +31,14 @@ def _mx(name, n):
 
 
 for _k, _w in [("xz", 4 * C + X0), ("xp", 4 * C), ("xs1", 4 * C), ("xs2", 4 * C), ("xs3", 4 * C), ("ub", 512), ("vb", 512),
-               ("ones", 512), ("zb", 512), ("band0", 512), ("band", 512), ("tri", 512), ("eye", 2048), ("iq", C), ("dg", C), ("keep", C),
-               ("ext", C), ("mt", 4 * sum(WIDTH)), ("junk", 7000), ("sg", 4 * C), ("rowd", C), ("tt", 4 * NS), ("hh", 4 * NS * R),
+               ("ones", 516), ("zb", NL // 3), ("cl", NL), ("band", 512), ("tri", 512), ("eye", 516), ("iq", KW), ("dg", KW), ("keep", KW),
+               ("ext", KW), ("mt", 4 * sum(WIDTH)), ("sums", 256 * (30 - SPLIT)), ("sg", 8 * SPLIT * SPLIT), ("rowd", C), ("tt", 4 * NS), ("hh", 4 * NS * R),
                ("xg", 384), ("bl", 384), ("cmp", NS), ("hs", NS), ("acs", NS), ("k16", NS), ("h144", NS)]:
     _sb(_k, _w, "bfloat16")
-for _k, _w in [("pm", 8), ("cc", NC), ("cl", NL), ("cls", NL), ("mm", C), ("yy", C), ("jj", C), ("ob", C), ("ex", C), ("rs", 32), ("w1", 32),
-               ("w2", 32), ("w3", 32), ("w4", 32), ("c0", 32), ("tab", 96), ("orep", 96), ("s1", C), ("bp", NS), ("cm", NS), ("oh", 240),
-               ("pr", 240), ("l0", 320), ("l1", 160), ("dd", 16), ("th", 16), ("cu", 16), ("tg", 64), ("nv", 192), ("tf", 32), ("o2", 96),
-               ("o5", 96), ("sel", 96), ("eq", 16), ("fr", 32), ("an", 80), ("yo", C), ("sko", 32)]:
+for _k, _w in [("pm", 8), ("cc", NC), ("cls", NL), ("mm", C), ("yy", C), ("jj", C), ("ob", C), ("ex", C), ("rs", 32), ("w1", 32),
+               ("w2", 32), ("w3", 32), ("w4", 32), ("c0", 32), ("tab", 96), ("orep", 96), ("s1", C), ("bp", NS), ("cm", NS), ("oh", 80),
+               ("pr", 96), ("pr2", 96), ("l0", 160), ("l1", 80), ("dd", 16), ("th", 16), ("cu", 16), ("tg", 64), ("nv", 192), ("tf", 32), ("o2", 96),
+               ("pk", 64), ("ow", 80), ("owr", 16), ("o5", 64), ("sel", 96), ("eq", 16), ("fr", 32), ("an", 80), ("yo", C), ("sko", 32)]:
     _sb(_k, _w, "float32")
 for _k, _w in [("pi", 8), ("ui", 16)]:
     _sb(_k, _w, "int32")
@@ -50,7 +52,7 @@ for _t in range(R):
     _mx("a%d" % _t, NS)
 for _t in range(8):
     SCRATCH["p%d" % _t] = ("psum", [128, 512], "float32")
-DMAS = ["dx", "dx2", "du", "dv", "dw", "dws", "d1", "d2", "d3", "dz", "dz2", "dz3", "dout"]
+DMAS = ["dx0", "dx1", "dx2", "du", "dv", "dw", "dws", "d1", "d2", "d3", "dz", "dz2", "dout"]
 SEMAPHORES = ["eV", "eS", "eP", "eG", "snt", "ar0", "ar1", "ar2", "aow", "aw1", "aw2"] + DMAS
 
 
@@ -142,8 +144,8 @@ def rank_program(g, core, T, topo):
     def cp(o, a):
         op("V", lambda: g.vector.tensor_copy(o[0], a[0]), [a], [o])
 
-    def scan(o, a, b, f0, f1):
-        op("V", lambda: g.vector.tensor_tensor_scan(o[0], a[0], b[0], 0.0, f0, f1), [a, b], [o])
+    def scan(o, a, b, f0, f1, first=0.0):
+        op("V", lambda: g.vector.tensor_tensor_scan(o[0], a[0], b[0], first, f0, f1), [a, b], [o])
 
     def fill(o, c):
         op("V", lambda: g.vector.memset(o[0], c), [], [o])
@@ -212,9 +214,9 @@ def rank_program(g, core, T, topo):
         return ap("mt", 4 * (START[k] + lo), 4 * (START[k] + WIDTH[k]))
 
     def zero(o):
-        act(o, ap("zb", 0, o[1][0][2] - o[1][0][1]), F.Copy)
+        act(o, ap("ones", 0, o[1][0][2] - o[1][0][1]), F.Copy, scale=0.0)
 
-    pm, pmoff, pc, pm10 = ap("pm", 0, 1), ap("pm", 1, 2), ap("pm", 2, 3), ap("pm", 3, 4)
+    pm, pmoff, pc, pm30 = ap("pm", 0, 1), ap("pm", 1, 2), ap("pm", 2, 3), ap("pm", 3, 4)
     X = ap("xz", X0, X0 + 4 * C)
     H = C // 2
 
@@ -229,25 +231,22 @@ def rank_program(g, core, T, topo):
 
     for t in range(R):
         arrives(prv, "ar%d" % t, [ap("qa%d" % t), ap("sa%d" % t)])
-    arrives(prv, "aow", [ap("tab", 64, 92)])
+    arrives(prv, "aow", [ap("tab", 64, 73), ap("tab", 73, 92)])
     arrives(nxt, "aw1", [ap("wl1")])
     arrives(nxt, "aw2", [ap("wl2")])
 
-    load("Y", "dx", half(0), T.x[:, 0:2 * C])
-    load("Y", "dx2", half(1), T.x[:, 2 * C:4 * C])
     load("S", "du", ap("ub"), T.u[:, :])
+    for i, (lo, hi) in enumerate(PIECES):
+        load("Y", "dx%d" % i, ap("xz", X0 + 4 * lo, X0 + 4 * hi), T.x[:, 4 * lo:4 * hi])
     fill(ap("ones"), 1.0)
-    fill(ap("zb"), 0.0)
-    wait("Y", "dx2", 16)
-    zero(ap("yo"))
-    zf = [ap("cl", lo, min(NL, lo + C)) for lo in range(0, NL, C)]
-    zg = [gap(k) for k in (2, 3, 6, 7)]
-    zh = [ap("eye", 512 * b, 512 * b + 512) for b in range(4)]
-    for sem, src, zeros in (("dz2", "yo", zf), ("dz3", "zb", zg), ("dz", "zb", zh)):
+    zero(ap("zb"))
+    zg = [gap(k) for k in range(3)]
+    zf = [ap("cl", lo, lo + NL // 3) for lo in range(0, NL, NL // 3)]
+    for sem, zeros in (("dz", zg), ("dz2", zf)):
         for o in zeros:
-            z = ap(src, 0, o[1][0][2] - o[1][0][1])
+            z = ap("zb", 0, o[1][0][2] - o[1][0][1])
             op("Y", lambda: g.sync.dma_start(o[0], z[0]), [z], [o], sem=sem, inc=16)
-        mark(sem, count[sem], [ap(src)[1][0]], [r for o in zeros for r in o[1]])
+        mark(sem, count[sem], [ap("zb")[1][0]], [r for o in zeros for r in o[1]])
     for t in range(1, 4):
         load("Y", "d%d" % t, ap("xs%d" % t, 0, 4 * C - t), T.x[:, t:4 * C])
     load("Y", "dw", u8(ap("qw")), T.wc[:, :])
@@ -255,36 +254,32 @@ def rank_program(g, core, T, topo):
     load("Y", "dv", ap("vb"), T.v[:, :])
 
     iota(ap("pi", 0, 1), [[0, 1]], 0, 1)
-    iota(ap("iq"), [[0, 30], [1, 16]])
     iota(ap("ui"), [[1, 2], [16, 8]])
+    iota(ap("iq"), [[0, KW // 16], [1, 16]])
+    aff(ap("acs", 0, 128), ap("ones", 0, 128), [[-16, 8], [0, 16]], A.is_ge, 0.0, 0, 1)
+    aff(ap("band", 0, 512, 4), ap("acs", 0, 128), [[16, 8], [0, 16]], A.is_ge, 0.0, 15, -1)
+    aff(ap("tri", 0, 512, 4), ap("band", 0, 512, 4), [[1, 128]], A.is_gt, 0.0, 0, -1)
     iota(ap("w2", 0, 16), [[0, 16]])
     iota(ap("w2", 0, 9), [[16, 3], [48, 3]], 15)
-    iota(ap("w3", 0, 30), [[1, 10], [160, 3]])
-    for k in (4, 5, 0):
-        zero(gap(k))
+    iota(ap("w3", 0, 30), [[1, 10], [10, 3]])
+    for k in (7, 6, 5):
+        fill(gap(k), 0.0)
     ts(ap("pi", 1, 2), ap("pi", 0, 1), 15, A.bitwise_and)
-    fill(gap(1), 0.0)
-    cp(pm, ap("pi", 1, 2))
-    act(pmoff, pm, F.Identity, scale=-OFF, bias=15 * OFF)
-    act(pc, pm, F.Identity, scale=OFF - 1, bias=16 - 15 * OFF)
-    act(pm10, pm, F.Copy, scale=10.0)
-    ts(ap("keep"), ap("iq"), pm, A.is_gt)
-    ts(ap("dg"), ap("iq"), pm, A.is_equal)
     cp(ap("ul"), ap("ui"))
-    act(ap("ext"), ap("keep"), F.Identity, scale=2.0 ** 20 + OFF, bias=-2.0 ** 20)
-    aff(ap("band0"), ap("ones"), [[-16, 8], [0, 64]], A.is_ge, 0.0, 0, 1)
-    aff(ap("band"), ap("band0"), [[16, 8], [0, 64]], A.is_ge, 0.0, 15, -1)
-    aff(ap("tri"), ap("band"), [[1, 128], [200, 4]], A.is_gt, 0.0, 0, -1)
+    cp(pm, ap("pi", 1, 2))
+    zero(gap(4))
+    zero(ap("rs", 0, 1))
     quant("u", ap("ub"))
-    ts(ap("lp", 0, 30), ap("w3", 0, 30), pm10, A.add)
+    ts(ap("dg"), ap("iq"), pm, A.is_equal)
     cp(u32(ap("qu0")), ind(u32(ap("qu")), ap("ul", 0, 8)))
     act(ap("su0"), ind(ap("su"), ap("ul", 0, 8)), F.Copy)
-    zero(ap("rs", 0, 1))
-    zero(ap("tab", 0, 64))
-    for lo in range(0, NC, 512):
-        zero(ap("cc", lo, min(NC, lo + 512)))
+    zero(gap(3))
+    act(pmoff, pm, F.Identity, scale=-OFF, bias=15 * OFF)
+    act(pc, pm, F.Identity, scale=OFF - 1, bias=16 - 15 * OFF)
+    act(pm30, pm, F.Copy, scale=30.0)
     iota(ap("jj"), [[1, C]])
-    iota(cc("c16"), [[16, 32]])
+    iota(cc("c16", 0, SPLIT), [[16, SPLIT]])
+    iota(cc("c16", SPLIT, 30), [[16, 30 - SPLIT]], 16 * SPLIT - KW)
 
     for lo, hi, pat, base in [(0, 4, [[0, 4]], 0), (4, 6, [[0, 2]], 1), (6, 8, [[1, 2]], 2), (8, 10, [[0, 2]], 1),
                               (10, 14, [[0, 2], [1, 2]], 2), (14, 16, [[1, 2]], 3), (16, 24, [[1, 2], [1, 2], [1, 2]], 2)]:
@@ -295,111 +290,126 @@ def rank_program(g, core, T, topo):
         iota(cc("FX", lo, hi), pat, base)
     for i in range(3):
         iota(cc("NA", 8 * i, 8 * i + 8), [[3, 2], [3, 2], [3, 2]], 9 + 3 * i)
+    aff(ap("eye"), ap("ones"), [[1, 516]], A.is_equal, 0.0, -3, -4)
+    iota(cc("T4", 0, 36), [[1, 6], [0, 6]])
+    iota(cc("S0", 0, 24), [[NS, 4], [16, 2], [48, 3]])
     iota(cl("LA", 0, 72), [[48, 3], [0, 24]], 47)
     iota(cl("LD", 0, 12), [[48, 3], [16, 2], [0, 2]], 15)
     iota(cl("LR", 0, 24), [[0, 4], [2, 2], [4, 3]], 1)
     iota(cl("LR0", 0, 24), [[0, 4], [1, 6]])
-    iota(cl("LR5", 0, 24), [[0, 4], [10, 2], [20, 3]], 4)
-    iota(cl("LH", 0, 24), [[0, 4], [5, 2], [10, 3]], 64)
+    iota(cl("LR5", 0, 24), [[0, 4], [5, 2], [10, 3]], 4)
+    iota(cl("LH", 0, 24), [[0, 4], [5, 2], [10, 3]], 34)
     iota(cl("LE", 0, 12), [[24, 3], [0, 2], [8, 2]], 7)
-    iota(cl("LC", 0, 60), [[1, 3], [0, 20]])
-    iota(cl("LC", 60, 90), [[1, 3], [0, 10]])
-    for c in range(3):
-        iota(cl("LT", 20 * c, 20 * c + 20), [[3, 2], [0, 2], [3, 5]], c)
-    iota(cl("LT", 60, 90), [[1, 3], [3, 2], [3, 5]], 32)
+    iota(cl("LF", 0, 12), [[10, 3], [5, 2], [0, 2]], 4)
+    iota(cl("LC", 0, 60), [[0, 2], [1, 3], [0, 10]])
+    for h in range(2):
+        iota(cl("LT", 30 * h, 30 * h + 30), [[1, 3], [3, 2], [3, 5]], 32 * h)
     iota(cl("LS", 0, 81), [[0, 9], [8, 9]], 7)
     iota(cl("LO", 0, 81), [[1, 27], [0, 3]])
     iota(cl("LK", 0, 30), [[1, 3], [3, 10]])
-    for b in range(4):
-        aff(ap("eye", 513 * b, 512 * b + 512, 4), ap("ones", 0, 128), [[1, 128]], A.is_equal, 0.0, 0, -1)
-    iota(cc("X8"), [[0, 10], [1, 8]])
-    aff(cc("K8"), ap("ones", 0, 240), [[0, 30], [1, 8]], A.is_gt, 0.0, 0, 0)
     aff(ap("acs"), ap("ones", 0, NS), [[0, 9], [1, 16]], A.is_gt, 2.0, 0, 0)
     aff(ap("h144"), ap("acs"), [[0, 3], [1, 48]], A.is_gt, 0.0, 0, 0)
-    iota(cc("T4", 0, 24), [[1, 4], [0, 6]])
-    iota(cc("S0", 0, 24), [[NS, 4], [16, 2], [48, 3]])
+    iota(cc("X8"), [[0, 10], [1, 8]])
     iota(cc("TH0"), [[0, 4], [2, 2], [0, 2]], 1)
+    aff(cc("K8"), ap("ones", 0, 80), [[0, 10], [1, 8]], A.is_gt, 0.0, 0, 0)
 
-    used = [0]
+    def scores(i):
+        lo, hi = PIECES[i]
+        quant("x", ap("xz", X0 + 4 * lo, X0 + 4 * hi), lo, hi)
+        mm((4, 5, 7)[i], "u0", 0, "x", lo, hi)
+        mm((6, 3, 1)[i], "u0", 0, "x", 0, min(hi, 16 * SPLIT))
 
-    def scores(h):
-        quant("x", half(h), H * h, H * h + H)
-        mm(4 + h, "u0", 0, "x", H * h, H * h + H)
+    def own_column(i):
+        lo, hi = PIECES[i]
+        tt(ap("mm", lo, hi), ap("p%d" % (4, 5, 7)[i], 0, hi - lo), ap("dg", 0, hi - lo), A.mult)
 
-    def own_column(h):
-        tt(ap("mm", H * h, H * h + H), ap("p%d" % (4 + h), 0, H), ap("dg", 0, H), A.mult)
+    def spread(i):
+        lo, hi = PIECES[i]
+        scan(ap("yy", lo, hi), ap("keep", 0, hi - lo), ap("mm", lo, hi), A.mult, A.add)
 
-    def spread(h):
-        scan(ap("yy", H * h, H * h + H), ap("keep", 0, H), ap("mm", H * h, H * h + H), A.mult, A.add)
+    def periodic(o, k, a, lo, hi, f0, f1, shift=0):
+        for i in range(lo, hi, KW):
+            j = min(hi, i + KW)
+            scan(ap(o, i, j), ap(k, 0, j - i), a(i + shift, j + shift), f0, f1)
 
     def pack(k):
         quant("m", ap("mt", 4 * START[k], 4 * (START[k] + WIDTH[k])), START[k], START[k] + WIDTH[k])
 
     def count_tile(k):
-        mm(2, "r" if k == 0 else "b", 0, "m", START[k], START[k] + WIDTH[k], k == 0, k == len(TILES) - 1)
+        mm(2, "r" if k == 0 else "b", 0, "m", START[k], START[k] + WIDTH[k], k == 0, k == 7)
 
-    def compare(k, bank, slots=range(4)):
-        for t, c in enumerate(TILES[k]):
-            if t in slots and c != "d" and c not in ON_SCALAR:
-                w = 16 * c
-                ts(slot(k, t, 0, w), ap(bank, 0, w), ap("yy", w + 15, w + 16), A.is_lt)
-                act(ap("junk", used[0], used[0] + w), slot(k, t, 0, w), F.Identity, acc=ap("rs", c, c + 1))
-                used[0] += w
+    def block(c, lo, hi):
+        k = [c in tl for tl in TILES].index(True)
+        return slot(k, TILES[k].index(c), lo, hi)
 
-    def on_scalar(k):
-        for t, c in enumerate(TILES[k]):
-            if c in ON_SCALAR:
-                i = ON_SCALAR.index(c)
-                act(ap("sg", C * i, C * i + 16 * c), ap("p1", 0, 16 * c), F.Sign, scale=-1.0, bias=ap("yy", 16 * c + 15, 16 * c + 16))
-        for t, c in enumerate(TILES[k]):
-            if c in ON_SCALAR:
-                i = ON_SCALAR.index(c)
-                act(slot(k, t, 0, 16 * c), ap("sg", C * i, C * i + 16 * c), F.Relu, acc=ap("rs", c, c + 1))
+    def compare(c):
+        ts(block(c, 0, 16 * c), ap("p0", 0, 16 * c), ap("yy", 16 * c + 15, 16 * c + 16), A.is_lt)
+
+    def row_sum(c):
+        end = 256 * (c - SPLIT + 1)
+        scan(ap("sums", end - 8 * c, end), block(c, 0, 8 * c), block(c, 8 * c, 16 * c), A.add, A.add, -float(KW))
+
+    def on_scalar(blocks):
+        def sg(c):
+            return ap("sg", 8 * c * (c - 1), 8 * c * (c + 1))
+        for a, b in zip([None] + blocks, blocks + [None]):
+            if b:
+                bank = (6, 3, 1)[[16 * b < hi for _, hi in PIECES].index(True)]
+                act(sg(b), ap("p%d" % bank, 0, 16 * b), F.Sign, scale=-1.0, bias=ap("yy", 16 * b + 15, 16 * b + 16))
+            if a:
+                act(block(a, 0, 16 * a), sg(a), F.Relu, acc=ap("rs", a, a + 1))
 
     scores(0)
-    scan(ap("w1", 0, 16), ap("ext", 0, 16), ap("w2", 0, 16), A.add, A.max)
+    ts(ap("keep"), ap("iq"), pm, A.is_gt)
     own_column(0)
-    ts(ap("lt0", 0, 1), ap("w1", 15, 16), pmoff, A.subtract)
-    spread(0)
-    compare(4, "p4")
     scores(1)
-    mm(1, "u0", 0, "x", 0, C)
-    mm(0, "u0", 0, "x", 0, C)
-    compare(5, "p4", (0, 1, 2))
+    spread(0)
     own_column(1)
-    compare(5, "p4", (3,))
+    ts(ap("ext"), ap("keep"), 2.0 ** 20 + OFF, A.mult, 2.0 ** 20, A.subtract)
     spread(1)
-    on_scalar(0)
-    act(ap("c0", 0, 30), cc("c16", 0, 30), F.Identity, bias=pc)
-    pack(4)
-    tt(slot(0, 0, 0, C), ap("p0", 0, C), ap("yy"), A.is_le)
-    pack(5)
-    scan(ap("rowd"), ap("keep"), slot(0, 0, 0, C), A.mult, A.add)
-    compare(1, "p0")
-    quant("r", ap("tri"))
+    for b in range(1, 4):
+        for k in ("band", "tri"):
+            cp(ap(k, b, 512, 4), ap("band", 0, 512, 4))
+    scores(2)
+    mm(0, "u0", 0, "x", 0, C)
     quant("b", ap("band"))
-    pack(0)
-    for k in (0, 4, 5):
-        count_tile(k)
-    tt(ap("w1", 0, 30), ap("c0", 0, 30), ap("rowd", 15, C, 16), A.subtract)
-    for k, j in ((2, 1), (3, 2), (6, 3), (7, 6)):
-        compare(k, "p0")
-        pack(j)
-        count_tile(j)
-    pack(7)
-    count_tile(7)
+    own_column(2)
+    ts(ap("lp", 0, 30), ap("w3", 0, 30), pm30, A.add)
+    spread(2)
+    on_scalar(list(range(3, SPLIT)) + [1, 2])
+    quant("r", ap("tri"))
+    tt(slot(0, 0, 0, C), ap("p0", 0, C), ap("yy"), A.is_le)
+    scan(ap("w1", 0, 16), ap("ext", 0, 16), ap("w2", 0, 16), A.add, A.max)
+    after = {28: (6,), 26: (0, 5), 24: (4,), SPLIT: (1, 3, 2, 7)}
+    for c in range(29, SPLIT - 1, -1):
+        compare(c)
+        if c < 29:
+            row_sum(c + 1)
+        else:
+            ts(ap("lt0", 0, 1), ap("w1", 15, 16), pmoff, A.subtract)
+            periodic("rowd", "keep", lambda i, j: slot(0, 0, i, j), 0, C, A.mult, A.add)
+        for k in after.get(c, ()):
+            if k == 1:
+                ts(ap("c0", 0, 30), cc("c16", 0, 30), pc, A.add)
+            if k == 3:
+                row_sum(SPLIT)
+                tt(ap("w1", 0, 30), ap("c0", 0, 30), ap("rowd", 15, C, 16), A.subtract)
+            if k == 2:
+                tt(ap("w2", SPLIT, 30), ap("w1", SPLIT, 30), ap("sums", 255, None, 256), A.subtract)
+            pack(k)
+            for j in {0: (0, 6), 6: ()}.get(k, (k,)):
+                count_tile(j)
     for c in range(3):
-        for o in (cl("LW0", 24 * c, 24 * c + 24), cl("L3", 80 + 24 * c, 104 + 24 * c)):
-            act(o, cc("IDX"), F.Identity, scale=3.0, bias=float(c))
-        act(cl("L3", 24 * c, 24 * c + 24), cc("NA"), F.Identity, bias=64.0 + c)
-        act(cl("L3", 160 + 24 * c, 184 + 24 * c), cc("NA"), F.Identity, bias=float(c))
+        act(cl("LW0", 24 * c, 24 * c + 24), cc("IDX"), F.Identity, scale=3.0, bias=float(c))
+        act(cl("L3", 24 * c, 24 * c + 24), cc("NA"), F.Identity, bias=float(c))
         act(cl("LW1", 24 * c, 24 * c + 24), cc("FX"), F.Identity, bias=24.0 * c)
+    zero(ap("tab", 0, 64))
     act(ap("su1"), ind(ap("su"), ap("ul", 8, 16)), F.Copy)
     act(ap("cm"), ap("dg", 0, NS), F.Identity, scale=-2 * BIG, bias=BIG)
     for t in range(R):
-        act(ap("pm", 4 + t, 5 + t), pm, F.Identity, scale=1027.0 / 1024, bias=t * (4 * NS + NS / 1024))
-    tt(ap("w2", 0, 30), ap("w1", 0, 30), ap("rs", 0, 30), A.subtract)
-    scan(ap("ex"), ap("ext"), ap("p2", 0, C), A.add, A.max)
+        act(ap("pm", 4 + t, 5 + t), pm, F.Identity, scale=1033.0 / 1024, bias=t * (4 * NS + NS / 1024))
+    tt(ap("w2", 0, SPLIT), ap("w1", 0, SPLIT), ap("rs", 0, SPLIT), A.subtract)
+    periodic("ex", "ext", lambda i, j: ap("p2", i, j), 0, C, A.add, A.max)
     tt(ap("w1", 0, 30), ap("w2", 0, 30), ap("ex", 15, C, 16), A.add)
     cp(ap("pos"), ap("w1", 0, 30))
     op("V", lambda: g.vector.tensor_copy(T.ob[:, :].indirect(T.pos[:, :]), T.jj[:, :]), [ap("pos"), ap("jj")], [ap("ob")])
@@ -420,22 +430,46 @@ def rank_program(g, core, T, topo):
         send(nxt, u8(ap("qa%d" % t)), u8(ap("qt%d" % t)), "ar%d" % t)
         send(nxt, ap("sa%d" % t), ap("st%d" % t), "ar%d" % t)
 
-    for b in range(3):
-        gather_t(b, X if b == 0 else ap("xs%d" % b, 0, 4 * C - 3), ap("tl0", 0, 9), 1.0, False)
-    scan(ap("ex", NS, 448), ap("ext", NS, 448), ap("yy", 16, 320), A.add, A.max)
-    ts(ap("tab", 0, 28), ap("ex", 15, 448, 16), pmoff, A.subtract, 4.0, A.mult)
-    send(nxt, ap("tab", 64, 92), ap("tab", 0, 28), "aow")
-    gather_t(3, ap("xs3", 0, 4 * C - 3), ap("tl0", 0, 9), 1.0, True)
+    ts(ap("tab", 0, 9), ap("ex", 15, NS, 16), pmoff, A.subtract, 4.0, A.mult)
+    send(nxt, ap("tab", 64, 73), ap("tab", 0, 9), "aow")
+    for b in range(4):
+        gather_t(b, X if b == 0 else ap("xs%d" % b, 0, 4 * C - 3), ap("tl0", 0, 9), 1.0, b > 1)
     send_t(0)
+    periodic("ex", "ext", lambda i, j: ap("yy", i, j), NS, 448, A.add, A.max, 16 - NS)
+    ts(ap("tab", 9, 28), ap("ex", NS + 15, 448, 16), pmoff, A.subtract, 4.0, A.mult)
+    send(nxt, ap("tab", 73, 92), ap("tab", 9, 28), "aow")
 
+    iota(cc("NV"), [[0, 80]])
     for c in range(3):
-        iota(cc("N0", c, 9, 3), [[16385, 3]], 49200 * c + 1)
-        iota(cc("NV", 24 * c + 7, 24 * c + 24, 8), [[16385, 3]], 49200 * c + 1)
-    iota(cc("HB", 0, 24), [[NS, 4], [0, 6]])
-    iota(cc("J5", 0, 90), [[0, 18], [1, 5]])
-    aff(cc("K5", 0, 90), ap("ones", 0, 90), [[0, 18], [1, 5]], A.is_gt, 0.0, 0, 0)
-    aff(cc("K3"), ap("ones", 0, 96), [[0, 32], [1, 3]], A.is_gt, 0.0, 0, 0)
-    iota(cc("H4"), [[0, 4], [1, 2], [1, 2]])
+        iota(cc("N0", c, 9, 3), [[16385, 3]], 49155 * c + 1)
+        iota(cc("NV", 24 * c + 7, 24 * c + 24, 8), [[16385, 3]], 49155 * c + 1)
+
+    def late_constants():
+        iota(ap("ow"), [[0, 80]])
+        iota(cc("J5", 0, 65), [[0, 13], [1, 5]])
+        iota(cc("HB", 0, 36), [[NS, 6], [0, 6]])
+        aff(cc("K3"), ap("ones", 0, 96), [[0, 32], [1, 3]], A.is_gt, 0.0, 0, 0)
+        aff(cc("K5", 0, 60), ap("ones", 0, 60), [[0, 12], [1, 5]], A.is_gt, 0.0, 0, 0)
+        iota(cc("H4"), [[0, 4], [1, 2], [1, 2]])
+        aff(cc("N3"), ap("ones", 0, 96), [[0, 32], [1, 3]], A.is_equal, 0.0, 0, 0)
+        aff(ap("k16"), ap("ones", 0, NS), [[0, 9], [1, 16]], A.is_gt, 0.0, 0, 0)
+        iota(ap("an"), [[0, 80]])
+        iota(ap("fr"), [[0, 32]])
+
+    def element(h, b):
+        return ap("xz", X0 + 4 * H * h + b, X0 + 4 * H * (h + 1), 4)
+
+    def piece(h, b):
+        return ap("xp", C * b + H * h, C * b + H * h + H)
+
+    def add_product(bank, h, b):
+        tt(piece(h, b), ap("p%d" % bank, 0, H), piece(h, b), A.add)
+
+    def unscale(h, b, on_v):
+        if on_v:
+            ts(element(h, b), piece(h, b), 2.0 ** -5, A.mult)
+        else:
+            act(element(h, b), piece(h, b), F.Copy, scale=2.0 ** -5)
 
     def targets(src, w):
         a = CAT["T4"][0]
@@ -458,8 +492,9 @@ def rank_program(g, core, T, topo):
     cp(u32(ap("qu1")), ind(u32(ap("qu")), ap("ul", 8, 16)))
     mm(3, "u1", 0, "x", 0, C)
     act(ap("s1"), ap("p3", 0, C), F.Copy)
-    for lo in range(0, NL, C):
-        hi = min(NL, lo + C)
+    act(ap("pk", 0, 32), ap("tab", 0, 32), F.Copy, scale=1.0 / 512)
+    for lo in range(0, NL, KW):
+        hi = min(NL, lo + KW)
         scan(ap("cls", lo, hi), ap("ext", 0, hi - lo), ap("cl", lo, hi), A.add, A.max)
     ts(ap("bl16"), ind(ap("ex", 0, NS), ap("lt0", 0, 1)), pmoff, A.subtract)
     ts(ap("ll"), ap("cls", 15, NL, 16), pmoff, A.subtract)
@@ -467,7 +502,8 @@ def rank_program(g, core, T, topo):
     targets(ind(ap("tab", 0, 32), ll("LR0", 2)), 32)
     own_scores()
     gather_targets(32)
-    quant("e", ap("eye"))
+    for b in range(4):
+        quant("e", ap("eye", 3 - b, 515 - b), 128 * b, 128 * b + 128)
     quant("v", ap("vb"))
 
     for t in range(R):
@@ -480,11 +516,13 @@ def rank_program(g, core, T, topo):
             act(ap("hh", 4 * NS * t + NS * b, 4 * NS * t + NS * b + NS), ap("p%d" % (4 + b), 0, NS), F.Copy, scale=0.5)
         tt(ap("cmp"), ap("p0", 0, NS), ap("bp"), A.is_ge)
         scan(ap("hs"), ap("h144"), ap("cmp"), A.mult, A.add)
+        if t == 0:
+            tt(ap("pk", 32, 60), ap("tab", 64, 92), ap("pk", 0, 28), A.add)
         if not last:
             tt(ap("oh", 0, 80), ind(ap("hs"), ll("LA", 5)), cc("X8"), A.is_equal)
         tt(ap("dd"), ind(ap("hs"), ll("LD", 1)), cc("TH0") if t == 0 else ap("th"), A.is_ge)
         if not last:
-            weigh(80, ap("tab", 64, 92) if t == 0 else ap("l0", 0, 160), "LW%d" % t)
+            weigh(80, ap("pk", 32, 60) if t == 0 else ap("l0", 0, 160), "LW%d" % t)
         else:
             scan(ap("acs"), ap("k16"), ap("cmp"), A.mult, A.add)
         tt(ap("w1"), ind(ap("dd"), ll("LR", 2)), ap("tf"), A.add)
@@ -494,29 +532,19 @@ def rank_program(g, core, T, topo):
             cp(ap("an", 7, 72, 8), ap("acs", 15, NS, 16))
         ts(ap("sl"), ap("w1"), float(X0), A.mult)
         if not last:
-            ts(ap("ws%d" % (t + 1)), ap("l%d" % t, 7, 80, 8), 0.25, A.mult)
+            ts(ap("ws%d" % (t + 1)), ap("l%d" % t, 7, 80, 8), 0.25, A.mult, 0.47, A.subtract)
             send(prv, ap("wl%d" % (t + 1)), ap("ws%d" % (t + 1)), "aw%d" % (t + 1))
+            if t == 0:
+                late_constants()
+                act(ap("tab", 32, 41), cc("N0", 0, 9), F.Identity, scale=1.0 / 1024, bias=ap("pm", 4, 5))
+                act(ap("orep"), ind(ap("pk", 0, 32), ll("LO", 6)), F.Copy)
             act(ap("nv", 96 * t, 96 * t + 96), ind(cc("NV"), ll("LS", 6)), F.Identity, scale=1.0 / 1024, bias=ap("pm", 5 + t, 6 + t))
-        else:
-            for b in (MAGIC, -MAGIC, 1.0 / 1024):
-                act(ap("c0", 0, 27), ap("tab", 32, 59) if b == MAGIC else ap("c0", 0, 27), F.Identity, bias=b)
-        if t == 0:
-            for h in (1, 2):
-                act(ap("oh", 80 * h, 80 * h + 80), ap("oh", 0, 80), F.Copy)
-            act(ap("tab", 32, 41), cc("N0", 0, 9), F.Identity, scale=1.0 / 1024, bias=ap("pm", 4, 5))
-            act(ap("orep"), ind(ap("tab", 0, 32), ll("LO", 6)), F.Copy)
-        if t == 1:
-            aff(ap("k16"), ap("ones", 0, NS), [[0, 9], [1, 16]], A.is_gt, 0.0, 0, 0)
-            iota(ap("an"), [[0, 80]])
-            iota(ap("fr"), [[0, 32]], -1)
         tt(ap("bl"), ind(ap("hh", 0, 4 * NS * (t + 1)), ap("gl", 32, 56)), ap("xg"), A.add)
-        if not last:
-            tt(ap("cu", 4 * t, 4 * t + 3), ap("dd", 1, 12, 4), ap("dd", 3, 12, 4), A.add)
-        else:
-            tt(ap("w4", 0, 27), ap("tab", 32, 59), ap("c0", 0, 27), A.subtract)
         op("V", lambda: g.vector.tensor_copy(T.xz[:, :].indirect(T.sl[:, 0:24]), T.bl[:, :]), [ap("sl", 0, 24), ap("bl")], [ap("xz")])
-        if t == 1:
-            tt(ap("cu", 8, 11), ap("cu", 0, 3), ap("cu", 4, 7), A.add)
+        if last:
+            for b in (MAGIC, -MAGIC):
+                act(ap("c0", 0, 27), ap("tab", 32, 59) if b > 0 else ap("c0", 0, 27), F.Identity, bias=b)
+            break
         for h in range(2):
             quant("z", half(h), H * h, H * h + H)
             mm(4 * h, "w", 0, "z", H * h, H * h + H)
@@ -524,76 +552,85 @@ def rank_program(g, core, T, topo):
             act(plane(b), xb(b), F.Copy, scale=32.0)
             if b:
                 mm(b, "w", 128 * b, "z", 0, C)
-        if not last:
-            tt(ap("o5"), ind(ap("cu", 8 * t, 8 * t + 3), ll("LC", 6)), cc("J5"), A.is_equal)
-        else:
-            tt(ap("pr", 0, 96), ind(ap("an"), ll("LS", 6)), ap("o2"), A.is_lt)
         for h in range(2):
-            pl = ap("xp", H * h, H * h + H)
-            tt(pl, ap("p%d" % (4 * h), 0, H), pl, A.add)
+            add_product(4 * h, h, 0)
         for b in range(4):
             if b:
                 tt(plane(b), ap("p%d" % b, 0, C), plane(b), A.add)
-            if not last:
-                gather_t(b, plane(b), ap("wl%d" % (t + 1), 0, 9), 2.0 ** -5, False)
-        if last:
-            break
-        ts(xb(2), plane(2), 2.0 ** -5, A.mult)
-        if t == 1:
-            weigh(80, ap("l0", 160, 320), "LW1")
+            gather_t(b, plane(b), ap("wl%d" % (t + 1), 0, 9), 2.0 ** -5, b == 3)
+        ts(ap("w3", 0, 9), ap("ws%d" % (t + 1), 0, 9), -4.0, A.mult)
         send_t(t + 1)
-        for b in (0, 1, 3):
-            act(xb(b), plane(b), F.Copy, scale=2.0 ** -5)
-        if t == 0:
-            weigh(240, ap("tab", 0, 92), "L3")
-        collect("l%d" % t, 80, 240 if t == 0 else 80)
-        own = ap("l0", 160, 240) if t == 0 else ap("l1", 80, 160)
-        k0 = own[1][0][1]
+        for h in range(2):
+            for b in range(3):
+                unscale(h, b, False)
+        ts(xb(3), plane(3), 2.0 ** -5, A.mult)
+        tt(ap("ow", 7, 72, 8), ap("l%d" % t, 7, 72, 8), ap("w3", 0, 9), A.add)
+        tt(ap("cu", 4 * t, 4 * t + 3), ap("dd", 1, 12, 4), ap("dd", 3, 12, 4), A.add)
         m = 54 + 27 * t
         k = (m + 15) // 16
-        tt(ap("o2", 0, 16 * k), ind(own, ll("LS", k)), ap("orep", 0, 16 * k), A.is_equal)
-        ts(ap("bl16", 0, 9), ap(own[1][0][0], k0 + 7, k0 + 72, 8), 0.25, A.mult)
-        tt(ap("pr", 0, m), ap("o2", 0, m), ap("nv", 96 * t, 96 * t + m), A.mult)
-        scan(ap("sel", 0, m), cc("K3", 0, m), ap("pr", 0, m), A.mult, A.max)
+        tt(ap("o2", 0, 16 * k), ind(ap("ow"), ll("LS", k)), ap("orep", 0, 16 * k), A.is_equal)
+        if t == 1:
+            tt(ap("cu", 8, 11), ap("cu", 0, 3), ap("cu", 4, 7), A.add)
+        else:
+            ts(ap("bl16", 0, 9), ap("ow", 7, 72, 8), 128.0, A.mult)
+        tt(ap("pr2", 0, m), ap("o2", 0, m), ap("nv", 96 * t, 96 * t + m), A.mult)
+        tt(ap("o5"), ind(ap("cu", 8 * t, 8 * t + 3), ll("LC", 4)), cc("J5", 0, 64), A.is_equal)
+        scan(ap("sel", 0, m), cc("K3", 0, m), ap("pr2", 0, m), A.mult, A.max)
+        if t == 0:
+            weigh(80, ap("pk", 32, 60), "L3")
+        else:
+            ts(ap("bl16", 0, 9), ap("ow", 7, 72, 8), 128.0, A.mult)
         tt(ap("tab", 32, 32 + m // 3), ap("tab", 32, 32 + m // 3), ap("sel", 2, m, 3), A.max)
-        quant("x", X)
-        mm(4, "u1", 0, "x", 0, C)
-        act(ap("s1"), ap("p4", 0, C), F.Copy)
-        tt(ap("pr", 0, 96), ind(ap("tab", 0, 64), ll("LT", 6)), ap("o5"), A.mult)
-        scan(ap("sel", 0, 90), cc("K5", 0, 90), ap("pr", 0, 90), A.mult, A.add)
-        targets(ind(ap("sel", 0, 90), ll("LR5", 4)), 64)
-        tt(ap("eq"), ind(own, ll("LE", 1)), ap("sel", 4, 80, 5), A.is_equal)
+        if t == 0:
+            collect("l0", 80, 80)
+        quant("x", half(0), 0, H)
+        tt(ap("pr2", 0, 64), ind(ap("tab", 0, 64), ll("LT", 4)), ap("o5"), A.mult)
+        quant("x", half(1), H, C)
+        act(ap("owr"), ind(ap("ow"), ll("LE", 1)), F.Copy, scale=512.0)
+        for h in range(2):
+            mm(4 + h, "u1", 0, "x", H * h, H * h + H)
+            act(ap("s1", H * h, H * h + H), ap("p%d" % (4 + h), 0, H), F.Copy)
+        scan(ap("sel", 0, 60), cc("K5", 0, 60), ap("pr2", 0, 60), A.mult, A.add)
+        targets(ind(ap("sel", 0, 60), ll("LR5", 4)), 64)
+        tt(ap("eq"), ind(ap("sel", 0, 60), ll("LF", 1)), ap("owr"), A.is_equal)
         gather_targets(64)
         scan(ap("th"), cc("H4"), ap("eq"), A.mult, A.add)
         own_scores()
 
-    def unscale(h, b):
-        o, a = ap("xz", X0 + 4 * H * h + b, X0 + 4 * H * (h + 1), 4), ap("xp", C * b + H * h, C * b + H * h + H)
-        if b < 2:
-            act(o, a, F.Copy, scale=2.0 ** -5)
-        else:
-            ts(o, a, 2.0 ** -5, A.mult)
-
     def finish(h):
         quant("x", half(h), H * h, H * h + H)
-        mm(4 + h, "v", 0, "x", H * h, H * h + H)
+        mm(h, "v", 0, "x", H * h, H * h + H)
         store("Y", T.oc[:, 4 * H * h:4 * H * (h + 1)], u8(ap("qx", H * h, H * h + H)))
 
-    for h, b in ((0, 0), (0, 1), (1, 0), (1, 1), (0, 2), (0, 3), (1, 2)):
-        unscale(h, b)
-    finish(0)
-    unscale(1, 3)
-    scan(ap("sel", 0, 81), cc("K3", 0, 81), ap("pr", 0, 81), A.mult, A.max)
-    finish(1)
     for h in range(2):
-        act(ap("yo", H * h, H * h + H), ap("p%d" % (4 + h), 0, H), F.Copy)
+        quant("z", half(h), H * h, H * h + H)
+        for b in range(4):
+            mm(4 * h + b, "w", 128 * b, "z", H * h, H * h + H)
+            act(piece(h, b), element(h, b), F.Copy, scale=32.0)
+    for b in range(4):
+        add_product(b, 0, b)
+    for b in range(4):
+        if b < 2:
+            unscale(0, b, False)
+        add_product(4 + b, 1, b)
+        if b < 2:
+            unscale(0, b + 2, True)
+        if b == 2:
+            finish(0)
+    for b in range(4):
+        unscale(1, b, b == 3)
+    finish(1)
+    tt(ap("pr", 0, 96), ind(ap("an"), ll("LS", 6)), ap("o2"), A.is_ge)
+    tt(ap("w4", 0, 27), ap("tab", 32, 59), ap("c0", 0, 27), A.subtract)
+    scan(ap("sel", 0, 81), cc("N3", 0, 81), ap("pr", 0, 81), A.max, A.min)
+    tt(ap("fr", 0, 27), ap("w4", 0, 27), ap("sel", 2, 81, 3), A.mult)
+    ts(ap("sko"), ind(ap("fr"), ll("LK", 2)), 1024.0, A.mult, 1.0, A.subtract)
+    for h in range(2):
+        act(ap("yo", H * h, H * h + H), ap("p%d" % h, 0, H), F.Copy)
         store("S", T.y[:, H * h:H * h + H], ap("yo", H * h, H * h + H))
     for k in range(4):
-        store("YYYS"[k], T.osc[4 * k:4 * k + 4, :], ap("sx"), T.sx[32 * k:32 * k + 4, :])
-    tt(ap("fr", 0, 27), ap("w4", 0, 27), ap("sel", 2, 81, 3), A.subtract)
-    ts(ap("sko"), ind(ap("fr"), ll("LK", 2)), 1024.0, A.mult, -1.0, A.max)
-    for c in range(3):
-        store("YSY"[c], T.sk[:, 160 * c:160 * c + 160], ap("sko", 10 * c, 10 * c + 10))
+        store("Y", T.osc[4 * k:4 * k + 4, :], ap("sx"), T.sx[32 * k:32 * k + 4, :])
+    store("Y", T.sk[:, :], ap("sko", 0, 30))
     for s in names:
         if count.get(s, 0):
             wait("Y", s, count[s])

@@ -7,12 +7,12 @@ X0 = 2048
 TILES = [["d", 29, 28, 27]] + [[c for c in range(h, h - 4, -1) if c > 0] for h in range(26, 0, -4)]
 WIDTH = [480] + [max(128, 16 * t[0]) for t in TILES[1:]]
 START = [sum(WIDTH[:i]) for i in range(len(WIDTH))]
-SPLIT = 23
+SPLIT = 22
 PIECES = [(0, 128), (128, 256), (256, C)]
 KW = 240
-LISTS = [("LA", 96), ("LW0", 96), ("L3", 96), ("LW1", 96), ("LD", 32), ("LR", 32), ("LR0", 32), ("LR5", 32), ("LH", 32),
+LISTS = [("LA", 96), ("LW0", 96), ("L3", 96), ("LW1", 96), ("LD", 32), ("LR", 32), ("LR0", 32), ("LR5", 32),
          ("LE", 32), ("LF", 32), ("LC", 64), ("LT", 64), ("LS", 96), ("LO", 96), ("LK", 32)]
-CONSTS = [("c16", 32), ("X8", 80), ("J5", 72), ("NV", 80), ("N0", 16), ("T4", 32), ("HB", 40), ("S0", 32), ("TH0", 16),
+CONSTS = [("c16", 32), ("X8", 80), ("J5", 72), ("NV", 80), ("N0", 16), ("T4", 32), ("S0", 8), ("TH0", 16),
           ("IDX", 24), ("NA", 24), ("FX", 24), ("K8", 80), ("K5", 64), ("K3", 96), ("N3", 96), ("H4", 16)]
 LAT = {k: (sum(v for _, v in LISTS[:i]), w) for i, (k, w) in enumerate(LISTS)}
 CAT = {k: (sum(v for _, v in CONSTS[:i]), w) for i, (k, w) in enumerate(CONSTS)}
@@ -31,13 +31,13 @@ def _mx(name, n):
 
 
 for _k, _w in [("xz", 4 * C + X0), ("xp", 4 * C), ("xs1", 4 * C), ("xs2", 4 * C), ("xs3", 4 * C), ("ub", 512), ("vb", 512),
-               ("ones", 516), ("zb", NL // 3), ("cl", NL), ("band", 512), ("tri", 512), ("eye", 516), ("iq", KW), ("dg", KW), ("keep", KW),
+               ("ones", 516), ("zb", NL // 2), ("cl", NL), ("band", 512), ("tri", 512), ("eye", 516), ("iq", KW), ("dg", KW), ("keep", KW),
                ("ext", KW), ("mt", 4 * sum(WIDTH)), ("sums", 256 * (30 - SPLIT)), ("sg", 8 * SPLIT * SPLIT), ("rowd", C), ("tt", 4 * NS), ("hh", 4 * NS * R),
                ("xg", 384), ("bl", 384), ("cmp", NS), ("hs", NS), ("acs", NS), ("k16", NS), ("h144", NS)]:
     _sb(_k, _w, "bfloat16")
 for _k, _w in [("pm", 8), ("cc", NC), ("cls", NL), ("mm", C), ("yy", C), ("jj", C), ("ob", C), ("ex", C), ("rs", 32), ("w1", 32),
                ("w2", 32), ("w3", 32), ("w4", 32), ("c0", 32), ("tab", 96), ("orep", 96), ("s1", C), ("bp", NS), ("cm", NS), ("oh", 80),
-               ("pr", 96), ("pr2", 96), ("l0", 160), ("l1", 80), ("dd", 16), ("th", 16), ("cu", 16), ("tg", 64), ("nv", 192), ("tf", 32), ("o2", 96),
+               ("pr", 96), ("pr2", 96), ("l0", 160), ("l1", 80), ("dd", 16), ("th", 16), ("cu", 16), ("tg", 32), ("nv", 192), ("tf", 32), ("o2", 96),
                ("pk", 64), ("ow", 80), ("owr", 16), ("o5", 64), ("sel", 96), ("eq", 16), ("fr", 32), ("an", 80), ("yo", C), ("sko", 32)]:
     _sb(_k, _w, "float32")
 for _k, _w in [("pi", 8), ("ui", 16)]:
@@ -241,7 +241,7 @@ def rank_program(g, core, T, topo):
     fill(ap("ones"), 1.0)
     zero(ap("zb"))
     zg = [gap(k) for k in range(3)]
-    zf = [ap("cl", lo, lo + NL // 3) for lo in range(0, NL, NL // 3)]
+    zf = [ap("cl", lo, lo + NL // 2) for lo in (0, NL // 2)]
     for sem, zeros in (("dz", zg), ("dz2", zf)):
         for o in zeros:
             z = ap("zb", 0, o[1][0][2] - o[1][0][1])
@@ -291,14 +291,15 @@ def rank_program(g, core, T, topo):
     for i in range(3):
         iota(cc("NA", 8 * i, 8 * i + 8), [[3, 2], [3, 2], [3, 2]], 9 + 3 * i)
     aff(ap("eye"), ap("ones"), [[1, 516]], A.is_equal, 0.0, -3, -4)
-    iota(cc("T4", 0, 36), [[1, 6], [0, 6]])
-    iota(cc("S0", 0, 24), [[NS, 4], [16, 2], [48, 3]])
+    iota(cc("T4", 0, 24), [[1, 4], [0, 6]])
+    iota(cc("T4", 24, 32), [[0, 8]])
+    iota(cc("S0", 0, 6), [[16, 2], [48, 3]])
     iota(cl("LA", 0, 72), [[48, 3], [0, 24]], 47)
     iota(cl("LD", 0, 12), [[48, 3], [16, 2], [0, 2]], 15)
     iota(cl("LR", 0, 24), [[0, 4], [2, 2], [4, 3]], 1)
     iota(cl("LR0", 0, 24), [[0, 4], [1, 6]])
     iota(cl("LR5", 0, 24), [[0, 4], [5, 2], [10, 3]], 4)
-    iota(cl("LH", 0, 24), [[0, 4], [5, 2], [10, 3]], 34)
+    iota(cl("LR5", 24, 30), [[5, 2], [10, 3]], 34)
     iota(cl("LE", 0, 12), [[24, 3], [0, 2], [8, 2]], 7)
     iota(cl("LF", 0, 12), [[10, 3], [5, 2], [0, 2]], 4)
     iota(cl("LC", 0, 60), [[0, 2], [1, 3], [0, 10]])
@@ -317,6 +318,8 @@ def rank_program(g, core, T, topo):
         lo, hi = PIECES[i]
         quant("x", ap("xz", X0 + 4 * lo, X0 + 4 * hi), lo, hi)
         mm((4, 5, 7)[i], "u0", 0, "x", lo, hi)
+        if hi == C:
+            mm(0, "u0", 0, "x", 0, C)
         mm((6, 3, 1)[i], "u0", 0, "x", 0, min(hi, 16 * SPLIT))
 
     def own_column(i):
@@ -352,7 +355,7 @@ def rank_program(g, core, T, topo):
     def on_scalar(blocks):
         def sg(c):
             return ap("sg", 8 * c * (c - 1), 8 * c * (c + 1))
-        for a, b in zip([None] + blocks, blocks + [None]):
+        for a, b in zip([None, None] + blocks, blocks + [None, None]):
             if b:
                 bank = (6, 3, 1)[[16 * b < hi for _, hi in PIECES].index(True)]
                 act(sg(b), ap("p%d" % bank, 0, 16 * b), F.Sign, scale=-1.0, bias=ap("yy", 16 * b + 15, 16 * b + 16))
@@ -361,32 +364,33 @@ def rank_program(g, core, T, topo):
 
     scores(0)
     ts(ap("keep"), ap("iq"), pm, A.is_gt)
+    for b in range(1, 4):
+        cp(ap("band", b, 512, 4), ap("band", 0, 512, 4))
     own_column(0)
     scores(1)
     spread(0)
-    own_column(1)
-    ts(ap("ext"), ap("keep"), 2.0 ** 20 + OFF, A.mult, 2.0 ** 20, A.subtract)
-    spread(1)
     for b in range(1, 4):
-        for k in ("band", "tri"):
-            cp(ap(k, b, 512, 4), ap("band", 0, 512, 4))
-    scores(2)
-    mm(0, "u0", 0, "x", 0, C)
+        cp(ap("tri", b, 512, 4), ap("band", 0, 512, 4))
     quant("b", ap("band"))
-    own_column(2)
+    own_column(1)
+    scores(2)
+    spread(1)
+    ts(ap("ext"), ap("keep"), 2.0 ** 20 + OFF, A.mult, 2.0 ** 20, A.subtract)
+    quant("r", ap("tri"))
     ts(ap("lp", 0, 30), ap("w3", 0, 30), pm30, A.add)
+    own_column(2)
+    scan(ap("w1", 0, 16), ap("ext", 0, 16), ap("w2", 0, 16), A.add, A.max)
     spread(2)
     on_scalar(list(range(3, SPLIT)) + [1, 2])
-    quant("r", ap("tri"))
+    ts(ap("lt0", 0, 1), ap("w1", 15, 16), pmoff, A.subtract)
+    pack(6)
     tt(slot(0, 0, 0, C), ap("p0", 0, C), ap("yy"), A.is_le)
-    scan(ap("w1", 0, 16), ap("ext", 0, 16), ap("w2", 0, 16), A.add, A.max)
-    after = {28: (6,), 26: (0, 5), 24: (4,), SPLIT: (1, 3, 2, 7)}
+    after = {26: (0,), 24: (4,), SPLIT: (1, 3, 2, 5, 7)}
     for c in range(29, SPLIT - 1, -1):
         compare(c)
         if c < 29:
             row_sum(c + 1)
         else:
-            ts(ap("lt0", 0, 1), ap("w1", 15, 16), pmoff, A.subtract)
             periodic("rowd", "keep", lambda i, j: slot(0, 0, i, j), 0, C, A.mult, A.add)
         for k in after.get(c, ()):
             if k == 1:
@@ -397,7 +401,7 @@ def rank_program(g, core, T, topo):
             if k == 2:
                 tt(ap("w2", SPLIT, 30), ap("w1", SPLIT, 30), ap("sums", 255, None, 256), A.subtract)
             pack(k)
-            for j in {0: (0, 6), 6: ()}.get(k, (k,)):
+            for j in (0, 6) if k == 0 else (k,):
                 count_tile(j)
     for c in range(3):
         act(cl("LW0", 24 * c, 24 * c + 24), cc("IDX"), F.Identity, scale=3.0, bias=float(c))
@@ -407,8 +411,9 @@ def rank_program(g, core, T, topo):
     act(ap("su1"), ind(ap("su"), ap("ul", 8, 16)), F.Copy)
     act(ap("cm"), ap("dg", 0, NS), F.Identity, scale=-2 * BIG, bias=BIG)
     for t in range(R):
-        act(ap("pm", 4 + t, 5 + t), pm, F.Identity, scale=1033.0 / 1024, bias=t * (4 * NS + NS / 1024))
+        act(ap("pm", 4 + t, 5 + t), pm, F.Identity, scale=1033.0 / 1024, bias=t * (NS + NS / 1024))
     tt(ap("w2", 0, SPLIT), ap("w1", 0, SPLIT), ap("rs", 0, SPLIT), A.subtract)
+    cp(u32(ap("qu1")), ind(u32(ap("qu")), ap("ul", 8, 16)))
     periodic("ex", "ext", lambda i, j: ap("p2", i, j), 0, C, A.add, A.max)
     tt(ap("w1", 0, 30), ap("w2", 0, 30), ap("ex", 15, C, 16), A.add)
     cp(ap("pos"), ap("w1", 0, 30))
@@ -447,7 +452,6 @@ def rank_program(g, core, T, topo):
     def late_constants():
         iota(ap("ow"), [[0, 80]])
         iota(cc("J5", 0, 65), [[0, 13], [1, 5]])
-        iota(cc("HB", 0, 36), [[NS, 6], [0, 6]])
         aff(cc("K3"), ap("ones", 0, 96), [[0, 32], [1, 3]], A.is_gt, 0.0, 0, 0)
         aff(cc("K5", 0, 60), ap("ones", 0, 60), [[0, 12], [1, 5]], A.is_gt, 0.0, 0, 0)
         iota(cc("H4"), [[0, 4], [1, 2], [1, 2]])
@@ -471,13 +475,12 @@ def rank_program(g, core, T, topo):
         else:
             act(element(h, b), piece(h, b), F.Copy, scale=2.0 ** -5)
 
-    def targets(src, w):
-        a = CAT["T4"][0]
-        tt(ap("tg", 0, w), src, ap("cc", a, a + w), A.add)
+    def targets(src):
+        tt(ap("tg"), src, cc("T4"), A.add)
 
     def gather_targets(w):
         cp(ap("gl", 0, w), ap("tg", 0, w))
-        act(ap("tf"), ap("tg", 0, 32), F.Copy, scale=1.0 / X0)
+        act(ap("tf"), ap("tg"), F.Copy, scale=1.0 / X0)
         act(ap("xg"), ind(X, ap("gl", 0, 24)), F.Copy, scale=0.5)
 
     def own_scores():
@@ -489,7 +492,6 @@ def rank_program(g, core, T, topo):
     def collect(out, lo, w):
         scan(ap(out, lo, lo + w), cc("K8", 0, w), ap("pr", 0, w), A.mult, A.add)
 
-    cp(u32(ap("qu1")), ind(u32(ap("qu")), ap("ul", 8, 16)))
     mm(3, "u1", 0, "x", 0, C)
     act(ap("s1"), ap("p3", 0, C), F.Copy)
     act(ap("pk", 0, 32), ap("tab", 0, 32), F.Copy, scale=1.0 / 512)
@@ -498,10 +500,10 @@ def rank_program(g, core, T, topo):
         scan(ap("cls", lo, hi), ap("ext", 0, hi - lo), ap("cl", lo, hi), A.add, A.max)
     ts(ap("bl16"), ind(ap("ex", 0, NS), ap("lt0", 0, 1)), pmoff, A.subtract)
     ts(ap("ll"), ap("cls", 15, NL, 16), pmoff, A.subtract)
-    ts(ap("gl", 32, 56), cc("S0", 0, 24), pm, A.add)
-    targets(ind(ap("tab", 0, 32), ll("LR0", 2)), 32)
+    ts(ap("gl", 24, 30), cc("S0", 0, 6), pm, A.add)
+    targets(ind(ap("tab", 0, 32), ll("LR0", 2)))
     own_scores()
-    gather_targets(32)
+    gather_targets(24)
     for b in range(4):
         quant("e", ap("eye", 3 - b, 515 - b), 128 * b, 128 * b + 128)
     quant("v", ap("vb"))
@@ -513,25 +515,29 @@ def rank_program(g, core, T, topo):
         for b in range(4):
             mm(4 + b, "e", 128 * b, a, 0, NS)
         for b in range(4):
-            act(ap("hh", 4 * NS * t + NS * b, 4 * NS * t + NS * b + NS), ap("p%d" % (4 + b), 0, NS), F.Copy, scale=0.5)
+            act(ap("hh", NS * (R * b + t), NS * (R * b + t + 1)), ap("p%d" % (4 + b), 0, NS), F.Copy, scale=0.5)
+
+        def blend(b):
+            o = (96 * b, 96 * b + 96)
+            tt(ap("bl", *o), ind(ap("hh", NS * R * b, NS * (R * b + t + 1)), ap("gl", 24, 30)), ap("xg", *o), A.add)
+
         tt(ap("cmp"), ap("p0", 0, NS), ap("bp"), A.is_ge)
-        scan(ap("hs"), ap("h144"), ap("cmp"), A.mult, A.add)
         if t == 0:
             tt(ap("pk", 32, 60), ap("tab", 64, 92), ap("pk", 0, 28), A.add)
+        scan(ap("hs"), ap("h144"), ap("cmp"), A.mult, A.add)
+        blend(0)
         if not last:
             tt(ap("oh", 0, 80), ind(ap("hs"), ll("LA", 5)), cc("X8"), A.is_equal)
         tt(ap("dd"), ind(ap("hs"), ll("LD", 1)), cc("TH0") if t == 0 else ap("th"), A.is_ge)
+        blend(1)
         if not last:
             weigh(80, ap("pk", 32, 60) if t == 0 else ap("l0", 0, 160), "LW%d" % t)
-        else:
-            scan(ap("acs"), ap("k16"), ap("cmp"), A.mult, A.add)
         tt(ap("w1"), ind(ap("dd"), ll("LR", 2)), ap("tf"), A.add)
+        blend(2)
         if not last:
             collect("l%d" % t, 0, 80)
-        else:
-            cp(ap("an", 7, 72, 8), ap("acs", 15, NS, 16))
-        ts(ap("sl"), ap("w1"), float(X0), A.mult)
-        if not last:
+            ts(ap("sl"), ap("w1"), float(X0), A.mult)
+            blend(3)
             ts(ap("ws%d" % (t + 1)), ap("l%d" % t, 7, 80, 8), 0.25, A.mult, 0.47, A.subtract)
             send(prv, ap("wl%d" % (t + 1)), ap("ws%d" % (t + 1)), "aw%d" % (t + 1))
             if t == 0:
@@ -539,61 +545,64 @@ def rank_program(g, core, T, topo):
                 act(ap("tab", 32, 41), cc("N0", 0, 9), F.Identity, scale=1.0 / 1024, bias=ap("pm", 4, 5))
                 act(ap("orep"), ind(ap("pk", 0, 32), ll("LO", 6)), F.Copy)
             act(ap("nv", 96 * t, 96 * t + 96), ind(cc("NV"), ll("LS", 6)), F.Identity, scale=1.0 / 1024, bias=ap("pm", 5 + t, 6 + t))
-        tt(ap("bl"), ind(ap("hh", 0, 4 * NS * (t + 1)), ap("gl", 32, 56)), ap("xg"), A.add)
-        op("V", lambda: g.vector.tensor_copy(T.xz[:, :].indirect(T.sl[:, 0:24]), T.bl[:, :]), [ap("sl", 0, 24), ap("bl")], [ap("xz")])
-        if last:
+            tt(ap("cu", 4 * t, 4 * t + 3), ap("dd", 1, 12, 4), ap("dd", 3, 12, 4), A.add)
+        else:
+            blend(3)
+            ts(ap("sl"), ap("w1"), float(X0), A.mult)
+            scan(ap("acs"), ap("k16"), ap("cmp"), A.mult, A.add)
             for b in (MAGIC, -MAGIC):
                 act(ap("c0", 0, 27), ap("tab", 32, 59) if b > 0 else ap("c0", 0, 27), F.Identity, bias=b)
+        op("V", lambda: g.vector.tensor_copy(T.xz[:, :].indirect(T.sl[:, 0:24]), T.bl[:, :]), [ap("sl", 0, 24), ap("bl")], [ap("xz")])
+        if last:
             break
+        m = 54 + 27 * t
+        k = (m + 15) // 16
+        ts(ap("w3", 0, 9), ap("ws%d" % (t + 1), 0, 9), -4.0, A.mult)
+        if t == 1:
+            tt(ap("cu", 8, 11), ap("cu", 0, 3), ap("cu", 4, 7), A.add)
         for h in range(2):
             quant("z", half(h), H * h, H * h + H)
-            mm(4 * h, "w", 0, "z", H * h, H * h + H)
-        for b in range(4):
+            for b in range(2):
+                mm(4 * h + b, "w", 128 * b, "z", H * h, H * h + H)
+                act(piece(h, b), element(h, b), F.Copy, scale=32.0)
+        for b in (2, 3):
+            mm(b, "w", 128 * b, "z", 0, C)
             act(plane(b), xb(b), F.Copy, scale=32.0)
-            if b:
-                mm(b, "w", 128 * b, "z", 0, C)
+        tt(ap("ow", 7, 72, 8), ap("l%d" % t, 7, 72, 8), ap("w3", 0, 9), A.add)
+        tt(ap("o5"), ind(ap("cu", 8 * t, 8 * t + 3), ll("LC", 4)), cc("J5", 0, 64), A.is_equal)
         for h in range(2):
-            add_product(4 * h, h, 0)
+            for b in range(2):
+                add_product(4 * h + b, h, b)
+        for b in (2, 3):
+            tt(plane(b), ap("p%d" % b, 0, C), plane(b), A.add)
+        tt(ap("o2", 0, 16 * k), ind(ap("ow"), ll("LS", k)), ap("orep", 0, 16 * k), A.is_equal)
         for b in range(4):
-            if b:
-                tt(plane(b), ap("p%d" % b, 0, C), plane(b), A.add)
             gather_t(b, plane(b), ap("wl%d" % (t + 1), 0, 9), 2.0 ** -5, b == 3)
-        ts(ap("w3", 0, 9), ap("ws%d" % (t + 1), 0, 9), -4.0, A.mult)
+        tt(ap("pr2", 0, m), ap("o2", 0, m), ap("nv", 96 * t, 96 * t + m), A.mult)
         send_t(t + 1)
         for h in range(2):
             for b in range(3):
                 unscale(h, b, False)
-        ts(xb(3), plane(3), 2.0 ** -5, A.mult)
-        tt(ap("ow", 7, 72, 8), ap("l%d" % t, 7, 72, 8), ap("w3", 0, 9), A.add)
-        tt(ap("cu", 4 * t, 4 * t + 3), ap("dd", 1, 12, 4), ap("dd", 3, 12, 4), A.add)
-        m = 54 + 27 * t
-        k = (m + 15) // 16
-        tt(ap("o2", 0, 16 * k), ind(ap("ow"), ll("LS", k)), ap("orep", 0, 16 * k), A.is_equal)
-        if t == 1:
-            tt(ap("cu", 8, 11), ap("cu", 0, 3), ap("cu", 4, 7), A.add)
-        else:
-            ts(ap("bl16", 0, 9), ap("ow", 7, 72, 8), 128.0, A.mult)
-        tt(ap("pr2", 0, m), ap("o2", 0, m), ap("nv", 96 * t, 96 * t + m), A.mult)
-        tt(ap("o5"), ind(ap("cu", 8 * t, 8 * t + 3), ll("LC", 4)), cc("J5", 0, 64), A.is_equal)
         scan(ap("sel", 0, m), cc("K3", 0, m), ap("pr2", 0, m), A.mult, A.max)
-        if t == 0:
-            weigh(80, ap("pk", 32, 60), "L3")
-        else:
-            ts(ap("bl16", 0, 9), ap("ow", 7, 72, 8), 128.0, A.mult)
+        unscale(0, 3, True)
+        unscale(1, 3, True)
         tt(ap("tab", 32, 32 + m // 3), ap("tab", 32, 32 + m // 3), ap("sel", 2, m, 3), A.max)
-        if t == 0:
-            collect("l0", 80, 80)
         quant("x", half(0), 0, H)
         tt(ap("pr2", 0, 64), ind(ap("tab", 0, 64), ll("LT", 4)), ap("o5"), A.mult)
+        if t == 0:
+            weigh(80, ap("pk", 32, 60), "L3")
+        ts(ap("bl16", 0, 9), ap("ow", 7, 72, 8), 128.0, A.mult)
+        scan(ap("sel", 0, 60), cc("K5", 0, 60), ap("pr2", 0, 60), A.mult, A.add)
         quant("x", half(1), H, C)
         act(ap("owr"), ind(ap("ow"), ll("LE", 1)), F.Copy, scale=512.0)
         for h in range(2):
             mm(4 + h, "u1", 0, "x", H * h, H * h + H)
             act(ap("s1", H * h, H * h + H), ap("p%d" % (4 + h), 0, H), F.Copy)
-        scan(ap("sel", 0, 60), cc("K5", 0, 60), ap("pr2", 0, 60), A.mult, A.add)
-        targets(ind(ap("sel", 0, 60), ll("LR5", 4)), 64)
+        targets(ind(ap("sel", 0, 60), ll("LR5", 2)))
         tt(ap("eq"), ind(ap("sel", 0, 60), ll("LF", 1)), ap("owr"), A.is_equal)
-        gather_targets(64)
+        if t == 0:
+            collect("l0", 80, 80)
+        gather_targets(30)
         scan(ap("th"), cc("H4"), ap("eq"), A.mult, A.add)
         own_scores()
 
@@ -602,11 +611,14 @@ def rank_program(g, core, T, topo):
         mm(h, "v", 0, "x", H * h, H * h + H)
         store("Y", T.oc[:, 4 * H * h:4 * H * (h + 1)], u8(ap("qx", H * h, H * h + H)))
 
+    cp(ap("an", 7, 72, 8), ap("acs", 15, NS, 16))
+    tt(ap("w4", 0, 27), ap("tab", 32, 59), ap("c0", 0, 27), A.subtract)
     for h in range(2):
         quant("z", half(h), H * h, H * h + H)
         for b in range(4):
             mm(4 * h + b, "w", 128 * b, "z", H * h, H * h + H)
             act(piece(h, b), element(h, b), F.Copy, scale=32.0)
+    tt(ap("pr", 0, 96), ind(ap("an"), ll("LS", 6)), ap("o2"), A.is_ge)
     for b in range(4):
         add_product(b, 0, b)
     for b in range(4):
@@ -617,13 +629,11 @@ def rank_program(g, core, T, topo):
             unscale(0, b + 2, True)
         if b == 2:
             finish(0)
+    scan(ap("sel", 0, 81), cc("N3", 0, 81), ap("pr", 0, 81), A.max, A.min)
     for b in range(4):
         unscale(1, b, b == 3)
-    finish(1)
-    tt(ap("pr", 0, 96), ind(ap("an"), ll("LS", 6)), ap("o2"), A.is_ge)
-    tt(ap("w4", 0, 27), ap("tab", 32, 59), ap("c0", 0, 27), A.subtract)
-    scan(ap("sel", 0, 81), cc("N3", 0, 81), ap("pr", 0, 81), A.max, A.min)
     tt(ap("fr", 0, 27), ap("w4", 0, 27), ap("sel", 2, 81, 3), A.mult)
+    finish(1)
     ts(ap("sko"), ind(ap("fr"), ll("LK", 2)), 1024.0, A.mult, 1.0, A.subtract)
     for h in range(2):
         act(ap("yo", H * h, H * h + H), ap("p%d" % h, 0, H), F.Copy)

@@ -1,18 +1,19 @@
 import numpy as np
-from concourse.mybir import dt, AluOpType as A, ActivationFunctionType as F
+from concourse.mybir import dt, AxisListType, AluOpType as A, ActivationFunctionType as F
 
 C, NS, R = 480, 144, 3
-BIG, MAGIC, OFF = 1e29, 12582912.0, 1024.0
+BIG, MAGIC, OFF, LOW = 1e29, 12582912.0, 1024.0, 2.0 ** 20
 X0 = 2048
 TILES = [["d", 29, 28, 27]] + [[c for c in range(h, h - 4, -1) if c > 0] for h in range(26, 0, -4)]
 WIDTH = [480] + [max(128, 16 * t[0]) for t in TILES[1:]]
 START = [sum(WIDTH[:i]) for i in range(len(WIDTH))]
 SPLIT = 22
+SHARE = 0
 PIECES = [(0, 128), (128, 256), (256, C)]
-KW = 240
-LISTS = [("LA", 96), ("LW0", 96), ("L3", 96), ("LW1", 96), ("LD", 32), ("LR", 32), ("LR0", 32), ("LR5", 32),
-         ("LE", 32), ("LF", 32), ("LC", 64), ("LT", 64), ("LS", 96), ("LO", 96), ("LK", 32)]
-CONSTS = [("c16", 32), ("X8", 80), ("J5", 72), ("NV", 80), ("N0", 16), ("T4", 32), ("S0", 8), ("TH0", 16),
+KW = 256
+LISTS = [("L0", 32), ("LA", 96), ("LD", 32), ("LR", 32), ("LR0", 32), ("LR5", 64), ("LE", 32), ("LF", 32), ("LC", 64),
+         ("LT", 64), ("LS", 96), ("LO", 96), ("LK", 32), ("LW0", 96), ("L3", 96), ("LW1", 96)]
+CONSTS = [("c16", 32), ("X8", 80), ("J5", 72), ("NV", 80), ("N0", 16), ("T4", 48), ("S0", 24), ("TH0", 16),
           ("IDX", 24), ("NA", 24), ("FX", 24), ("K8", 80), ("K5", 64), ("K3", 96), ("N3", 96), ("H4", 16)]
 LAT = {k: (sum(v for _, v in LISTS[:i]), w) for i, (k, w) in enumerate(LISTS)}
 CAT = {k: (sum(v for _, v in CONSTS[:i]), w) for i, (k, w) in enumerate(CONSTS)}
@@ -30,19 +31,19 @@ def _mx(name, n):
     _sb("s" + name, n, "uint8")
 
 
-for _k, _w in [("xz", 4 * C + X0), ("xp", 4 * C), ("xs1", 4 * C), ("xs2", 4 * C), ("xs3", 4 * C), ("ub", 512), ("vb", 512),
+for _k, _w in [("xz", 4 * C + X0), ("xp", 4 * C), ("ub", 512), ("vb", 512),
                ("ones", 516), ("zb", NL // 2), ("cl", NL), ("band", 512), ("tri", 512), ("eye", 516), ("iq", KW), ("dg", KW), ("keep", KW),
                ("ext", KW), ("mt", 4 * sum(WIDTH)), ("sums", 256 * (30 - SPLIT)), ("sg", 8 * SPLIT * SPLIT), ("rowd", C), ("tt", 4 * NS), ("hh", 4 * NS * R),
-               ("xg", 384), ("bl", 384), ("cmp", NS), ("hs", NS), ("acs", NS), ("k16", NS), ("h144", NS)]:
+               ("xg", 768), ("bl", 768), ("alt", 384), ("cmp", NS), ("hs", NS), ("acs", NS), ("k16", NS), ("h144", NS)]:
     _sb(_k, _w, "bfloat16")
-for _k, _w in [("pm", 8), ("cc", NC), ("cls", NL), ("mm", C), ("yy", C), ("jj", C), ("ob", C), ("ex", C), ("rs", 32), ("w1", 32),
+for _k, _w in [("pm", 8), ("cc", NC), ("cls", NL), ("mm", C), ("yy", C), ("jj", C), ("ob", C), ("ex", C), ("step", C), ("rs", 32), ("w1", 32),
                ("w2", 32), ("w3", 32), ("w4", 32), ("c0", 32), ("tab", 96), ("orep", 96), ("s1", C), ("bp", NS), ("cm", NS), ("oh", 80),
-               ("pr", 96), ("pr2", 96), ("l0", 160), ("l1", 80), ("dd", 16), ("th", 16), ("cu", 16), ("tg", 32), ("nv", 192), ("tf", 32), ("o2", 96),
+               ("pr", 96), ("pr2", 96), ("l0", 160), ("l1", 80), ("dd", 16), ("th", 16), ("cu", 16), ("tg", 48), ("nv", 192), ("tf", 32), ("o2", 96),
                ("pk", 64), ("ow", 80), ("owr", 16), ("o5", 64), ("sel", 96), ("eq", 16), ("fr", 32), ("an", 80), ("yo", C), ("sko", 32)]:
     _sb(_k, _w, "float32")
 for _k, _w in [("pi", 8), ("ui", 16)]:
     _sb(_k, _w, "int32")
-for _k, _w in [("ul", 16), ("lt0", 2), ("lp", 32), ("ll", NL // 16), ("pos", 30), ("tl0", 16), ("bl16", 16), ("ws1", 10), ("ws2", 10),
+for _k, _w in [("ul", 16), ("ll", NL // 16), ("pos", 30), ("bl16", 16), ("ws1", 10), ("ws2", 10),
                ("wl1", 10), ("wl2", 10), ("gl", 64), ("sl", 32)]:
     _sb(_k, _w, "uint16")
 for _k, _w in [("u", 128), ("u0", 128), ("u1", 128), ("v", 128), ("w", 512), ("e", 512), ("b", 128), ("r", 128), ("x", C), ("z", C), ("m", sum(WIDTH))]:
@@ -52,7 +53,7 @@ for _t in range(R):
     _mx("a%d" % _t, NS)
 for _t in range(8):
     SCRATCH["p%d" % _t] = ("psum", [128, 512], "float32")
-DMAS = ["dx0", "dx1", "dx2", "du", "dv", "dw", "dws", "d1", "d2", "d3", "dz", "dz2", "dout"]
+DMAS = ["dx0", "dx1", "dx2", "du", "dv", "dw", "dws", "dz", "dz2", "dout"]
 SEMAPHORES = ["eV", "eS", "eP", "eG", "snt", "ar0", "ar1", "ar2", "aow", "aw1", "aw2"] + DMAS
 
 
@@ -216,9 +217,9 @@ def rank_program(g, core, T, topo):
     def zero(o):
         act(o, ap("ones", 0, o[1][0][2] - o[1][0][1]), F.Copy, scale=0.0)
 
-    pm, pmoff, pc, pm30 = ap("pm", 0, 1), ap("pm", 1, 2), ap("pm", 2, 3), ap("pm", 3, 4)
+    pm, pmoff, pc, pm16, poff = (ap("pm", i, i + 1) for i in (0, 1, 2, 3, 7))
     X = ap("xz", X0, X0 + 4 * C)
-    H = C // 2
+    H, THIRD = C // 2, C // 3
 
     def xb(b):
         return ap("xz", X0 + b, X0 + 4 * C, 4)
@@ -247,8 +248,6 @@ def rank_program(g, core, T, topo):
             z = ap("zb", 0, o[1][0][2] - o[1][0][1])
             op("Y", lambda: g.sync.dma_start(o[0], z[0]), [z], [o], sem=sem, inc=16)
         mark(sem, count[sem], [ap("zb")[1][0]], [r for o in zeros for r in o[1]])
-    for t in range(1, 4):
-        load("Y", "d%d" % t, ap("xs%d" % t, 0, 4 * C - t), T.x[:, t:4 * C])
     load("Y", "dw", u8(ap("qw")), T.wc[:, :])
     load("Y", "dws", ap("sw"), T.ws[:, :])
     load("Y", "dv", ap("vb"), T.v[:, :])
@@ -259,30 +258,26 @@ def rank_program(g, core, T, topo):
     aff(ap("acs", 0, 128), ap("ones", 0, 128), [[-16, 8], [0, 16]], A.is_ge, 0.0, 0, 1)
     aff(ap("band", 0, 512, 4), ap("acs", 0, 128), [[16, 8], [0, 16]], A.is_ge, 0.0, 15, -1)
     aff(ap("tri", 0, 512, 4), ap("band", 0, 512, 4), [[1, 128]], A.is_gt, 0.0, 0, -1)
-    iota(ap("w2", 0, 16), [[0, 16]])
-    iota(ap("w2", 0, 9), [[16, 3], [48, 3]], 15)
-    iota(ap("w3", 0, 30), [[1, 10], [10, 3]])
     for k in (7, 6, 5):
         fill(gap(k), 0.0)
     ts(ap("pi", 1, 2), ap("pi", 0, 1), 15, A.bitwise_and)
     cp(ap("ul"), ap("ui"))
     cp(pm, ap("pi", 1, 2))
     zero(gap(4))
-    zero(ap("rs", 0, 1))
+    zero(ap("rs"))
     quant("u", ap("ub"))
     ts(ap("dg"), ap("iq"), pm, A.is_equal)
     cp(u32(ap("qu0")), ind(u32(ap("qu")), ap("ul", 0, 8)))
     act(ap("su0"), ind(ap("su"), ap("ul", 0, 8)), F.Copy)
     zero(gap(3))
     act(pmoff, pm, F.Identity, scale=-OFF, bias=15 * OFF)
-    act(pc, pm, F.Identity, scale=OFF - 1, bias=16 - 15 * OFF)
-    act(pm30, pm, F.Copy, scale=30.0)
+    act(pm16, pm, F.Identity, scale=-1.0, bias=16.0)
     iota(ap("jj"), [[1, C]])
     iota(cc("c16", 0, SPLIT), [[16, SPLIT]])
     iota(cc("c16", SPLIT, 30), [[16, 30 - SPLIT]], 16 * SPLIT - KW)
 
-    for lo, hi, pat, base in [(0, 4, [[0, 4]], 0), (4, 6, [[0, 2]], 1), (6, 8, [[1, 2]], 2), (8, 10, [[0, 2]], 1),
-                              (10, 14, [[0, 2], [1, 2]], 2), (14, 16, [[1, 2]], 3), (16, 24, [[1, 2], [1, 2], [1, 2]], 2)]:
+    for lo, hi, pat, base in [(0, 4, [[0, 4]], 0), (4, 6, [[0, 2]], 3), (6, 8, [[3, 2]], 6), (8, 10, [[0, 2]], 3),
+                              (10, 14, [[0, 2], [3, 2]], 6), (14, 16, [[3, 2]], 9), (16, 24, [[3, 2], [3, 2], [3, 2]], 6)]:
         iota(cc("IDX", lo, hi), pat, base)
     for lo, hi, pat, base in [(0, 4, [[0, 4]], 7), (4, 6, [[0, 2]], 15), (6, 8, [[64, 2]], 23), (8, 10, [[0, 2]], 15),
                               (10, 14, [[0, 2], [64, 2]], 23), (14, 16, [[8, 2]], 87), (16, 18, [[64, 2]], 23),
@@ -290,16 +285,13 @@ def rank_program(g, core, T, topo):
         iota(cc("FX", lo, hi), pat, base)
     for i in range(3):
         iota(cc("NA", 8 * i, 8 * i + 8), [[3, 2], [3, 2], [3, 2]], 9 + 3 * i)
-    aff(ap("eye"), ap("ones"), [[1, 516]], A.is_equal, 0.0, -3, -4)
-    iota(cc("T4", 0, 24), [[1, 4], [0, 6]])
-    iota(cc("T4", 24, 32), [[0, 8]])
-    iota(cc("S0", 0, 6), [[16, 2], [48, 3]])
+    iota(cl("L0", 0, 9), [[16, 3], [48, 3]], 15)
     iota(cl("LA", 0, 72), [[48, 3], [0, 24]], 47)
     iota(cl("LD", 0, 12), [[48, 3], [16, 2], [0, 2]], 15)
     iota(cl("LR", 0, 24), [[0, 4], [2, 2], [4, 3]], 1)
     iota(cl("LR0", 0, 24), [[0, 4], [1, 6]])
     iota(cl("LR5", 0, 24), [[0, 4], [5, 2], [10, 3]], 4)
-    iota(cl("LR5", 24, 30), [[5, 2], [10, 3]], 34)
+    iota(cl("LR5", 24, 48), [[0, 4], [5, 2], [10, 3]], 34)
     iota(cl("LE", 0, 12), [[24, 3], [0, 2], [8, 2]], 7)
     iota(cl("LF", 0, 12), [[10, 3], [5, 2], [0, 2]], 4)
     iota(cl("LC", 0, 60), [[0, 2], [1, 3], [0, 10]])
@@ -308,11 +300,11 @@ def rank_program(g, core, T, topo):
     iota(cl("LS", 0, 81), [[0, 9], [8, 9]], 7)
     iota(cl("LO", 0, 81), [[1, 27], [0, 3]])
     iota(cl("LK", 0, 30), [[1, 3], [3, 10]])
-    aff(ap("acs"), ap("ones", 0, NS), [[0, 9], [1, 16]], A.is_gt, 2.0, 0, 0)
-    aff(ap("h144"), ap("acs"), [[0, 3], [1, 48]], A.is_gt, 0.0, 0, 0)
-    iota(cc("X8"), [[0, 10], [1, 8]])
-    iota(cc("TH0"), [[0, 4], [2, 2], [0, 2]], 1)
-    aff(cc("K8"), ap("ones", 0, 80), [[0, 10], [1, 8]], A.is_gt, 0.0, 0, 0)
+    aff(ap("eye"), ap("ones"), [[1, 516]], A.is_equal, 0.0, -3, -4)
+    iota(cc("S0"), [[NS, 4], [16, 2], [48, 3]])
+    iota(cc("T4", 0, 24), [[1, 4], [0, 6]])
+    iota(cc("T4", 24, 48), [[NS, 4], [0, 6]])
+    iota(ap("alt"), [[0, 192], [1, 2]])
 
     def scores(i):
         lo, hi = PIECES[i]
@@ -339,31 +331,40 @@ def rank_program(g, core, T, topo):
         quant("m", ap("mt", 4 * START[k], 4 * (START[k] + WIDTH[k])), START[k], START[k] + WIDTH[k])
 
     def count_tile(k):
-        mm(2, "r" if k == 0 else "b", 0, "m", START[k], START[k] + WIDTH[k], k == 0, k == 7)
+        mm(2, "r" if k == 0 else "b", 0, "m", START[k], START[k] + WIDTH[k], k == 0, k == 5)
 
     def block(c, lo, hi):
         k = [c in tl for tl in TILES].index(True)
         return slot(k, TILES[k].index(c), lo, hi)
 
+    def shared(c):
+        return 16 * c if c < SPLIT else SHARE if c == SPLIT else 0
+
     def compare(c):
-        ts(block(c, 0, 16 * c), ap("p0", 0, 16 * c), ap("yy", 16 * c + 15, 16 * c + 16), A.is_lt)
+        ts(block(c, shared(c), 16 * c), ap("p0", shared(c), 16 * c), ap("yy", 16 * c + 15, 16 * c + 16), A.is_lt)
 
     def row_sum(c):
-        end = 256 * (c - SPLIT + 1)
-        scan(ap("sums", end - 8 * c, end), block(c, 0, 8 * c), block(c, 8 * c, 16 * c), A.add, A.add, -float(KW))
+        end, lo, w = 256 * (c - SPLIT + 1), shared(c), 8 * c - shared(c) // 2
+        scan(ap("sums", end - w, end), block(c, lo, lo + w), block(c, lo + w, 16 * c), A.add, A.add, -float(KW))
 
     def on_scalar(blocks):
         def sg(c):
-            return ap("sg", 8 * c * (c - 1), 8 * c * (c + 1))
+            return ap("sg", 8 * c * (c - 1), 8 * c * (c - 1) + shared(c))
         for a, b in zip([None, None] + blocks, blocks + [None, None]):
             if b:
                 bank = (6, 3, 1)[[16 * b < hi for _, hi in PIECES].index(True)]
-                act(sg(b), ap("p%d" % bank, 0, 16 * b), F.Sign, scale=-1.0, bias=ap("yy", 16 * b + 15, 16 * b + 16))
+                act(sg(b), ap("p%d" % bank, 0, shared(b)), F.Sign, scale=-1.0, bias=ap("yy", 16 * b + 15, 16 * b + 16))
             if a:
-                act(block(a, 0, 16 * a), sg(a), F.Relu, acc=ap("rs", a, a + 1))
+                act(block(a, 0, shared(a)), sg(a), F.Relu, acc=ap("rs", a, a + 1))
+            if a == 12:
+                act(ap("c0", 0, 30), cc("c16", 0, 30), F.Identity, bias=pc)
 
     scores(0)
     ts(ap("keep"), ap("iq"), pm, A.is_gt)
+    act(pc, ap("dg", 0, 1), F.Identity, scale=-LOW, bias=pm16)
+    act(poff, ap("dg", 0, 1), F.Identity, scale=-LOW, bias=pmoff)
+    for lo in range(0, C, H):
+        act(ap("step", lo, lo + H), ap("keep", 1, H + 1), F.Identity, scale=LOW + OFF, bias=-LOW)
     for b in range(1, 4):
         cp(ap("band", b, 512, 4), ap("band", 0, 512, 4))
     own_column(0)
@@ -375,79 +376,130 @@ def rank_program(g, core, T, topo):
     own_column(1)
     scores(2)
     spread(1)
-    ts(ap("ext"), ap("keep"), 2.0 ** 20 + OFF, A.mult, 2.0 ** 20, A.subtract)
+    ts(ap("ext"), ap("keep"), LOW + OFF, A.mult, LOW, A.subtract)
     quant("r", ap("tri"))
-    ts(ap("lp", 0, 30), ap("w3", 0, 30), pm30, A.add)
+    for c in (1, 2):
+        ts(block(c, 0, 16 * c), ap("p4", 0, 16 * c), ap("yy", 16 * c + 15, 16 * c + 16), A.is_lt)
     own_column(2)
-    scan(ap("w1", 0, 16), ap("ext", 0, 16), ap("w2", 0, 16), A.add, A.max)
+    for c in (1, 2):
+        o, a = ap("rs", c, c + 1), block(c, 0, 16 * c)
+        op("V", lambda: g.vector.tensor_reduce(o[0], a[0], AxisListType.X, A.add), [a], [o])
     spread(2)
-    on_scalar(list(range(3, SPLIT)) + [1, 2])
-    ts(ap("lt0", 0, 1), ap("w1", 15, 16), pmoff, A.subtract)
-    pack(6)
-    tt(slot(0, 0, 0, C), ap("p0", 0, C), ap("yy"), A.is_le)
-    after = {26: (0,), 24: (4,), SPLIT: (1, 3, 2, 5, 7)}
-    for c in range(29, SPLIT - 1, -1):
+    on_scalar(list(range(3, 8)) + list(range(11, 16)) + list(range(SPLIT - (SHARE == 0), 15, -1)) + [8, 9, 10])
+    pack(7)
+    compare(29)
+    after = {27: (6,), 26: (0,), 24: (4,), SPLIT: (1, 2, 3, 5)}
+    for c in range(28, SPLIT - 1, -1):
         compare(c)
-        if c < 29:
-            row_sum(c + 1)
-        else:
+        row_sum(c + 1)
+        if c == 28:
+            tt(slot(0, 0, 0, C), ap("p0", 0, C), ap("yy"), A.is_le)
+        if c == 27:
             periodic("rowd", "keep", lambda i, j: slot(0, 0, i, j), 0, C, A.mult, A.add)
         for k in after.get(c, ()):
             if k == 1:
-                ts(ap("c0", 0, 30), cc("c16", 0, 30), pc, A.add)
-            if k == 3:
-                row_sum(SPLIT)
                 tt(ap("w1", 0, 30), ap("c0", 0, 30), ap("rowd", 15, C, 16), A.subtract)
             if k == 2:
-                tt(ap("w2", SPLIT, 30), ap("w1", SPLIT, 30), ap("sums", 255, None, 256), A.subtract)
+                row_sum(SPLIT)
+            if k == 5:
+                tt(ap("w1", SPLIT, 30), ap("w1", SPLIT, 30), ap("sums", 255, None, 256), A.subtract)
             pack(k)
-            for j in (0, 6) if k == 0 else (k,):
+            for j in {0: (0, 6, 7), 6: ()}.get(k, (k,)):
                 count_tile(j)
-    for c in range(3):
-        act(cl("LW0", 24 * c, 24 * c + 24), cc("IDX"), F.Identity, scale=3.0, bias=float(c))
-        act(cl("L3", 24 * c, 24 * c + 24), cc("NA"), F.Identity, bias=float(c))
-        act(cl("LW1", 24 * c, 24 * c + 24), cc("FX"), F.Identity, bias=24.0 * c)
-    zero(ap("tab", 0, 64))
     act(ap("su1"), ind(ap("su"), ap("ul", 8, 16)), F.Copy)
+    for c, (lst, k, f) in [(c, e) for e in (("LW0", "IDX", 1.0), ("L3", "NA", 1.0), ("LW1", "FX", 24.0)) for c in range(3)]:
+        act(cl(lst, 24 * c, 24 * c + 24), cc(k), F.Identity, bias=f * c)
+    zero(ap("tab", 0, 64))
     act(ap("cm"), ap("dg", 0, NS), F.Identity, scale=-2 * BIG, bias=BIG)
     for t in range(R):
-        act(ap("pm", 4 + t, 5 + t), pm, F.Identity, scale=1033.0 / 1024, bias=t * (NS + NS / 1024))
-    tt(ap("w2", 0, SPLIT), ap("w1", 0, SPLIT), ap("rs", 0, SPLIT), A.subtract)
-    cp(u32(ap("qu1")), ind(u32(ap("qu")), ap("ul", 8, 16)))
-    periodic("ex", "ext", lambda i, j: ap("p2", i, j), 0, C, A.add, A.max)
-    tt(ap("w1", 0, 30), ap("w2", 0, 30), ap("ex", 15, C, 16), A.add)
-    cp(ap("pos"), ap("w1", 0, 30))
-    op("V", lambda: g.vector.tensor_copy(T.ob[:, :].indirect(T.pos[:, :]), T.jj[:, :]), [ap("pos"), ap("jj")], [ap("ob")])
-    cp(ap("mm", 0, NS), ind(ap("ob"), ap("lp", 0, 9)))
-    act(ap("yy", 0, 320), ind(ap("ob"), ap("lp", 8, 28)), F.Copy)
-    scan(ap("ex", 0, NS), ap("ext", 0, NS), ap("mm", 0, NS), A.add, A.max)
-    ts(ap("tl0"), ind(ap("ex", 0, NS), ap("lt0", 0, 1)), pmoff, A.subtract, 4.0, A.mult)
+        act(ap("pm", 4 + t, 5 + t), pm, F.Identity, scale=1027.0 / 1024, bias=t * (4 * NS + NS / 1024))
 
-    def gather_t(b, win, lst, scale, on_v):
-        o = ap("tt", b, 4 * NS, 4)
+    def wrap_lists(lo, hi):
+        scan(ap("cls", lo, hi), ap("ext", 0, hi - lo), ap("cl", lo, hi), A.add, A.max)
+
+    def cast_lists(lo, hi):
+        ts(ap("ll", lo // 16, hi // 16), ap("cls", lo + 15, hi, 16), pmoff, A.subtract)
+
+    def pack_eye(b):
+        quant("e", ap("eye", 3 - b, 515 - b), 128 * b, 128 * b + 128)
+
+    tt(ap("step", 15, C, 16), ap("w1", 0, 30), ap("rs", 0, 30), A.subtract)
+    cp(u32(ap("qu1")), ind(u32(ap("qu")), ap("ul", 8, 16)))
+    mm(3, "u1", 0, "x", 0, C)
+    for b in range(4):
+        act(plane(b), xb(b), F.Copy)
+    act(ap("s1"), ap("p3", 0, C), F.Copy)
+    wrap_lists(0, 128)
+    scan(ap("ex"), ap("p2", 0, C), ap("step"), A.max, A.add, -LOW)
+    wrap_lists(128, 256)
+    ts(ap("pos"), ap("ex", 15, C, 16), poff, A.subtract)
+    wrap_lists(256, 384)
+    op("V", lambda: g.vector.tensor_copy(T.ob[:, :].indirect(T.pos[:, :]), T.jj[:, :]), [ap("pos"), ap("jj")], [ap("ob")])
+
+    def wrap_item(k):
+        scan(ap("ex", 48 * k, 48 * k + 48), ap("ext", 0, 48), ap("ob", k, C, 10), A.add, A.max)
+
+    cast_lists(0, 384)
+    ts(ap("gl", 24, 48), cc("S0"), pm, A.add)
+    for k in range(6):
+        wrap_item(k)
+    ts(ap("bl16"), ind(ap("ex", 0, NS), ll("L0", 1)), pmoff, A.subtract)
+
+    def gather_t(b, win, lst, scale, on_v, lo=0, hi=9):
+        o = ap("tt", 64 * lo + b, 64 * hi, 4)
         if on_v:
-            ts(o, ind(win, lst), scale, A.mult)
+            ts(o, ind(win, ap(lst, lo, hi)), scale, A.mult)
         else:
-            act(o, ind(win, lst), F.Copy, scale=scale)
+            act(o, ind(win, ap(lst, lo, hi)), F.Copy, scale=scale)
 
     def send_t(t):
         quant("t%d" % t, ap("tt"))
         send(nxt, u8(ap("qa%d" % t)), u8(ap("qt%d" % t)), "ar%d" % t)
         send(nxt, ap("sa%d" % t), ap("st%d" % t), "ar%d" % t)
 
+    def targets(win, lst, k):
+        tt(ap("tg", 0, 16 * k), ind(win, ll(lst, k)), cc("T4", 0, 16 * k), A.add)
+
+    def gather_targets(w):
+        cp(ap("gl", 0, w), ap("tg", 0, w))
+        act(ap("tf"), ap("tg", 0, 32), F.Copy, scale=1.0 / X0)
+        act(ap("xg", 0, 768, 2), ind(X, ap("gl", 0, 24)), F.Copy, scale=0.5)
+
+    def own_scores():
+        tt(ap("bp"), ind(ap("s1"), ap("bl16", 0, 9)), ap("cm"), A.max)
+
     ts(ap("tab", 0, 9), ap("ex", 15, NS, 16), pmoff, A.subtract, 4.0, A.mult)
     send(nxt, ap("tab", 64, 73), ap("tab", 0, 9), "aow")
+    wrap_item(6)
+    wrap_item(7)
     for b in range(4):
-        gather_t(b, X if b == 0 else ap("xs%d" % b, 0, 4 * C - 3), ap("tl0", 0, 9), 1.0, b > 1)
+        gather_t(b, plane(b), "bl16", 1.0, b > 1)
+    wrap_item(8)
     send_t(0)
-    periodic("ex", "ext", lambda i, j: ap("yy", i, j), NS, 448, A.add, A.max, 16 - NS)
-    ts(ap("tab", 9, 28), ap("ex", NS + 15, 448, 16), pmoff, A.subtract, 4.0, A.mult)
+    ts(ap("tab", 9, 27), ap("ex", NS + 15, 432, 16), pmoff, A.subtract, 4.0, A.mult)
     send(nxt, ap("tab", 73, 92), ap("tab", 9, 28), "aow")
+    targets(ap("tab", 0, 8), "LR0", 2)
+    pack_eye(0)
+    pack_eye(1)
+    gather_targets(24)
+    own_scores()
+    pack_eye(2)
+    pack_eye(3)
+    for lo in range(384, NL, KW):
+        wrap_lists(lo, min(lo + KW, NL))
+    quant("v", ap("vb"))
+    cast_lists(384, NL)
+    act(ap("pk", 0, 32), ap("tab", 0, 32), F.Copy, scale=1.0 / 512)
 
+    aff(ap("acs"), ap("ones", 0, NS), [[0, 9], [1, 16]], A.is_gt, 2.0, 0, 0)
+    aff(ap("h144"), ap("acs"), [[0, 3], [1, 48]], A.is_gt, 0.0, 0, 0)
+    iota(cc("X8"), [[0, 10], [1, 8]])
+    iota(cc("TH0"), [[0, 4], [2, 2], [0, 2]], 1)
+    aff(cc("K8"), ap("ones", 0, 80), [[0, 10], [1, 8]], A.is_gt, 0.0, 0, 0)
     iota(cc("NV"), [[0, 80]])
     for c in range(3):
-        iota(cc("N0", c, 9, 3), [[16385, 3]], 49155 * c + 1)
-        iota(cc("NV", 24 * c + 7, 24 * c + 24, 8), [[16385, 3]], 49155 * c + 1)
+        iota(cc("N0", c, 9, 3), [[16385, 3]], 49200 * c + 1)
+        iota(cc("NV", 24 * c + 7, 24 * c + 24, 8), [[16385, 3]], 49200 * c + 1)
 
     def late_constants():
         iota(ap("ow"), [[0, 80]])
@@ -460,53 +512,34 @@ def rank_program(g, core, T, topo):
         iota(ap("an"), [[0, 80]])
         iota(ap("fr"), [[0, 32]])
 
-    def element(h, b):
-        return ap("xz", X0 + 4 * H * h + b, X0 + 4 * H * (h + 1), 4)
+    def columns(run):
+        return ap("xz", X0 + 4 * run[0], X0 + 4 * run[1])
 
-    def piece(h, b):
-        return ap("xp", C * b + H * h, C * b + H * h + H)
+    def element(run, b):
+        return ap("xz", X0 + 4 * run[0] + b, X0 + 4 * run[1], 4)
 
-    def add_product(bank, h, b):
-        tt(piece(h, b), ap("p%d" % bank, 0, H), piece(h, b), A.add)
+    def piece(run, b):
+        return ap("xp", C * b + run[0], C * b + run[1])
 
-    def unscale(h, b, on_v):
+    def products(run, bank):
+        for b in range(4):
+            mm(bank + b, "w", 128 * b, "z", *run)
+            act(piece(run, b), element(run, b), F.Copy, scale=32.0)
+
+    def add_product(run, bank, b):
+        tt(piece(run, b), ap("p%d" % (bank + b), 0, run[1] - run[0]), piece(run, b), A.add)
+
+    def unscale(run, b, on_v):
         if on_v:
-            ts(element(h, b), piece(h, b), 2.0 ** -5, A.mult)
+            ts(element(run, b), piece(run, b), 2.0 ** -5, A.mult)
         else:
-            act(element(h, b), piece(h, b), F.Copy, scale=2.0 ** -5)
-
-    def targets(src):
-        tt(ap("tg"), src, cc("T4"), A.add)
-
-    def gather_targets(w):
-        cp(ap("gl", 0, w), ap("tg", 0, w))
-        act(ap("tf"), ap("tg"), F.Copy, scale=1.0 / X0)
-        act(ap("xg"), ind(X, ap("gl", 0, 24)), F.Copy, scale=0.5)
-
-    def own_scores():
-        tt(ap("bp"), ind(ap("s1"), ap("bl16", 0, 9)), ap("cm"), A.max)
+            act(element(run, b), piece(run, b), F.Copy, scale=2.0 ** -5)
 
     def weigh(w, win, lst):
         tt(ap("pr", 0, w), ind(win, ll(lst, w // 16)), ap("oh", 0, w), A.mult)
 
     def collect(out, lo, w):
         scan(ap(out, lo, lo + w), cc("K8", 0, w), ap("pr", 0, w), A.mult, A.add)
-
-    mm(3, "u1", 0, "x", 0, C)
-    act(ap("s1"), ap("p3", 0, C), F.Copy)
-    act(ap("pk", 0, 32), ap("tab", 0, 32), F.Copy, scale=1.0 / 512)
-    for lo in range(0, NL, KW):
-        hi = min(NL, lo + KW)
-        scan(ap("cls", lo, hi), ap("ext", 0, hi - lo), ap("cl", lo, hi), A.add, A.max)
-    ts(ap("bl16"), ind(ap("ex", 0, NS), ap("lt0", 0, 1)), pmoff, A.subtract)
-    ts(ap("ll"), ap("cls", 15, NL, 16), pmoff, A.subtract)
-    ts(ap("gl", 24, 30), cc("S0", 0, 6), pm, A.add)
-    targets(ind(ap("tab", 0, 32), ll("LR0", 2)))
-    own_scores()
-    gather_targets(24)
-    for b in range(4):
-        quant("e", ap("eye", 3 - b, 515 - b), 128 * b, 128 * b + 128)
-    quant("v", ap("vb"))
 
     for t in range(R):
         last = t == R - 1
@@ -515,16 +548,27 @@ def rank_program(g, core, T, topo):
         for b in range(4):
             mm(4 + b, "e", 128 * b, a, 0, NS)
         for b in range(4):
-            act(ap("hh", NS * (R * b + t), NS * (R * b + t + 1)), ap("p%d" % (4 + b), 0, NS), F.Copy, scale=0.5)
+            act(ap("hh", NS * (4 * t + b), NS * (4 * t + b + 1)), ap("p%d" % (4 + b), 0, NS), F.Copy, scale=0.5)
+
+        def held(b):
+            return ind(ap("hh", 0, NS * (4 * t + b + 1)), ap("gl", 24 + 6 * b, 30 + 6 * b))
 
         def blend(b):
-            o = (96 * b, 96 * b + 96)
-            tt(ap("bl", *o), ind(ap("hh", NS * R * b, NS * (R * b + t + 1)), ap("gl", 24, 30)), ap("xg", *o), A.add)
+            tt(ap("bl", 192 * b + 1, 192 * b + 192, 2), held(b), ap("xg", 192 * b, 192 * b + 192, 2), A.add)
+
+        def blend_from(b):
+            scan(ap("bl", 192 * b, 768), ap("alt", 192 * b - 384, 384), ap("xg", 192 * b, 768), A.mult, A.add)
+
+        shared_from = 3 if last else 2
+        for b in range(shared_from, 4):
+            act(ap("xg", 192 * b + 1, 192 * b + 192, 2), held(b), F.Copy)
 
         tt(ap("cmp"), ap("p0", 0, NS), ap("bp"), A.is_ge)
+        scan(ap("hs"), ap("h144"), ap("cmp"), A.mult, A.add)
         if t == 0:
             tt(ap("pk", 32, 60), ap("tab", 64, 92), ap("pk", 0, 28), A.add)
-        scan(ap("hs"), ap("h144"), ap("cmp"), A.mult, A.add)
+        if last:
+            scan(ap("acs"), ap("k16"), ap("cmp"), A.mult, A.add)
         blend(0)
         if not last:
             tt(ap("oh", 0, 80), ind(ap("hs"), ll("LA", 5)), cc("X8"), A.is_equal)
@@ -533,11 +577,10 @@ def rank_program(g, core, T, topo):
         if not last:
             weigh(80, ap("pk", 32, 60) if t == 0 else ap("l0", 0, 160), "LW%d" % t)
         tt(ap("w1"), ind(ap("dd"), ll("LR", 2)), ap("tf"), A.add)
-        blend(2)
         if not last:
+            blend_from(2)
             collect("l%d" % t, 0, 80)
             ts(ap("sl"), ap("w1"), float(X0), A.mult)
-            blend(3)
             ts(ap("ws%d" % (t + 1)), ap("l%d" % t, 7, 80, 8), 0.25, A.mult, 0.47, A.subtract)
             send(prv, ap("wl%d" % (t + 1)), ap("ws%d" % (t + 1)), "aw%d" % (t + 1))
             if t == 0:
@@ -545,102 +588,117 @@ def rank_program(g, core, T, topo):
                 act(ap("tab", 32, 41), cc("N0", 0, 9), F.Identity, scale=1.0 / 1024, bias=ap("pm", 4, 5))
                 act(ap("orep"), ind(ap("pk", 0, 32), ll("LO", 6)), F.Copy)
             act(ap("nv", 96 * t, 96 * t + 96), ind(cc("NV"), ll("LS", 6)), F.Identity, scale=1.0 / 1024, bias=ap("pm", 5 + t, 6 + t))
-            tt(ap("cu", 4 * t, 4 * t + 3), ap("dd", 1, 12, 4), ap("dd", 3, 12, 4), A.add)
         else:
-            blend(3)
+            blend(2)
             ts(ap("sl"), ap("w1"), float(X0), A.mult)
-            scan(ap("acs"), ap("k16"), ap("cmp"), A.mult, A.add)
+            blend_from(3)
+            act(ap("an", 7, 72, 8), ap("acs", 15, NS, 16), F.Copy)
+            tt(ap("pr", 0, 96), ind(ap("an"), ll("LS", 6)), ap("o2"), A.is_ge)
             for b in (MAGIC, -MAGIC):
                 act(ap("c0", 0, 27), ap("tab", 32, 59) if b > 0 else ap("c0", 0, 27), F.Identity, bias=b)
-        op("V", lambda: g.vector.tensor_copy(T.xz[:, :].indirect(T.sl[:, 0:24]), T.bl[:, :]), [ap("sl", 0, 24), ap("bl")], [ap("xz")])
+        op("V", lambda: g.vector.tensor_copy(T.xz[:, :].indirect(T.sl[:, 0:24]), T.bl[:, 1:768:2]), [ap("sl", 0, 24), ap("bl", 1, 768, 2)], [ap("xz")])
         if last:
             break
         m = 54 + 27 * t
         k = (m + 15) // 16
         ts(ap("w3", 0, 9), ap("ws%d" % (t + 1), 0, 9), -4.0, A.mult)
-        if t == 1:
-            tt(ap("cu", 8, 11), ap("cu", 0, 3), ap("cu", 4, 7), A.add)
-        for h in range(2):
-            quant("z", half(h), H * h, H * h + H)
-            for b in range(2):
-                mm(4 * h + b, "w", 128 * b, "z", H * h, H * h + H)
-                act(piece(h, b), element(h, b), F.Copy, scale=32.0)
-        for b in (2, 3):
-            mm(b, "w", 128 * b, "z", 0, C)
-            act(plane(b), xb(b), F.Copy, scale=32.0)
+        tt(ap("cu", 4 * t, 4 * t + 3), ap("dd", 1, 12, 4), ap("dd", 3, 12, 4), A.add)
+
+        def at_cursor():
+            tt(ap("o5"), ind(ap("cu", 8 * t, 8 * t + 3), ll("LC", 4)), cc("J5", 0, 64), A.is_equal)
+
+        runs = ((0, THIRD), (THIRD, C))
+        for h, run in enumerate(runs):
+            quant("z", columns(run), *run)
+            products(run, 4 * h)
         tt(ap("ow", 7, 72, 8), ap("l%d" % t, 7, 72, 8), ap("w3", 0, 9), A.add)
-        tt(ap("o5"), ind(ap("cu", 8 * t, 8 * t + 3), ll("LC", 4)), cc("J5", 0, 64), A.is_equal)
-        for h in range(2):
-            for b in range(2):
-                add_product(4 * h + b, h, b)
-        for b in (2, 3):
-            tt(plane(b), ap("p%d" % b, 0, C), plane(b), A.add)
+        if t == 0:
+            at_cursor()
+        else:
+            tt(ap("cu", 8, 11), ap("cu", 0, 3), ap("cu", 4, 7), A.add)
+        for h, run in enumerate(runs):
+            for b in range(4):
+                add_product(run, 4 * h, b)
         tt(ap("o2", 0, 16 * k), ind(ap("ow"), ll("LS", k)), ap("orep", 0, 16 * k), A.is_equal)
         for b in range(4):
-            gather_t(b, plane(b), ap("wl%d" % (t + 1), 0, 9), 2.0 ** -5, b == 3)
+            gather_t(b, plane(b), "wl%d" % (t + 1), 2.0 ** -5, b == 3)
         tt(ap("pr2", 0, m), ap("o2", 0, m), ap("nv", 96 * t, 96 * t + m), A.mult)
         send_t(t + 1)
-        for h in range(2):
-            for b in range(3):
-                unscale(h, b, False)
+        for b in range(2):
+            unscale((0, C), b, False)
         scan(ap("sel", 0, m), cc("K3", 0, m), ap("pr2", 0, m), A.mult, A.max)
-        unscale(0, 3, True)
-        unscale(1, 3, True)
+        for b in (3, 2):
+            unscale((0, C), b, True)
         tt(ap("tab", 32, 32 + m // 3), ap("tab", 32, 32 + m // 3), ap("sel", 2, m, 3), A.max)
+        if t == 1:
+            at_cursor()
         quant("x", half(0), 0, H)
         tt(ap("pr2", 0, 64), ind(ap("tab", 0, 64), ll("LT", 4)), ap("o5"), A.mult)
+        quant("x", half(1), H, C)
+        scan(ap("sel", 0, 60), cc("K5", 0, 60), ap("pr2", 0, 60), A.mult, A.add)
         if t == 0:
             weigh(80, ap("pk", 32, 60), "L3")
         ts(ap("bl16", 0, 9), ap("ow", 7, 72, 8), 128.0, A.mult)
-        scan(ap("sel", 0, 60), cc("K5", 0, 60), ap("pr2", 0, 60), A.mult, A.add)
-        quant("x", half(1), H, C)
         act(ap("owr"), ind(ap("ow"), ll("LE", 1)), F.Copy, scale=512.0)
         for h in range(2):
             mm(4 + h, "u1", 0, "x", H * h, H * h + H)
             act(ap("s1", H * h, H * h + H), ap("p%d" % (4 + h), 0, H), F.Copy)
-        targets(ind(ap("sel", 0, 60), ll("LR5", 2)))
+        targets(ap("sel", 0, 60), "LR5", 3)
         tt(ap("eq"), ind(ap("sel", 0, 60), ll("LF", 1)), ap("owr"), A.is_equal)
         if t == 0:
             collect("l0", 80, 80)
-        gather_targets(30)
+        gather_targets(48)
         scan(ap("th"), cc("H4"), ap("eq"), A.mult, A.add)
         own_scores()
 
-    def finish(h):
-        quant("x", half(h), H * h, H * h + H)
-        mm(h, "v", 0, "x", H * h, H * h + H)
-        store("Y", T.oc[:, 4 * H * h:4 * H * (h + 1)], u8(ap("qx", H * h, H * h + H)))
+    runs = [(0, THIRD), (THIRD, C - 128), (C - 128, C)]
 
-    cp(ap("an", 7, 72, 8), ap("acs", 15, NS, 16))
-    tt(ap("w4", 0, 27), ap("tab", 32, 59), ap("c0", 0, 27), A.subtract)
-    for h in range(2):
-        quant("z", half(h), H * h, H * h + H)
-        for b in range(4):
-            mm(4 * h + b, "w", 128 * b, "z", H * h, H * h + H)
-            act(piece(h, b), element(h, b), F.Copy, scale=32.0)
-    tt(ap("pr", 0, 96), ind(ap("an"), ll("LS", 6)), ap("o2"), A.is_ge)
-    for b in range(4):
-        add_product(b, 0, b)
-    for b in range(4):
-        if b < 2:
-            unscale(0, b, False)
-        add_product(4 + b, 1, b)
-        if b < 2:
-            unscale(0, b + 2, True)
-        if b == 2:
-            finish(0)
+    def finish(i):
+        lo, hi = runs[i]
+        quant("x", columns(runs[i]), lo, hi)
+        mm(4 + i, "v", 0, "x", lo, hi)
+        store("Y", T.oc[:, 4 * lo:4 * hi], u8(ap("qx", lo, hi)))
+
+    def store_y(i):
+        lo, hi = runs[i]
+        act(ap("yo", lo, hi), ap("p%d" % (4 + i), 0, hi - lo), F.Copy)
+        store("YSS"[i], T.y[:, lo:hi], ap("yo", lo, hi))
+
     scan(ap("sel", 0, 81), cc("N3", 0, 81), ap("pr", 0, 81), A.max, A.min)
-    for b in range(4):
-        unscale(1, b, b == 3)
+    tt(ap("w4", 0, 27), ap("tab", 32, 59), ap("c0", 0, 27), A.subtract)
+    for i in range(3):
+        quant("z", columns(runs[i]), *runs[i])
+    products(runs[0], 0)
     tt(ap("fr", 0, 27), ap("w4", 0, 27), ap("sel", 2, 81, 3), A.mult)
+    act(ap("sko"), ind(ap("fr"), ll("LK", 2)), F.Identity, scale=1024.0, bias=-1.0)
+    for c in range(3):
+        store("Y", T.sk[:, 160 * c:160 * c + 160], ap("sko", 10 * c, 10 * c + 10))
+    products(runs[1], 4)
+    for b in range(4):
+        add_product(runs[0], 0, b)
+    products(runs[2], 0)
+    for b in range(4):
+        unscale(runs[0], b, True)
+    for b in range(4):
+        add_product(runs[1], 4, b)
+        if b < 2:
+            unscale(runs[1], b, False)
+        if b == 1:
+            finish(0)
+    store_y(0)
+    for b in range(4):
+        add_product(runs[2], 0, b)
+        if b == 1:
+            unscale(runs[1], 2, True)
+            unscale(runs[1], 3, True)
     finish(1)
-    ts(ap("sko"), ind(ap("fr"), ll("LK", 2)), 1024.0, A.mult, 1.0, A.subtract)
-    for h in range(2):
-        act(ap("yo", H * h, H * h + H), ap("p%d" % h, 0, H), F.Copy)
-        store("S", T.y[:, H * h:H * h + H], ap("yo", H * h, H * h + H))
+    for b in range(4):
+        unscale(runs[2], b, b > 1)
+    finish(2)
+    store_y(1)
+    store_y(2)
     for k in range(4):
         store("Y", T.osc[4 * k:4 * k + 4, :], ap("sx"), T.sx[32 * k:32 * k + 4, :])
-    store("Y", T.sk[:, :], ap("sko", 0, 30))
     for s in names:
         if count.get(s, 0):
             wait("Y", s, count[s])

import numpy as np
from concourse.mybir import dt, AxisListType, AluOpType as A, ActivationFunctionType as F

C, NS, R = 480, 144, 3
BIG, MAGIC, OFF, LOW = 1e29, 12582912.0, 1024.0, 2.0 ** 20
X0 = 2048
TILES = [["d", 29, 28, 27]] + [[c for c in range(h, h - 4, -1) if c > 0] for h in range(26, 0, -4)]
WIDTH = [480] + [max(128, 16 * t[0]) for t in TILES[1:]]
START = [sum(WIDTH[:i]) for i in range(len(WIDTH))]
SPLIT = 22
SHARE = 0
PIECES = [(0, 128), (128, 256), (256, C)]
KW = 256
LISTS = [("L0", 32), ("LA", 96), ("LD", 32), ("LR", 32), ("LR0", 32), ("LR5", 64), ("LE", 32), ("LF", 32), ("LC", 64),
         ("LT", 64), ("LS", 96), ("LO", 96), ("LK", 32), ("LW0", 96), ("L3", 96), ("LW1", 96)]
CONSTS = [("c16", 32), ("X8", 80), ("J5", 72), ("NV", 80), ("N0", 16), ("T4", 48), ("S0", 24), ("TH0", 16),
          ("IDX", 24), ("NA", 24), ("FX", 24), ("K8", 80), ("K5", 64), ("K3", 96), ("N3", 96), ("H4", 16)]
LAT = {k: (sum(v for _, v in LISTS[:i]), w) for i, (k, w) in enumerate(LISTS)}
CAT = {k: (sum(v for _, v in CONSTS[:i]), w) for i, (k, w) in enumerate(CONSTS)}
NL, NC = sum(w for _, w in LISTS), sum(w for _, w in CONSTS)

SCRATCH = {}


def _sb(name, n, d):
    SCRATCH[name] = ("sbuf", [128, n], d)


def _mx(name, n):
    _sb("q" + name, n, "float8_e4m3fn_x4")
    _sb("s" + name, n, "uint8")


for _k, _w in [("xz", 4 * C + X0), ("xp", 4 * C), ("ub", 512), ("vb", 512),
               ("ones", 516), ("zb", NL // 2), ("cl", NL), ("band", 512), ("tri", 512), ("eye", 516), ("iq", KW), ("dg", KW), ("keep", KW),
               ("ext", KW), ("mt", 4 * sum(WIDTH)), ("sums", 256 * (30 - SPLIT)), ("sg", 8 * SPLIT * SPLIT), ("rowd", C), ("tt", 4 * NS), ("hh", 4 * NS * R),
               ("xg", 768), ("bl", 768), ("alt", 384), ("cmp", NS), ("hs", NS), ("acs", NS), ("k16", NS), ("h144", NS)]:
    _sb(_k, _w, "bfloat16")
for _k, _w in [("pm", 8), ("cc", NC), ("cls", NL), ("mm", C), ("yy", C), ("jj", C), ("ob", C), ("ex", C), ("step", C), ("rs", 32), ("w1", 32),
               ("w2", 32), ("w3", 32), ("w4", 32), ("c0", 32), ("tab", 96), ("orep", 96), ("s1", C), ("bp", NS), ("cm", NS), ("oh", 80),
               ("pr", 96), ("pr2", 96), ("l0", 160), ("l1", 80), ("dd", 16), ("th", 16), ("cu", 16), ("tg", 48), ("nv", 192), ("tf", 32), ("o2", 96),
               ("pk", 64), ("ow", 80), ("owr", 16), ("o5", 64), ("sel", 96), ("eq", 16), ("fr", 32), ("an", 80), ("yo", C), ("sko", 32)]:
    _sb(_k, _w, "float32")
for _k, _w in [("pi", 8), ("ui", 16)]:
    _sb(_k, _w, "int32")
for _k, _w in [("ul", 16), ("ll", NL // 16), ("pos", 30), ("bl16", 16), ("ws1", 10), ("ws2", 10),
               ("wl1", 10), ("wl2", 10), ("gl", 64), ("sl", 32)]:
    _sb(_k, _w, "uint16")
for _k, _w in [("u", 128), ("u0", 128), ("u1", 128), ("v", 128), ("w", 512), ("e", 512), ("b", 128), ("r", 128), ("x", C), ("z", C), ("m", sum(WIDTH))]:
    _mx(_k, _w)
for _t in range(R):
    _mx("t%d" % _t, NS)
    _mx("a%d" % _t, NS)
for _t in range(8):
    SCRATCH["p%d" % _t] = ("psum", [128, 512], "float32")
DMAS = ["dx0", "dx1", "dx2", "du", "dv", "dw", "dws", "dz", "dz2", "dout"]
SEMAPHORES = ["eV", "eS", "eP", "eG", "snt", "ar0", "ar1", "ar2", "aow", "aw1", "aw2"] + DMAS


def rank_program(g, core, T, topo):
    rank = T.rank_of(core)
    if rank is None:
        return
    n = len(T.cores)
    nxt, prv = T.cores[(rank + 1) % n], T.cores[(rank - 1) % n]
    Q = {"V": g.vector, "S": g.scalar, "P": g.tensor, "G": g, "Y": g.sync}
    count, waited, wr, rd = {}, {}, {}, {}
    names = list(SEMAPHORES)

    def ap(name, lo=0, hi=None, st=1):
        hi = SCRATCH[name][1][1] if hi is None else hi
        return (T[name][:, lo:hi:st] if st > 1 else T[name][:, lo:hi], [(name, lo, hi, st)])

    def ind(w, o):
        return (w[0].indirect(o[0]), w[1] + o[1])

    def u8(v):
        return (v[0].bitcast(dt.uint8), v[1])

    def u32(v):
        return (v[0].bitcast(dt.uint32), v[1])

    def cells(name):
        if name not in wr:
            k = 1 if SCRATCH[name][0] == "psum" else SCRATCH[name][1][1]
            wr[name] = np.zeros((len(names), k), np.int64)
            rd[name] = np.zeros((len(names), k), np.int64)
        return wr[name], rd[name]

    def sl(r):
        return slice(0, 1) if SCRATCH[r[0]][0] == "psum" else slice(r[1], r[2], r[3])

    def wait(e, s, v):
        if waited.get((e, s), 0) < v:
            Q[e].wait_ge(T.sem[s], int(v))
            waited[(e, s)] = v

    def mark(s, v, reads, writes):
        i = names.index(s)
        for r in writes:
            w, q = cells(r[0])
            w[:, sl(r)] = 0
            q[:, sl(r)] = 0
            w[i, sl(r)] = v
        for r in reads:
            cells(r[0])[1][i, sl(r)] = v

    def op(e, call, reads, writes, sem=None, inc=1, chain=False):
        reads = [r for v in reads if isinstance(v, tuple) for r in v[1]]
        writes = [r for v in writes for r in v[1]]
        s = sem or "e" + e
        need = np.zeros(len(names), np.int64)
        for r in reads:
            w, q = cells(r[0])
            need = np.maximum(need, w[:, sl(r)].max(axis=1))
            if SCRATCH[r[0]][0] == "psum":
                o = q[:, 0].copy()
                o[names.index(s)] = 0
                need = np.maximum(need, o)
        for r in writes:
            w, q = cells(r[0])
            need = np.maximum(need, np.maximum(w[:, sl(r)].max(axis=1), q[:, sl(r)].max(axis=1)))
        if chain:
            need[names.index(s)] = 0
        for i in np.nonzero(need)[0]:
            wait(e, names[i], need[i])
        ins = call()
        if ins is not None:
            ins.then_inc(T.sem[s], inc)
        count[s] = count.get(s, 0) + inc
        mark(s, count[s], reads, writes)

    def x(v):
        return v[0] if isinstance(v, tuple) else v

    def tt(o, a, b, f):
        op("V", lambda: g.vector.tensor_tensor(o[0], a[0], b[0], f), [a, b], [o])

    def ts(o, a, s1, f1, s2=None, f2=None):
        if f2 is None:
            op("V", lambda: g.vector.tensor_scalar(o[0], a[0], x(s1), None, f1), [a, s1], [o])
        else:
            op("V", lambda: g.vector.tensor_scalar(o[0], a[0], x(s1), x(s2), f1, f2), [a, s1, s2], [o])

    def cp(o, a):
        op("V", lambda: g.vector.tensor_copy(o[0], a[0]), [a], [o])

    def scan(o, a, b, f0, f1, first=0.0):
        op("V", lambda: g.vector.tensor_tensor_scan(o[0], a[0], b[0], first, f0, f1), [a, b], [o])

    def fill(o, c):
        op("V", lambda: g.vector.memset(o[0], c), [], [o])

    def act(o, a, f, scale=None, bias=None, acc=None):
        kw = {}
        if scale is not None:
            kw["scale"] = scale
        if bias is not None:
            kw["bias"] = x(bias)
        if acc is not None:
            kw["accum_out"] = acc[0]
        op("S", lambda: g.scalar.activation(o[0], a[0], f, **kw), [a, bias], [o] + ([acc] if acc else []))

    def quant(name, src, lo=0, hi=None):
        q, s = ap("q" + name, lo, hi), ap("s" + name, lo, hi)
        op("V", lambda: g.vector.quantize_mx(q[0], s[0], src[0]), [src], [q, s])

    def mm(bank, wn, w0, xn, lo, hi, start=True, stop=True):
        o = ap("p%d" % bank, 0, hi - lo)
        a = [ap("q" + wn, w0, w0 + 128), ap("s" + wn, w0, w0 + 128), ap("q" + xn, lo, hi), ap("s" + xn, lo, hi)]
        op("P", lambda: g.tensor.matmul_mx(o[0], a[0][0], a[1][0], a[2][0], a[3][0], start, stop), a, [o], chain=not start)

    def iota(o, pat, base=0, cm=0):
        small = SCRATCH[o[1][0][0]][2] != "int32"
        op("G", lambda: g.iota(o[0], pat, base, cm, allow_small_or_imprecise_dtypes=True) if small else g.iota(o[0], pat, base, cm), [], [o])

    def aff(o, a, pat, f, fl, base, cm):
        op("G", lambda: g.affine_select(o[0], a[0], pat, f, fl, base, cm), [a], [o])

    def load(e, sem, o, src):
        op(e, lambda: Q[e].dma_start(o[0], src), [], [o], sem=sem, inc=16)

    def store(e, dst, src, view=None):
        op(e, lambda: Q[e].dma_start(dst, src[0] if view is None else view), [src], [], sem="dout", inc=16)

    def send(dst, o, a, sem):
        rid, pid = topo.addr(dst)[:2]
        mask = topo.mask(core, dst)

        def call():
            g.remote_dma(o[0], a[0], T.sem[sem], T.sem.snt, pid, rid, mask)
        op("G", call, [a], [], sem="snt", inc=len(topo.engines(core, dst)))

    def arrives(src, sem, views):
        count[sem] = len(views) * len(topo.engines(src, core))
        mark(sem, count[sem], [], [r for v in views for r in v[1]])

    def cc(name, lo=0, hi=None, st=1):
        a, w = CAT[name]
        return ap("cc", a + lo, a + (w if hi is None else hi), st)

    def cl(name, lo=0, hi=None):
        a, w = LAT[name]
        return ap("cl", a + lo, a + (w if hi is None else hi))

    def ll(name, k):
        a = LAT[name][0] // 16
        return ap("ll", a, a + k)

    def slot(k, t, lo, hi):
        return ap("mt", 4 * (START[k] + lo) + t, 4 * (START[k] + hi), 4)

    def gap(k):
        lo = 16 * TILES[k][-1] if len(TILES[k]) == 4 else 0
        return ap("mt", 4 * (START[k] + lo), 4 * (START[k] + WIDTH[k]))

    def zero(o):
        act(o, ap("ones", 0, o[1][0][2] - o[1][0][1]), F.Copy, scale=0.0)

    pm, pmoff, pc, pm16, poff = (ap("pm", i, i + 1) for i in (0, 1, 2, 3, 7))
    X = ap("xz", X0, X0 + 4 * C)
    H, THIRD = C // 2, C // 3

    def xb(b):
        return ap("xz", X0 + b, X0 + 4 * C, 4)

    def half(h):
        return ap("xz", X0 + 4 * H * h, X0 + 4 * H * (h + 1))

    def plane(b):
        return ap("xp", C * b, C * b + C)

    for t in range(R):
        arrives(prv, "ar%d" % t, [ap("qa%d" % t), ap("sa%d" % t)])
    arrives(prv, "aow", [ap("tab", 64, 73), ap("tab", 73, 92)])
    arrives(nxt, "aw1", [ap("wl1")])
    arrives(nxt, "aw2", [ap("wl2")])

    load("S", "du", ap("ub"), T.u[:, :])
    for i, (lo, hi) in enumerate(PIECES):
        load("Y", "dx%d" % i, ap("xz", X0 + 4 * lo, X0 + 4 * hi), T.x[:, 4 * lo:4 * hi])
    fill(ap("ones"), 1.0)
    zero(ap("zb"))
    zg = [gap(k) for k in range(3)]
    zf = [ap("cl", lo, lo + NL // 2) for lo in (0, NL // 2)]
    for sem, zeros in (("dz", zg), ("dz2", zf)):
        for o in zeros:
            z = ap("zb", 0, o[1][0][2] - o[1][0][1])
            op("Y", lambda: g.sync.dma_start(o[0], z[0]), [z], [o], sem=sem, inc=16)
        mark(sem, count[sem], [ap("zb")[1][0]], [r for o in zeros for r in o[1]])
    load("Y", "dw", u8(ap("qw")), T.wc[:, :])
    load("Y", "dws", ap("sw"), T.ws[:, :])
    load("Y", "dv", ap("vb"), T.v[:, :])

    iota(ap("pi", 0, 1), [[0, 1]], 0, 1)
    iota(ap("ui"), [[1, 2], [16, 8]])
    iota(ap("iq"), [[0, KW // 16], [1, 16]])
    aff(ap("acs", 0, 128), ap("ones", 0, 128), [[-16, 8], [0, 16]], A.is_ge, 0.0, 0, 1)
    aff(ap("band", 0, 512, 4), ap("acs", 0, 128), [[16, 8], [0, 16]], A.is_ge, 0.0, 15, -1)
    aff(ap("tri", 0, 512, 4), ap("band", 0, 512, 4), [[1, 128]], A.is_gt, 0.0, 0, -1)
    for k in (7, 6, 5):
        fill(gap(k), 0.0)
    ts(ap("pi", 1, 2), ap("pi", 0, 1), 15, A.bitwise_and)
    cp(ap("ul"), ap("ui"))
    cp(pm, ap("pi", 1, 2))
    zero(gap(4))
    zero(ap("rs"))
    quant("u", ap("ub"))
    ts(ap("dg"), ap("iq"), pm, A.is_equal)
    cp(u32(ap("qu0")), ind(u32(ap("qu")), ap("ul", 0, 8)))
    act(ap("su0"), ind(ap("su"), ap("ul", 0, 8)), F.Copy)
    zero(gap(3))
    act(pmoff, pm, F.Identity, scale=-OFF, bias=15 * OFF)
    act(pm16, pm, F.Identity, scale=-1.0, bias=16.0)
    iota(ap("jj"), [[1, C]])
    iota(cc("c16", 0, SPLIT), [[16, SPLIT]])
    iota(cc("c16", SPLIT, 30), [[16, 30 - SPLIT]], 16 * SPLIT - KW)

    for lo, hi, pat, base in [(0, 4, [[0, 4]], 0), (4, 6, [[0, 2]], 3), (6, 8, [[3, 2]], 6), (8, 10, [[0, 2]], 3),
                              (10, 14, [[0, 2], [3, 2]], 6), (14, 16, [[3, 2]], 9), (16, 24, [[3, 2], [3, 2], [3, 2]], 6)]:
        iota(cc("IDX", lo, hi), pat, base)
    for lo, hi, pat, base in [(0, 4, [[0, 4]], 7), (4, 6, [[0, 2]], 15), (6, 8, [[64, 2]], 23), (8, 10, [[0, 2]], 15),
                              (10, 14, [[0, 2], [64, 2]], 23), (14, 16, [[8, 2]], 87), (16, 18, [[64, 2]], 23),
                              (18, 22, [[0, 2], [8, 2]], 87), (22, 24, [[8, 2]], 95)]:
        iota(cc("FX", lo, hi), pat, base)
    for i in range(3):
        iota(cc("NA", 8 * i, 8 * i + 8), [[3, 2], [3, 2], [3, 2]], 9 + 3 * i)
    iota(cl("L0", 0, 9), [[16, 3], [48, 3]], 15)
    iota(cl("LA", 0, 72), [[48, 3], [0, 24]], 47)
    iota(cl("LD", 0, 12), [[48, 3], [16, 2], [0, 2]], 15)
    iota(cl("LR", 0, 24), [[0, 4], [2, 2], [4, 3]], 1)
    iota(cl("LR0", 0, 24), [[0, 4], [1, 6]])
    iota(cl("LR5", 0, 24), [[0, 4], [5, 2], [10, 3]], 4)
    iota(cl("LR5", 24, 48), [[0, 4], [5, 2], [10, 3]], 34)
    iota(cl("LE", 0, 12), [[24, 3], [0, 2], [8, 2]], 7)
    iota(cl("LF", 0, 12), [[10, 3], [5, 2], [0, 2]], 4)
    iota(cl("LC", 0, 60), [[0, 2], [1, 3], [0, 10]])
    for h in range(2):
        iota(cl("LT", 30 * h, 30 * h + 30), [[1, 3], [3, 2], [3, 5]], 32 * h)
    iota(cl("LS", 0, 81), [[0, 9], [8, 9]], 7)
    iota(cl("LO", 0, 81), [[1, 27], [0, 3]])
    iota(cl("LK", 0, 30), [[1, 3], [3, 10]])
    aff(ap("eye"), ap("ones"), [[1, 516]], A.is_equal, 0.0, -3, -4)
    iota(cc("S0"), [[NS, 4], [16, 2], [48, 3]])
    iota(cc("T4", 0, 24), [[1, 4], [0, 6]])
    iota(cc("T4", 24, 48), [[NS, 4], [0, 6]])
    iota(ap("alt"), [[0, 192], [1, 2]])

    def scores(i):
        lo, hi = PIECES[i]
        quant("x", ap("xz", X0 + 4 * lo, X0 + 4 * hi), lo, hi)
        mm((4, 5, 7)[i], "u0", 0, "x", lo, hi)
        if hi == C:
            mm(0, "u0", 0, "x", 0, C)
        mm((6, 3, 1)[i], "u0", 0, "x", 0, min(hi, 16 * SPLIT))

    def own_column(i):
        lo, hi = PIECES[i]
        tt(ap("mm", lo, hi), ap("p%d" % (4, 5, 7)[i], 0, hi - lo), ap("dg", 0, hi - lo), A.mult)

    def spread(i):
        lo, hi = PIECES[i]
        scan(ap("yy", lo, hi), ap("keep", 0, hi - lo), ap("mm", lo, hi), A.mult, A.add)

    def periodic(o, k, a, lo, hi, f0, f1, shift=0):
        for i in range(lo, hi, KW):
            j = min(hi, i + KW)
            scan(ap(o, i, j), ap(k, 0, j - i), a(i + shift, j + shift), f0, f1)

    def pack(k):
        quant("m", ap("mt", 4 * START[k], 4 * (START[k] + WIDTH[k])), START[k], START[k] + WIDTH[k])

    def count_tile(k):
        mm(2, "r" if k == 0 else "b", 0, "m", START[k], START[k] + WIDTH[k], k == 0, k == 5)

    def block(c, lo, hi):
        k = [c in tl for tl in TILES].index(True)
        return slot(k, TILES[k].index(c), lo, hi)

    def shared(c):
        return 16 * c if c < SPLIT else SHARE if c == SPLIT else 0

    def compare(c):
        ts(block(c, shared(c), 16 * c), ap("p0", shared(c), 16 * c), ap("yy", 16 * c + 15, 16 * c + 16), A.is_lt)

    def row_sum(c):
        end, lo, w = 256 * (c - SPLIT + 1), shared(c), 8 * c - shared(c) // 2
        scan(ap("sums", end - w, end), block(c, lo, lo + w), block(c, lo + w, 16 * c), A.add, A.add, -float(KW))

    def on_scalar(blocks):
        def sg(c):
            return ap("sg", 8 * c * (c - 1), 8 * c * (c - 1) + shared(c))
        for a, b in zip([None, None] + blocks, blocks + [None, None]):
            if b:
                bank = (6, 3, 1)[[16 * b < hi for _, hi in PIECES].index(True)]
                act(sg(b), ap("p%d" % bank, 0, shared(b)), F.Sign, scale=-1.0, bias=ap("yy", 16 * b + 15, 16 * b + 16))
            if a:
                act(block(a, 0, shared(a)), sg(a), F.Relu, acc=ap("rs", a, a + 1))
            if a == 12:
                act(ap("c0", 0, 30), cc("c16", 0, 30), F.Identity, bias=pc)

    scores(0)
    ts(ap("keep"), ap("iq"), pm, A.is_gt)
    act(pc, ap("dg", 0, 1), F.Identity, scale=-LOW, bias=pm16)
    act(poff, ap("dg", 0, 1), F.Identity, scale=-LOW, bias=pmoff)
    for lo in range(0, C, H):
        act(ap("step", lo, lo + H), ap("keep", 1, H + 1), F.Identity, scale=LOW + OFF, bias=-LOW)
    for b in range(1, 4):
        cp(ap("band", b, 512, 4), ap("band", 0, 512, 4))
    own_column(0)
    scores(1)
    spread(0)
    for b in range(1, 4):
        cp(ap("tri", b, 512, 4), ap("band", 0, 512, 4))
    quant("b", ap("band"))
    own_column(1)
    scores(2)
    spread(1)
    ts(ap("ext"), ap("keep"), LOW + OFF, A.mult, LOW, A.subtract)
    quant("r", ap("tri"))
    for c in (1, 2):
        ts(block(c, 0, 16 * c), ap("p4", 0, 16 * c), ap("yy", 16 * c + 15, 16 * c + 16), A.is_lt)
    own_column(2)
    for c in (1, 2):
        o, a = ap("rs", c, c + 1), block(c, 0, 16 * c)
        op("V", lambda: g.vector.tensor_reduce(o[0], a[0], AxisListType.X, A.add), [a], [o])
    spread(2)
    on_scalar(list(range(3, 8)) + list(range(11, 16)) + list(range(SPLIT - (SHARE == 0), 15, -1)) + [8, 9, 10])
    pack(7)
    compare(29)
    after = {27: (6,), 26: (0,), 24: (4,), SPLIT: (1, 2, 3, 5)}
    for c in range(28, SPLIT - 1, -1):
        compare(c)
        row_sum(c + 1)
        if c == 28:
            tt(slot(0, 0, 0, C), ap("p0", 0, C), ap("yy"), A.is_le)
        if c == 27:
            periodic("rowd", "keep", lambda i, j: slot(0, 0, i, j), 0, C, A.mult, A.add)
        for k in after.get(c, ()):
            if k == 1:
                tt(ap("w1", 0, 30), ap("c0", 0, 30), ap("rowd", 15, C, 16), A.subtract)
            if k == 2:
                row_sum(SPLIT)
            if k == 5:
                tt(ap("w1", SPLIT, 30), ap("w1", SPLIT, 30), ap("sums", 255, None, 256), A.subtract)
            pack(k)
            for j in {0: (0, 6, 7), 6: ()}.get(k, (k,)):
                count_tile(j)
    act(ap("su1"), ind(ap("su"), ap("ul", 8, 16)), F.Copy)
    for c, (lst, k, f) in [(c, e) for e in (("LW0", "IDX", 1.0), ("L3", "NA", 1.0), ("LW1", "FX", 24.0)) for c in range(3)]:
        act(cl(lst, 24 * c, 24 * c + 24), cc(k), F.Identity, bias=f * c)
    zero(ap("tab", 0, 64))
    act(ap("cm"), ap("dg", 0, NS), F.Identity, scale=-2 * BIG, bias=BIG)
    for t in range(R):
        act(ap("pm", 4 + t, 5 + t), pm, F.Identity, scale=1027.0 / 1024, bias=t * (4 * NS + NS / 1024))

    def wrap_lists(lo, hi):
        scan(ap("cls", lo, hi), ap("ext", 0, hi - lo), ap("cl", lo, hi), A.add, A.max)

    def cast_lists(lo, hi):
        ts(ap("ll", lo // 16, hi // 16), ap("cls", lo + 15, hi, 16), pmoff, A.subtract)

    def pack_eye(b):
        quant("e", ap("eye", 3 - b, 515 - b), 128 * b, 128 * b + 128)

    tt(ap("step", 15, C, 16), ap("w1", 0, 30), ap("rs", 0, 30), A.subtract)
    cp(u32(ap("qu1")), ind(u32(ap("qu")), ap("ul", 8, 16)))
    mm(3, "u1", 0, "x", 0, C)
    for b in range(4):
        act(plane(b), xb(b), F.Copy)
    act(ap("s1"), ap("p3", 0, C), F.Copy)
    wrap_lists(0, 128)
    scan(ap("ex"), ap("p2", 0, C), ap("step"), A.max, A.add, -LOW)
    wrap_lists(128, 256)
    ts(ap("pos"), ap("ex", 15, C, 16), poff, A.subtract)
    wrap_lists(256, 384)
    op("V", lambda: g.vector.tensor_copy(T.ob[:, :].indirect(T.pos[:, :]), T.jj[:, :]), [ap("pos"), ap("jj")], [ap("ob")])

    def wrap_item(k):
        scan(ap("ex", 48 * k, 48 * k + 48), ap("ext", 0, 48), ap("ob", k, C, 10), A.add, A.max)

    cast_lists(0, 384)
    ts(ap("gl", 24, 48), cc("S0"), pm, A.add)
    for k in range(6):
        wrap_item(k)
    ts(ap("bl16"), ind(ap("ex", 0, NS), ll("L0", 1)), pmoff, A.subtract)

    def gather_t(b, win, lst, scale, on_v, lo=0, hi=9):
        o = ap("tt", 64 * lo + b, 64 * hi, 4)
        if on_v:
            ts(o, ind(win, ap(lst, lo, hi)), scale, A.mult)
        else:
            act(o, ind(win, ap(lst, lo, hi)), F.Copy, scale=scale)

    def send_t(t):
        quant("t%d" % t, ap("tt"))
        send(nxt, u8(ap("qa%d" % t)), u8(ap("qt%d" % t)), "ar%d" % t)
        send(nxt, ap("sa%d" % t), ap("st%d" % t), "ar%d" % t)

    def targets(win, lst, k):
        tt(ap("tg", 0, 16 * k), ind(win, ll(lst, k)), cc("T4", 0, 16 * k), A.add)

    def gather_targets(w):
        cp(ap("gl", 0, w), ap("tg", 0, w))
        act(ap("tf"), ap("tg", 0, 32), F.Copy, scale=1.0 / X0)
        act(ap("xg", 0, 768, 2), ind(X, ap("gl", 0, 24)), F.Copy, scale=0.5)

    def own_scores():
        tt(ap("bp"), ind(ap("s1"), ap("bl16", 0, 9)), ap("cm"), A.max)

    ts(ap("tab", 0, 9), ap("ex", 15, NS, 16), pmoff, A.subtract, 4.0, A.mult)
    send(nxt, ap("tab", 64, 73), ap("tab", 0, 9), "aow")
    wrap_item(6)
    wrap_item(7)
    for b in range(4):
        gather_t(b, plane(b), "bl16", 1.0, b > 1)
    wrap_item(8)
    send_t(0)
    ts(ap("tab", 9, 27), ap("ex", NS + 15, 432, 16), pmoff, A.subtract, 4.0, A.mult)
    send(nxt, ap("tab", 73, 92), ap("tab", 9, 28), "aow")
    targets(ap("tab", 0, 8), "LR0", 2)
    pack_eye(0)
    pack_eye(1)
    gather_targets(24)
    own_scores()
    pack_eye(2)
    pack_eye(3)
    for lo in range(384, NL, KW):
        wrap_lists(lo, min(lo + KW, NL))
    quant("v", ap("vb"))
    cast_lists(384, NL)
    act(ap("pk", 0, 32), ap("tab", 0, 32), F.Copy, scale=1.0 / 512)

    aff(ap("acs"), ap("ones", 0, NS), [[0, 9], [1, 16]], A.is_gt, 2.0, 0, 0)
    aff(ap("h144"), ap("acs"), [[0, 3], [1, 48]], A.is_gt, 0.0, 0, 0)
    iota(cc("X8"), [[0, 10], [1, 8]])
    iota(cc("TH0"), [[0, 4], [2, 2], [0, 2]], 1)
    aff(cc("K8"), ap("ones", 0, 80), [[0, 10], [1, 8]], A.is_gt, 0.0, 0, 0)
    iota(cc("NV"), [[0, 80]])
    for c in range(3):
        iota(cc("N0", c, 9, 3), [[16385, 3]], 49200 * c + 1)
        iota(cc("NV", 24 * c + 7, 24 * c + 24, 8), [[16385, 3]], 49200 * c + 1)

    def late_constants():
        iota(ap("ow"), [[0, 80]])
        iota(cc("J5", 0, 65), [[0, 13], [1, 5]])
        aff(cc("K3"), ap("ones", 0, 96), [[0, 32], [1, 3]], A.is_gt, 0.0, 0, 0)
        aff(cc("K5", 0, 60), ap("ones", 0, 60), [[0, 12], [1, 5]], A.is_gt, 0.0, 0, 0)
        iota(cc("H4"), [[0, 4], [1, 2], [1, 2]])
        aff(cc("N3"), ap("ones", 0, 96), [[0, 32], [1, 3]], A.is_equal, 0.0, 0, 0)
        aff(ap("k16"), ap("ones", 0, NS), [[0, 9], [1, 16]], A.is_gt, 0.0, 0, 0)
        iota(ap("an"), [[0, 80]])
        iota(ap("fr"), [[0, 32]])

    def columns(run):
        return ap("xz", X0 + 4 * run[0], X0 + 4 * run[1])

    def element(run, b):
        return ap("xz", X0 + 4 * run[0] + b, X0 + 4 * run[1], 4)

    def piece(run, b):
        return ap("xp", C * b + run[0], C * b + run[1])

    def products(run, bank):
        for b in range(4):
            mm(bank + b, "w", 128 * b, "z", *run)
            act(piece(run, b), element(run, b), F.Copy, scale=32.0)

    def add_product(run, bank, b):
        tt(piece(run, b), ap("p%d" % (bank + b), 0, run[1] - run[0]), piece(run, b), A.add)

    def unscale(run, b, on_v):
        if on_v:
            ts(element(run, b), piece(run, b), 2.0 ** -5, A.mult)
        else:
            act(element(run, b), piece(run, b), F.Copy, scale=2.0 ** -5)

    def weigh(w, win, lst):
        tt(ap("pr", 0, w), ind(win, ll(lst, w // 16)), ap("oh", 0, w), A.mult)

    def collect(out, lo, w):
        scan(ap(out, lo, lo + w), cc("K8", 0, w), ap("pr", 0, w), A.mult, A.add)

    for t in range(R):
        last = t == R - 1
        a = "a%d" % t
        mm(0, "u1", 0, a, 0, NS)
        for b in range(4):
            mm(4 + b, "e", 128 * b, a, 0, NS)
        for b in range(4):
            act(ap("hh", NS * (4 * t + b), NS * (4 * t + b + 1)), ap("p%d" % (4 + b), 0, NS), F.Copy, scale=0.5)

        def held(b):
            return ind(ap("hh", 0, NS * (4 * t + b + 1)), ap("gl", 24 + 6 * b, 30 + 6 * b))

        def blend(b):
            tt(ap("bl", 192 * b + 1, 192 * b + 192, 2), held(b), ap("xg", 192 * b, 192 * b + 192, 2), A.add)

        def blend_from(b):
            scan(ap("bl", 192 * b, 768), ap("alt", 192 * b - 384, 384), ap("xg", 192 * b, 768), A.mult, A.add)

        shared_from = 3 if last else 2
        for b in range(shared_from, 4):
            act(ap("xg", 192 * b + 1, 192 * b + 192, 2), held(b), F.Copy)

        tt(ap("cmp"), ap("p0", 0, NS), ap("bp"), A.is_ge)
        scan(ap("hs"), ap("h144"), ap("cmp"), A.mult, A.add)
        if t == 0:
            tt(ap("pk", 32, 60), ap("tab", 64, 92), ap("pk", 0, 28), A.add)
        if last:
            scan(ap("acs"), ap("k16"), ap("cmp"), A.mult, A.add)
        blend(0)
        if not last:
            tt(ap("oh", 0, 80), ind(ap("hs"), ll("LA", 5)), cc("X8"), A.is_equal)
        tt(ap("dd"), ind(ap("hs"), ll("LD", 1)), cc("TH0") if t == 0 else ap("th"), A.is_ge)
        blend(1)
        if not last:
            weigh(80, ap("pk", 32, 60) if t == 0 else ap("l0", 0, 160), "LW%d" % t)
        tt(ap("w1"), ind(ap("dd"), ll("LR", 2)), ap("tf"), A.add)
        if not last:
            blend_from(2)
            collect("l%d" % t, 0, 80)
            ts(ap("sl"), ap("w1"), float(X0), A.mult)
            ts(ap("ws%d" % (t + 1)), ap("l%d" % t, 7, 80, 8), 0.25, A.mult, 0.47, A.subtract)
            send(prv, ap("wl%d" % (t + 1)), ap("ws%d" % (t + 1)), "aw%d" % (t + 1))
            if t == 0:
                late_constants()
                act(ap("tab", 32, 41), cc("N0", 0, 9), F.Identity, scale=1.0 / 1024, bias=ap("pm", 4, 5))
                act(ap("orep"), ind(ap("pk", 0, 32), ll("LO", 6)), F.Copy)
            act(ap("nv", 96 * t, 96 * t + 96), ind(cc("NV"), ll("LS", 6)), F.Identity, scale=1.0 / 1024, bias=ap("pm", 5 + t, 6 + t))
        else:
            blend(2)
            ts(ap("sl"), ap("w1"), float(X0), A.mult)
            blend_from(3)
            act(ap("an", 7, 72, 8), ap("acs", 15, NS, 16), F.Copy)
            tt(ap("pr", 0, 96), ind(ap("an"), ll("LS", 6)), ap("o2"), A.is_ge)
            for b in (MAGIC, -MAGIC):
                act(ap("c0", 0, 27), ap("tab", 32, 59) if b > 0 else ap("c0", 0, 27), F.Identity, bias=b)
        op("V", lambda: g.vector.tensor_copy(T.xz[:, :].indirect(T.sl[:, 0:24]), T.bl[:, 1:768:2]), [ap("sl", 0, 24), ap("bl", 1, 768, 2)], [ap("xz")])
        if last:
            break
        m = 54 + 27 * t
        k = (m + 15) // 16
        ts(ap("w3", 0, 9), ap("ws%d" % (t + 1), 0, 9), -4.0, A.mult)
        tt(ap("cu", 4 * t, 4 * t + 3), ap("dd", 1, 12, 4), ap("dd", 3, 12, 4), A.add)

        def at_cursor():
            tt(ap("o5"), ind(ap("cu", 8 * t, 8 * t + 3), ll("LC", 4)), cc("J5", 0, 64), A.is_equal)

        runs = ((0, THIRD), (THIRD, C))
        for h, run in enumerate(runs):
            quant("z", columns(run), *run)
            products(run, 4 * h)
        tt(ap("ow", 7, 72, 8), ap("l%d" % t, 7, 72, 8), ap("w3", 0, 9), A.add)
        if t == 0:
            at_cursor()
        else:
            tt(ap("cu", 8, 11), ap("cu", 0, 3), ap("cu", 4, 7), A.add)
        for h, run in enumerate(runs):
            for b in range(4):
                add_product(run, 4 * h, b)
        tt(ap("o2", 0, 16 * k), ind(ap("ow"), ll("LS", k)), ap("orep", 0, 16 * k), A.is_equal)
        for b in range(4):
            gather_t(b, plane(b), "wl%d" % (t + 1), 2.0 ** -5, b == 3)
        tt(ap("pr2", 0, m), ap("o2", 0, m), ap("nv", 96 * t, 96 * t + m), A.mult)
        send_t(t + 1)
        for b in range(2):
            unscale((0, C), b, False)
        scan(ap("sel", 0, m), cc("K3", 0, m), ap("pr2", 0, m), A.mult, A.max)
        for b in (3, 2):
            unscale((0, C), b, True)
        tt(ap("tab", 32, 32 + m // 3), ap("tab", 32, 32 + m // 3), ap("sel", 2, m, 3), A.max)
        if t == 1:
            at_cursor()
        quant("x", half(0), 0, H)
        tt(ap("pr2", 0, 64), ind(ap("tab", 0, 64), ll("LT", 4)), ap("o5"), A.mult)
        quant("x", half(1), H, C)
        scan(ap("sel", 0, 60), cc("K5", 0, 60), ap("pr2", 0, 60), A.mult, A.add)
        if t == 0:
            weigh(80, ap("pk", 32, 60), "L3")
        ts(ap("bl16", 0, 9), ap("ow", 7, 72, 8), 128.0, A.mult)
        act(ap("owr"), ind(ap("ow"), ll("LE", 1)), F.Copy, scale=512.0)
        for h in range(2):
            mm(4 + h, "u1", 0, "x", H * h, H * h + H)
            act(ap("s1", H * h, H * h + H), ap("p%d" % (4 + h), 0, H), F.Copy)
        targets(ap("sel", 0, 60), "LR5", 3)
        tt(ap("eq"), ind(ap("sel", 0, 60), ll("LF", 1)), ap("owr"), A.is_equal)
        if t == 0:
            collect("l0", 80, 80)
        gather_targets(48)
        scan(ap("th"), cc("H4"), ap("eq"), A.mult, A.add)
        own_scores()

    runs = [(0, THIRD), (THIRD, C - 128), (C - 128, C)]

    def finish(i):
        lo, hi = runs[i]
        quant("x", columns(runs[i]), lo, hi)
        mm(4 + i, "v", 0, "x", lo, hi)
        store("Y", T.oc[:, 4 * lo:4 * hi], u8(ap("qx", lo, hi)))

    def store_y(i):
        lo, hi = runs[i]
        act(ap("yo", lo, hi), ap("p%d" % (4 + i), 0, hi - lo), F.Copy)
        store("YSS"[i], T.y[:, lo:hi], ap("yo", lo, hi))

    scan(ap("sel", 0, 81), cc("N3", 0, 81), ap("pr", 0, 81), A.max, A.min)
    tt(ap("w4", 0, 27), ap("tab", 32, 59), ap("c0", 0, 27), A.subtract)
    for i in range(3):
        quant("z", columns(runs[i]), *runs[i])
    products(runs[0], 0)
    tt(ap("fr", 0, 27), ap("w4", 0, 27), ap("sel", 2, 81, 3), A.mult)
    act(ap("sko"), ind(ap("fr"), ll("LK", 2)), F.Identity, scale=1024.0, bias=-1.0)
    for c in range(3):
        store("Y", T.sk[:, 160 * c:160 * c + 160], ap("sko", 10 * c, 10 * c + 10))
    products(runs[1], 4)
    for b in range(4):
        add_product(runs[0], 0, b)
    products(runs[2], 0)
    for b in range(4):
        unscale(runs[0], b, True)
    for b in range(4):
        add_product(runs[1], 4, b)
        if b < 2:
            unscale(runs[1], b, False)
        if b == 1:
            finish(0)
    store_y(0)
    for b in range(4):
        add_product(runs[2], 0, b)
        if b == 1:
            unscale(runs[1], 2, True)
            unscale(runs[1], 3, True)
    finish(1)
    for b in range(4):
        unscale(runs[2], b, b > 1)
    finish(2)
    store_y(1)
    store_y(2)
    for k in range(4):
        store("Y", T.osc[4 * k:4 * k + 4, :], ap("sx"), T.sx[32 * k:32 * k + 4, :])
    for s in names:
        if count.get(s, 0):
            wait("Y", s, count[s])
